import numpy as np, ml_dtypes
CORES = [16,18,20,22]
N = 4
BF = ml_dtypes.bfloat16
W, M, H, L, CAP, RO = 2048, 2048, 4096, 256, 48, 4
def sums(w, x):
    return np.add.reduce(w[..., 0:1] * x, axis=2) & 4095, np.add.reduce(w[..., 1:2] * x, axis=2) & 4095
def probe(w, lm, tl, mo, m):
    u, v = sums(w, m); a = (u * v) >> 5
    c = (a[:, :, None] + w[..., 2:3] * u[:, :, None]) & (W - 1)
    x = np.take_along_axis(lm, c.reshape(N, 8, 1, 16 * L), 3).reshape(N, 8, 16, 16, L)
    ok = np.all(x <= m[:, :, :, None], axis=2); has = np.any(ok, axis=2)
    g = np.take_along_axis(c, np.argmax(ok, axis=2)[:, :, None], 2)
    tg = np.take_along_axis(tl, g, 3); q = m - np.take_along_axis(lm, g, 3)
    y = np.take_along_axis(mo, tg.reshape(N, 8, 1, 16 * L), 3).reshape(N, 8, 16, 16, L)
    p = np.minimum(q[:, :, :, None] + y, 255).reshape(N, 8, 16, 16 * L)
    e, f = sums(w, p); h = (((e * f) >> 5) + e) & (H - 1)
    return a, c[:, :, 0], has, tg, p, h
def seek(sn, has, p, h):
    new = np.any(np.take_along_axis(sn, h[:, :, None], 3) != p, axis=2).reshape(N, 8, 16, L) & has[:, :, None]
    return np.any(new, axis=2), np.argmax(new, axis=2)
def first(key):
    o = np.argsort(key, axis=2, kind="stable"); s = np.take_along_axis(key, o, 2)
    b = np.ones(key.shape, bool); b[..., 1:] = s[..., 1:] != s[..., :-1]
    win = np.zeros(key.shape, bool); np.put_along_axis(win, o, b, 2); return win
def turn(st, pr, fill):
    lm, tl, sn, m, ct, ci = st; a, c0, has, tg, p, h = pr
    child, i = seek(sn, has, p, h); j = i * L + np.arange(L)
    pc = np.take_along_axis(p, j[:, :, None], 3); hc = np.take_along_axis(h, j, 2)
    win = first(np.where(child, hc, np.where(has, 2 ** 15 + np.arange(L), 2 ** 14 + c0)))
    wt = np.where(np.arange(16)[:, None] == ci[:, :, None], (a & (M - 1))[:, :, None], ct)
    lm, tl, sn = lm.copy(), tl.copy(), sn.copy()
    for r in range(N):
        for g in range(8):
            b = win[r, g] & child[r, g]; sn[r, g][:, hc[r, g, b]] = pc[r, g][:, b]
            b = win[r, g] & ~has[r, g]; lm[r, g][:, c0[r, g, b]] = m[r, g][:, b]; tl[r, g][:, c0[r, g, b]] = wt[r, g][:, b]
    nm, nt, ni = fill.copy(), tl[..., :L].copy(), np.zeros((N, 8, L), np.int64)
    for d in range(N):
        f = child & ((hc & (N - 1)) == d); f = f & (np.add.accumulate(f.astype(np.int64), axis=2) <= CAP)
        for r in range(N):
            for g in range(8):
                b = np.flatnonzero(f[r, g]); z = r * CAP + np.arange(b.size)
                nm[d, g][:, z] = pc[r, g][:, b]; nt[d, g][:, z] = tg[r, g][:, b]; ni[d, g, z] = i[r, g, b]
    return lm, tl, sn, nm, nt, ni
def mono(rng, n, den, top):
    return ((rng.random((N, 8, 16, n), dtype=np.float32) < den) * rng.integers(1, top + 1, (N, 8, 16, n), dtype=np.int32)).astype(np.int32)
def uneven(rng, n, den):
    v = np.exp2(8 * rng.random((N, 8, 1, n), dtype=np.float32) * rng.random((N, 8, 16, n), dtype=np.float32))
    return ((rng.random((N, 8, 16, n), dtype=np.float32) < den) * np.minimum(v, 255).astype(np.int32)).astype(np.int32)
def base(rng):
    w = np.tile(rng.integers(0, 128, (1, 8, 16, 3), dtype=np.int32), (N, 1, 1, 1)); dens = np.array([0.15, 0.5, 0.8, 1.0, 1.0])
    lm = mono(rng, W, rng.choice(np.array([0.2, 0.3, 0.5]), (N, 8, 1, W)), 160); mo = mono(rng, M, rng.choice(np.array([0.2, 0.4]), (N, 8, 1, M)), 120)
    tl = rng.integers(0, M, (N, 8, 16, W), dtype=np.int32)
    sn = np.where(rng.random((N, 8, 1, H)) < 0.5, -1, mono(rng, H, 0.5, 255)).astype(np.int32)
    m = mono(rng, L, rng.choice(dens, (N, 8, 1, L)), 255); fr = mono(rng, RO * L, rng.choice(dens, (N, 8, 1, RO * L)), 255)
    old = np.take_along_axis(m, rng.integers(0, L, (N, 8, 1, RO * L)), 3)
    return w, lm, tl, mo, sn, m, np.where(rng.random((N, 8, 1, RO * L)) < 0.3, old, fr)
def plant(rng, w, lm, tl, mo, sn, m, fr, until=1, n=L - N * CAP - 8):
    pr = probe(w, lm, tl, mo, m); a, c0, has, tg, p, h = pr; used = np.zeros((N, 8, H), bool)
    cnt = rng.choice(np.array([0, 1, 2, 5, 15, 16]), (N, 8, L), p=[0.5, 0.2, 0.15, 0.05, 0.05, 0.05])
    for r in range(N):
        for g in range(8):
            for k in (1, 2, 5, 15, 16):
                x = np.flatnonzero(has[r, g] & (cnt[r, g] == k)); j = (np.arange(k)[:, None] * L + x).reshape(-1)
                sn[r, g][:, h[r, g, j]] = p[r, g][:, j]; used[r, g, h[r, g, j]] = True
    st = (lm, tl, sn, m, tl[..., :L], np.zeros((N, 8, L), np.int64))
    for t in range(until):
        was, row = st[1], st[5]; st = turn(st, pr, fr[..., t * L:(t + 1) * L])
        pr = probe(w, st[0], st[1], mo, st[3])
    own = pr[0] & (M - 1); came = np.any(st[3] != fr[..., (until - 1) * L:until * L], axis=2)
    stale = ~pr[2] & ~came & (row > 0)
    lone = ~pr[2] & came; anew = ~pr[2] & ~came & ~stale & np.any(st[1][..., :L] != was[..., :L], axis=2)
    used = used | np.any(st[2] != sn, axis=2)
    for r in range(N):
        for g in range(8):
            x = np.flatnonzero(lone[r, g]); v = np.flatnonzero(anew[r, g])[:4]
            s0 = np.flatnonzero(stale[r, g])[:4]
            if x.size + v.size + s0.size == 0: continue
            o = np.concatenate([s0, v, np.resize(x, n - v.size - s0.size)]) if x.size else np.concatenate([s0, v])
            fr[r, g][:, until * L + N * CAP:until * L + N * CAP + o.size] = st[3][r, g][:, o]
            half = rng.random(x.size) < 0.5
            col = np.concatenate([st[4][r, g][:, x][np.arange(16)[:, None] < st[5][r, g, x]],
                own[r, g, x[half]], own[r, g, v]])
            for part, cs in ((True, own[r, g, x[~half]]), (False, col)):
                y = mo[r, g][:, cs]
                e = np.add.reduce(w[r, g, :, 0:1] * y, axis=0) & 4095; f = np.add.reduce(w[r, g, :, 1:2] * y, axis=0) & 4095
                z = (((e * f) >> 5) + e) & (H - 1); b = ~used[r, g, z]
                if part: y = np.where((y == 0) & (rng.random(y.shape) < rng.choice(np.array([0.1, 0.5]), (1, y.shape[1]))), -1, y)
                sn[r, g][:, z[b]] = y[:, b]
def pack(w, lm, tl, mo, sn, m, fr):
    d = {"lm": lm, "tl": tl, "mo": mo, "sn": sn, "fm": m, "fr": fr, "wk": w}
    return {k: np.ascontiguousarray(x.reshape(N, 128, -1)).astype(np.int32) if k in ("tl", "wk") else np.ascontiguousarray(x.reshape(N, 128, -1)).astype(np.float32).astype(BF) for k, x in d.items()}
def setup_inputs(rng):
    s = base(rng); plant(rng, *s); return pack(*s)
def setup_inputs_again(rng):
    w, lm, tl, mo, sn, m, fr = base(rng); w[:, 2, :, 2] = 0; w[:, 3, :, 0] = 0; lm[:, 0] = 255; lm[:, 1] = 0; lm[N - 1, 3, :, 0] = 0; sn[:] = -1
    few = np.tile(rng.integers(0, M, (1, 8, 1, 5), dtype=np.int32), (N, 1, 1, 1))
    tl = np.take_along_axis(few, rng.integers(0, 5, (N, 8, 16, W)), 3); tl[:, :, 7] = rng.integers(0, M, (N, 8, W))
    fr = np.take_along_axis(m, rng.integers(0, 12, (N, 8, 1, RO * L)), 3); m = np.take_along_axis(m, rng.integers(0, 12, (N, 8, 1, L)), 3)
    return pack(w, lm, tl, mo, sn, m, fr)
def setup_inputs_corners(rng):
    w, lm, tl, mo, sn, m, fr = base(rng)
    lm[:, :, 0] = np.where(np.any(lm > 0, axis=2), lm[:, :, 0], 1); tl[:, 5] = rng.choice(np.array([0, M - 1]), (N, 16, W))
    fr[..., ::7] = 0; fr[..., 3::7] = 255
    pool, to = [], []
    for z in range(2):
        x = mono(rng, L, 0.9, 255); pr = probe(w, lm, tl, mo, x); child, i = seek(sn, pr[2], pr[4], pr[5])
        hc = np.take_along_axis(pr[5], i * L + np.arange(L), 2); pool.append(x); to.append(np.where(child, hc & (N - 1), -1))
    pool = np.concatenate(pool, axis=3); to = np.concatenate(to, axis=2)
    for r in range(N):
        for g in range(8):
            left = L; lanes = []
            for e in range(N):
                n = int(rng.choice(np.array([0, 1, CAP - 1, CAP, CAP + 1, 2 * CAP])))
                if r == 0 and e == 0: n = (CAP, CAP + 1, CAP - 1, 0, 1, CAP, CAP + 1, 2 * CAP)[g]
                if r == N - 1 and e == 0: n = CAP
                x = np.flatnonzero(to[r, g] == (r + 1 + e) % N)[:min(n, left)]; lanes.append(x); left -= x.size
            x = np.concatenate(lanes); m[r, g] = 0; m[r, g][:, rng.permutation(L)[:x.size]] = pool[r, g][:, x]
    return pack(w, lm, tl, mo, sn, m, fr)
def setup_inputs_ends(rng):
    def sub(n, den):
        return 255 * (rng.random((N, 8, 16, n)) < den).astype(np.int32)
    w = 127 * rng.integers(0, 2, (8, 16, 3)); w[6, :, 0:2] = 127; w[7, :, 0:2] = 0; w[:, 0, 2] = 0; w[:, 15, 2] = 127
    w[7, 0:4, 0] = 127; w[7, 4:8, 1] = 127; w[7, 13:16, 0] = (127, 127, 3); w[7, 10:13, 1] = (127, 127, 3)
    w = np.tile(w[None], (N, 1, 1, 1)).astype(np.int32); dens = np.array([0.0, 0.3, 0.6, 0.9, 1.0])
    lm = sub(W, 0.15); mo = sub(M, 0.3); tl = (M - 1) * rng.integers(0, 2, (N, 8, 16, W))
    t = rng.integers(0, 3, (N, 8, 1, H)); sn = np.where(t == 0, -1, np.where(t == 1, 255, 256 * rng.integers(0, 2, (N, 8, 16, H)) - 1))
    m = sub(L, rng.choice(dens, (N, 8, 1, L))); fr = sub(RO * L, rng.choice(dens, (N, 8, 1, RO * L)))
    for x in (m, fr):
        x[..., 0] = 255; x[..., -1] = 255
        z = rng.random(x.shape[-1]) < 0.3; z[0] = True; z[-1] = True
        x[:, 7, 0:8][:, :, z] = 0; x[:, 7, 10:16][:, :, z] = 255
    return pack(w, lm, tl, mo, sn, m, fr)
def setup_inputs_late(rng):
    w, lm, tl, mo, sn, m, fr = base(rng)
    lm = mono(rng, W, rng.choice(np.array([0.5, 0.6]), (N, 8, 1, W)), 160)
    pool = mono(rng, 8192, 0.5, 255); u, v = sums(w, pool)
    aim = np.where(np.arange(8) % 2 == 1, H - 1, 0)[:, None]
    k = np.argmax(((((u * v) >> 5) + u) & (H - 1)) == aim, axis=2)
    mo[..., M - 1:] = np.take_along_axis(pool, k[:, :, None, None], 3); sn[..., 0] = -1; sn[..., H - 1] = -1
    x = mono(rng, 4, 0.6, 255); u, v = sums(w, x); c0 = (((u * v) >> 5) + w[:, :, 0, 2:3] * u) & (W - 1)
    np.put_along_axis(lm, c0[:, :, None], x, 3); np.put_along_axis(tl[:, :, 0], c0, M - 1, 2)
    for t in (1, 2):
        fr[..., t * L + N * CAP + 24:t * L + N * CAP + 28] = x
    one = mono(rng, 1, 0.4, 255)
    for g in (3, 4):
        fr[:, g, :, :L] = one[:, g]
    s = (w, lm, tl, mo, sn, m, fr); plant(rng, *s, until=2, n=24); return pack(*s)
def setup_inputs_spread(rng):
    w = np.tile((np.exp2(7 * rng.random((1, 8, 16, 3))) - 1).astype(np.int32), (N, 1, 1, 1)); dens = np.array([0.3, 0.7, 1.0])
    lm = uneven(rng, W, rng.choice(np.array([0.2, 0.4]), (N, 8, 1, W))); mo = uneven(rng, M, 0.4)
    tl = np.minimum(M * rng.random((N, 8, 16, W)) ** 3, M - 1).astype(np.int32); sn = uneven(rng, H, 0.7) - 1
    m = uneven(rng, L, rng.choice(dens, (N, 8, 1, L))); fr = uneven(rng, RO * L, rng.choice(dens, (N, 8, 1, RO * L)))
    s = (w, lm, tl, mo, sn, m, fr); plant(rng, *s); return pack(*s)
def check_inputs(d):
    bad = []
    for k, lo, hi in (("lm", 0, 255), ("tl", 0, M - 1), ("mo", 0, 255), ("sn", -1, 255), ("fm", 0, 255), ("fr", 0, 255), ("wk", 0, 127)):
        x = np.asarray(d[k]).astype(np.float32)
        if not (np.all(x >= lo) and np.all(x <= hi)): bad.append("range of " + k)
        elif np.any(x != np.floor(x)): bad.append("whole numbers in " + k)
    if np.any(d["wk"] != d["wk"][:1]): bad.append("wk alike on all ranks")
    return bad
def reference(lm, tl, mo, sn, fm, fr, wk):
    lead, tail, mon, seen, front, fill, w = [x.astype(np.float32).astype(np.int32).reshape(N, 8, 16, -1) for x in (lm, tl, mo, sn, fm, fr, wk)]
    st = (lead, tail, seen, front, tail[..., :L], np.zeros((N, 8, L), np.int64))
    for t in range(RO):
        st = turn(st, probe(w, st[0], st[1], mon, st[3]), fill[..., t * L:(t + 1) * L])
    return {"yl": st[0].reshape(N, 128, W).astype(np.float32).astype(BF), "yf": st[3].reshape(N, 128, L).astype(np.float32).astype(BF)}

@@ -1,0 +1,667 @@
+from concourse.bass import DstId, RemoteDMATransfer
+from concourse.mybir import AluOpType as A, ActivationFunctionType as F
+
+BF, FP, I32, U16 = "bfloat16", "float32", "int32", "uint16"
+POOLS = {
+    "PLFP": ["LANE", "BASE", "BD", "L1", "L2", "L6", "HASF", "NOH", "VH", "PLF", "S3", "S4", "NN", "NONE", "N8", "CH", "A1", "A2",
+             "A3", "KA", "KH", "WIN", "DD", "NA", "PLB"],
+    "PLI": ["TPR", "TAL", "KK", "KC", "C0T", "C0I", "CPR", "CHH", "DI", "KEY", "CPS"],
+    "PLU": ["GL", "LSEL", "PL", "SLOT", "PL2", "LLa", "LLb"],
+}
+SIZES = {
+    BF: {"TAB": 6400, "MO": 2048, "FR": 1024, "M": 1280, "BLK": 128, "IDN": 128, "Z": 128, "NTR": 128, "ONES": 128, "DK": 128, "WBU": 128,
+         "WBV": 128, "KUH": 128, "KUL": 128, "IDM": 128, "RHK": 256, "JC": 256, "KB": 2, "SEG": 256, "C255": 256, "ZER": 256, "C256": 64,
+         "WU": 2048, "WV": 2048, "VN": 2048, "MS": 2048, "SEL": 2048, "TRI": 2048, "MREF": 192, "MX": 4096, "MXR": 3072, "X": 4096,
+         "MN": 256, "ZQ": 256, "ZX": 4096, "R": 4352, "TT": 4096, "PCB": 256, "E": 64, "CS": 64, "KPB": 32, "EQ": 4096, "DUPS": 256,
+         "VAL": 256, "SM0": 1280, "SM1": 1280, "SM2": 1280, "SM3": 1280},
+    FP: {"TL": 2304, "PF": 4, "WF": 4, "WN": 4, "K0": 1, "CAP": 256, "TRC": 16, "ROW": 16, "SELM": 32, "NBC": 2, "COLF": 32, "SC": 256,
+         "YY": 256, "SL": 64, "S2": 32, "TGF": 256, "SELG": 256, "LT": 768, "NB": 256, "MT": 256, "MK": 256, "MT1": 256, "MT2": 256,
+         "MKA": 256, "KF": 16, "NKF": 16, "EQT": 1280, "ST0": 1280, "ST1": 1280, "ST2": 1280},
+    I32: {"TLI": 2048, "WKI": 3, "CI": 256, "CM": 256, "PI": 1, "PR": 1, "PG": 1, "CG": 128, "KWI": 128, "KWT": 128, "UI": 512, "PRD": 256,
+          "AR": 256, "ARF": 192, "CT": 256, "TUI": 32, "HP": 256, "HI": 256, "CUI": 32, "KP": 32},
+    U16: {"LST": 256, "LSTR": 192, "TG": 256, "HL": 256, "KR": 256},
+}
+SCRATCH = {"FL": ("sbuf", [128, 16, 256], BF)}
+for _d in SIZES:
+    for _n in SIZES[_d]:
+        SCRATCH[_n] = ("sbuf", [128, SIZES[_d][_n]], _d)
+for _n, _d in (("PLFP", FP), ("PLI", I32), ("PLU", U16)):
+    SCRATCH[_n] = ("sbuf", [128, 16 * len(POOLS[_n])], _d)
+for _b in range(8):
+    SCRATCH["b%d" % _b] = ("psum", [128, 512], FP)
+_DMAS = ["wk", "fm", "fr", "lm", "tl", "mo", "sn", "rf", "yl", "yf"]
+SEMAPHORES = (["sv", "ss", "st", "sg", "loc"] + ["d" + x for x in _DMAS]
+              + ["pre%d" % t for t in range(4)] + ["fm%d" % t for t in range(1, 5)] + ["ft%d" % t for t in range(1, 4)])
+L_S0 = [(12, 14), (14, 16), (8, 10)]
+L_S = [(12, 14), (14, 16), (8, 10)]
+P_S = [(4, 6), (6, 8), (12, 14), (14, 16)]
+P_V = [(0, 4), (8, 12)]
+S_S = [(4, 6), (6, 8), (14, 16)]
+ZX_S, EQ_S = 4, 10
+EST = {"vL": 0.47, "vT": 0.68, "vR": 0.26, "sG": 0.70, "sP": 0.53}
+
+US = {"v": {"FL": 0.45, "TT": 1.35, "R": 0.48, "ZX": 0.16, "UI": 0.3, "PRD": 0.28, "AR": 0.2, "CT": 0.2, "LST": 0.2, "LSTR": 0.2, "SC": 0.26,
+            "YY": 0.26, "TG": 0.42, "ZQ": 0.42, "SM": 0.9, "ST": 0.9, "LM": 0.9, "TL": 1.3, "MT": 0.45, "MKAa": 0.4, "KR": 0.26, "EQ": 0.12,
+            "VN": 0.9, "ARF": 0.2, "HP": 0.15, "HI": 0.15, "HL": 0.15},
+      "s": {"X": 0.72, "FL": 0.26, "R": 0.48, "MX": 0.21, "MXR": 0.21, "ZX": 0.26, "WU": 1.75, "WV": 1.75, "SN": 3.4, "TGF": 0.42, "NB": 0.26,
+            "PCB": 0.42, "SELG": 0.42, "VAL": 0.42, "MT": 0.26, "MK": 0.26, "DUPS": 0.26, "MN": 0.26, "Rm": 0.26, "EQT": 0.13}}
+LOADED = {"dlm": 6.0, "dtl": 10.0, "dmo": 13.0, "dfr": 14.0, "dsn": 18.0, "drf": 19.0}
+WINDOW, WAKE = {"v": 60, "s": 4, "t": 60, "g": 1, "y": 1}, 0.1
+
+
+def rank_program(g, core, T, topo):
+    rank = T.rank_of(core)
+    if rank is None:
+        return
+    peers = [r for r in range(len(T.cores)) if r != rank]
+    S = T.sem
+    Q = {"v": g.vector, "s": g.scalar, "t": g.tensor, "g": g, "y": g.sync}
+    SN = {"v": "sv", "s": "ss", "t": "st", "g": "sg"}
+    cnt = {k: 0 for k in SEMAPHORES}
+    known = {e: {} for e in Q}
+    snap, wr_, rd_, ps_ = {}, {}, {}, {}
+    P = {}
+    for pn in POOLS:
+        for i, n in enumerate(POOLS[pn]):
+            P[n] = T[pn][:, 16 * i:16 * i + 16]
+
+    def is_bank(k):
+        return k[0] == "b" and k[1:].isdigit()
+
+    def sync(e, toks):
+        need = {}
+        for s, v in toks:
+            if known[e].get(s, 0) < v:
+                need[s] = max(need.get(s, 0), v)
+        drop = [s for s in need if any(s2 != s and snap.get((s2, need[s2]), {}).get(s, 0) >= need[s] for s2 in need)]
+        for s, v in need.items():
+            if s not in drop:
+                Q[e].wait_ge(S[s], v)
+        for s, v in need.items():
+            known[e][s] = max(known[e].get(s, 0), v)
+            for a, b in snap.get((s, v), {}).items():
+                known[e][a] = max(known[e].get(a, 0), b)
+
+    rec = []
+
+    def add(e, sem, inc, rd, wr, cost, late, call):
+        n, before, order = len(rec), set(), set()
+        for k in list(rd) + list(wr):
+            if is_bank(k):
+                cur = ps_.setdefault(k, [None, [], []])
+                if cur[0] != e:
+                    ps_[k] = cur = [e, [], cur[1]]
+                before.update(cur[2])
+                if e == "t":
+                    order.update(cur[1][-1:])
+                cur[1].append(n)
+            elif k in rd:
+                before.update(wr_.get(k, []))
+        for k in wr:
+            if not is_bank(k):
+                before.update(wr_.get(k, []) + rd_.get(k, []))
+        for k in rd:
+            rd_.setdefault(k, []).append(n)
+        for k in wr:
+            wr_[k], rd_[k] = [n], []
+        before.discard(n)
+        rec.append((e, sem, inc, before, order, cost, late, call))
+        return n
+
+    def op(e, rd, wr, name, *a, **kw):
+        f = {"cp": lambda: g.vector.tensor_copy, "tt": lambda: g.vector.tensor_tensor, "ts": lambda: g.vector.tensor_scalar,
+             "scan": lambda: g.vector.tensor_tensor_scan, "ms": lambda: g.vector.memset, "act": lambda: g.scalar.activation,
+             "mm": lambda: g.tensor.matmul, "iota": lambda: g.iota}[name]()
+        key = wr[0].rstrip("0123456789")
+        c = (0.3 if wr[0] in ("b5", "b6") else 0.045) if e == "t" else US[e].get(key, 0.11) if e in US else 0.3
+        add(e, SN[e], 1, rd, wr, c, 0.0, lambda: f(*a, **kw))
+
+    def dma(e, sem, out, in_, rd, wr):
+        return add(e, sem, 16, rd, wr, 0.1, LOADED.get(sem, 2.5), lambda: Q[e].dma_start(out, in_))
+
+    def issue():
+        todo = {e: [i for i in range(len(rec)) if rec[i][0] == e] for e in Q}
+        now, fin = {e: 0.0 for e in Q}, {}
+        for i in range(len(rec)):
+            if rec[i][0] is None:
+                fin[i] = None
+        left, pos = sum(len(x) for x in todo.values()), {}
+        while left:
+            best = None
+            for e in Q:
+                head = pick = None
+                for i in todo[e][:WINDOW[e]]:
+                    st = now[e]
+                    for d in rec[i][3] | rec[i][4]:
+                        f = fin.get(d)
+                        if rec[d][0] is None:
+                            f = fin.get(rec[d][3])
+                            f = None if f is None else f + 2.0
+                        if f is None:
+                            st = None
+                            break
+                        if d in rec[i][3] and f > now[e] - WAKE:
+                            st = max(st, f + WAKE)
+                    if head is None:
+                        head = (st, i)
+                        if st is not None:
+                            pick = (st, i)
+                    elif st is not None and (pick is None or (st < pick[0] and (head[0] is None or st + rec[i][5] <= head[0] + 0.04))):
+                        pick = (st, i)
+                if pick is not None and (best is None or pick[0] < best[0]):
+                    best = (pick[0], e, pick[1])
+            st, e, i = best
+            _, sem, inc, before, order, cost, late, call = rec[i]
+            todo[e].remove(i)
+            left -= 1
+            now[e] = st + cost
+            fin[i] = st + cost + late
+            toks = []
+            for d in before:
+                if not (e == "t" and rec[d][0] == "t"):
+                    toks.append(pos[d] if rec[d][0] is not None else (rec[d][1], rec[d][2]))
+            sync(e, toks)
+            cnt[sem] += inc
+            pos[i] = (sem, cnt[sem])
+            ins = call()
+            if sem != "loc":
+                ins.then_inc(S[sem], inc)
+            snap[pos[i]] = dict(known[e])
+
+    def V(rd, wr, name, *a):
+        op("v", rd, wr, name, *a)
+
+    def ops(*rows):
+        for r in rows:
+            name, out, ins = r[0], r[1], [x for x in r[2:] if isinstance(x, str)]
+            V(ins, [out], name, *[ap(x) if isinstance(x, str) else x for x in r[1:]])
+
+    def ap(n):
+        return P[n] if n in P else T[n][:]
+
+    def SA(rd, wr, out, in_, fn=F.Copy, **kw):
+        op("s", rd, wr, "act", out, in_, fn, **kw)
+
+    def mm(rd, bank, out, lhsT, rhs, start, stop):
+        op("t", rd, [bank], "mm", out, lhsT, rhs, start, stop)
+
+    def blk(name, r):
+        return T[name][:, 128 * r:128 * (r + 1)]
+
+    lands = {}
+
+    def land(key, sem):
+        cnt[sem] += 12
+        lands[sem] = len(rec)
+        wr_[key] = [len(rec)]
+        rec.append((None, sem, 12, None, set(), 0.0, 0.0, None))
+
+    def send(sem, pieces, rd):
+        tr = []
+        for n, p in enumerate(peers):
+            rid, pid, _ = topo.addr(T.cores[p])
+            dst, src = pieces(p)
+            eng = topo.engines(core, T.cores[p])
+            tr.append(RemoteDMATransfer(dst_ids=[DstId(rid=rid, pnc=pid)], dma_engine_mask=sum(1 << x for x in eng[4 * n:4 * n + 4]),
+                                        remote_sem=S[sem], src=src, dst=dst))
+        n = add("g", "loc", 12, rd, [], 0.3, 1.0, lambda: g.remote_dma_fused(tr, local_sem=S.loc))
+        rec[lands[sem]] = (None, sem, 12, n, set(), 0.0, 0.0, None)
+
+    for t in range(4):
+        land("SM%dp" % t, "pre%d" % t)
+    for t in range(1, 5):
+        land("M%dr" % t, "fm%d" % t)
+    for t in range(1, 4):
+        land("LT%dr" % t, "ft%d" % t)
+    dma("y", "dwk", T.WKI[:], T.wk[:], [], ["WKI"])
+    dma("s", "dfm", T.M[:, 0:256], T.fm[:], [], ["M0"])
+    dma("y", "dlm", T.TAB[:, 4096:6144], T.lm[:], [], ["LM"])
+    dma("y", "dtl", T.TLI[:], T.tl[:], [], ["TLI"])
+    dma("y", "dmo", T.MO[:], T.mo[:], [], ["MO"])
+    dma("y", "dfr", T.FR[:], T.fr[:], [], ["FR"])
+    dma("y", "dsn", T.TAB[:, 0:4096], T.sn[:], [], ["SN"])
+    rf = []
+    for t in range(4):
+        rf.append(dma("y", "drf", T["SM%d" % t][:, 256 * rank:256 * rank + 48], T.fr[:, 256 * t + 48 * rank:256 * t + 48 * rank + 48], [], ["SM%do" % t]))
+        rf.append(dma("y", "drf", T.M[:, 256 * t + 448:256 * t + 512], T.fr[:, 256 * t + 192:256 * t + 256], [], ["M%df" % (t + 1)]))
+    for t in range(4):
+        wr_["SM%do" % t], wr_["M%df" % (t + 1)] = list(rf), list(rf)
+
+    op("g", [], ["CI"], "iota", T.CI[:], [[1, 256]], 0, 0)
+    op("g", [], ["PI"], "iota", T.PI[:], [[0, 1]], 0, 1)
+    for t in range(3):
+        for d in range(4):
+            op("g", [], ["ST%d_%d" % (t, d)], "iota", T["ST%d" % t][:, 256 * d:256 * d + 48], [[0, 48]], 0, 0, allow_small_or_imprecise_dtypes=True)
+        op("g", [], ["LT%df" % (t + 1)], "iota", T.LT[:, 256 * t + 192:256 * t + 256], [[0, 64]], 0, 0, allow_small_or_imprecise_dtypes=True)
+    for t in range(4):
+        send("pre%d" % t, lambda p: (T["SM%d" % t][:, 256 * rank:256 * rank + 48], T.FR[:, 256 * t + 48 * p:256 * t + 48 * p + 48]), ["FR"])
+    rp, gp, pf = T.PF[:, 0:1], T.PF[:, 1:2], T.PF[:, 2:3]
+    wc, kc = T.WF[:, 0:1], T.WF[:, 2:3]
+    V([], ["ONES"], "ms", T.ONES[:], 1.0)
+    ops(("ts", "CM", "CI", 15, None, A.bitwise_and), ("ts", "PR", "PI", 15, None, A.bitwise_and), ("ts", "PG", "PI", 4, None, A.arith_shift_right))
+    V(["CI"], ["CG"], "ts", T.CG[:], T.CI[:, 0:128], 4, None, A.arith_shift_right)
+    V(["PR"], ["PF0"], "cp", rp, T.PR[:])
+    V(["PG"], ["PF1"], "cp", gp, T.PG[:])
+    V(["PI"], ["PF2"], "cp", pf, T.PI[:])
+    V(["CG", "PF1"], ["BLK"], "ts", T.BLK[:], T.CG[:], gp, None, A.is_equal)
+    V(["CI", "PF2"], ["IDN"], "ts", T.IDN[:], T.CI[:, 0:128], pf, None, A.is_equal)
+    V(["WKI"], ["WF"], "cp", T.WF[:, 0:3], T.WKI[:])
+    V(["IDN", "WF"], ["DK"], "ts", T.DK[:], T.IDN[:], kc, None, A.mult)
+    mm(["ONES", "DK"], "b0", T.b0[:, 0:128], T.ONES[:], T.DK[:], True, True)
+    V(["BLK", "WF"], ["WBU"], "ts", T.WBU[:], T.BLK[:], wc, None, A.mult)
+    V(["BLK", "WF"], ["WBV"], "ts", T.WBV[:], T.BLK[:], T.WF[:, 1:2], None, A.mult)
+    V(["WKI"], ["WN"], "ts", T.WN[:, 0:3], T.WKI[:], -1.0, None, A.mult)
+    V(["b0", "WF"], ["KWI"], "ts", T.KWI[:], T.b0[:, 0:128], wc, None, A.mult)
+    ops(("ts", "KWT", "KWI", 2040, None, A.bitwise_and), ("tt", "KUH", "KWT", "BLK", A.mult),
+        ("ts", "KWT", "KWI", 7, None, A.bitwise_and), ("tt", "KUL", "KWT", "BLK", A.mult))
+
+    def candidates(n, src, key, lst, lkey, ar, akey):
+        mm(["WBU"] + key, "b0", T.b0[:, 0:n], T.WBU[:], src, True, True)
+        mm(["WBV"] + key, "b0", T.b0[:, n:2 * n], T.WBV[:], src, True, True)
+        mm(["KUH"] + key, "b1", T.b1[:, 0:n], T.KUH[:], src, True, False)
+        mm(["KUL"] + key, "b1", T.b1[:, 0:n], T.KUL[:], src, False, True)
+        V(["b0"], ["UI"], "cp", T.UI[:, 0:2 * n], T.b0[:, 0:2 * n])
+        V(["UI"], ["UI"], "ts", T.UI[:, 0:2 * n], T.UI[:, 0:2 * n], 4095, None, A.bitwise_and)
+        V(["UI"], ["PRD"], "tt", T.PRD[:, 0:n], T.UI[:, 0:n], T.UI[:, n:2 * n], A.mult)
+        V(["PRD"], [akey], "ts", ar, T.PRD[:, 0:n], 5, 2047, A.arith_shift_right, A.bitwise_and)
+        V([akey, "b1"], ["CT"], "tt", T.CT[:, 0:n], ar, T.b1[:, 0:n], A.add)
+        V(["CT"], ["CT"], "ts", T.CT[:, 0:n], T.CT[:, 0:n], 2047, None, A.bitwise_and)
+        V(["CT"], [lkey], "cp", lst, T.CT[:, 0:n])
+
+    for i in range(16):
+        SA(["M0"], ["MX%d" % i], T.MX[:, i::16], T.M[:, 0:256])
+    candidates(256, T.M[:, 0:256], ["M0"], T.LST[:], "LST", T.AR[:], "AR")
+
+    V(["CM"], ["Z"], "ts", T.Z[:], T.CM[:, 0:128], -99.0, None, A.add)
+    ops(("tt", "Z", "Z", "BLK", A.mult), ("ts", "Z", "Z", 99.0, None, A.add))
+    for r in range(16):
+        V(["Z"], ["MS%d" % r], "ts", blk("MS", r), T.Z[:], float(r), None, A.is_equal)
+    MSK = ["MS%d" % r for r in range(16)]
+    V(MSK, ["VN"], "ts", T.VN[:], T.MS[:], -4096.0, None, A.mult)
+    SA(MSK + ["WN"], ["WU"], T.WU[:], T.MS[:], scale=T.WN[:, 0:1])
+    SA(MSK + ["WN"], ["WV"], T.WV[:], T.MS[:], scale=T.WN[:, 1:2])
+    V(["CI", "PF2"], ["IDM"], "ts", T.IDM[:], T.CI[:, 0:128], pf, -1.0, A.is_equal, A.mult)
+    ops(("ts", "SEG", "CM", 0.0, None, A.is_gt), ("ts", "CAP", "CM", -0.0625, 1.0, A.mult, A.add), ("ts", "JC", "CAP", 2048.0, None, A.mult))
+    V(["CM", "PF0", "WF"], ["RHK"], "ts", T.RHK[:], T.CM[:], rp, kc, A.is_equal, A.mult)
+    V([], ["C255"], "ms", T.C255[:], 255.0)
+    V([], ["ZER"], "ms", T.ZER[:], 0.0)
+    V(["TLI"], ["TL"], "cp", T.TL[:, 0:2048], T.TLI[:])
+    V(["M0"], ["MN"], "ts", T.MN[:], T.M[:, 0:256], -1.0, 255.0, A.mult, A.add)
+
+    def constants_2():
+        V(["CI", "PF0"], ["ROW"], "ts", T.ROW[:], T.CI[:, 0:16], rp, None, A.is_equal)
+        V(["CI", "PF0"], ["TRC"], "ts", T.TRC[:], T.CI[:, 0:16], rp, None, A.is_gt)
+        V(["WF"], ["KB"], "cp", T.KB[:], T.WF[:, 1:3])
+        V(["CM", "PF0"], ["NTR"], "ts", T.NTR[:], T.CM[:, 0:128], rp, -1.0, A.is_le, A.mult)
+        ops(("tt", "NTR", "NTR", "BLK", A.mult))
+        V(["CI", "PF0"], ["COLF"], "ts", T.COLF[:], T.CI[:, 0:32], rp, None, A.add)
+        ops(("ts", "SELM", "COLF", 16.0, 12288.0, A.is_equal, A.mult))
+        V(["CI"], ["LANE"], "ts", P["LANE"], T.CI[:, 0:16], 16.0, None, A.mult)
+        V(["LANE", "PF0"], ["LANE"], "ts", P["LANE"], P["LANE"], rp, None, A.add)
+        ops(("ts", "BASE", "LANE", 16.0, 16.0, A.mult, A.add), ("ts", "BD", "LANE", -15.0, 4080.0, A.mult, A.add),
+            ("ts", "L1", "LANE", 1024.0, None, A.add), ("ts", "L2", "LANE", 2048.0, None, A.add), ("ts", "L6", "LANE", 6144.0, None, A.add))
+        V(["PF0"], ["NBC0"], "ts", T.NBC[:, 0:1], rp, 0.0, None, A.is_gt)
+        V(["PF0"], ["NBC1"], "ts", T.NBC[:, 1:2], rp, 0.0, 4096.0, A.is_equal, A.mult)
+        for d in range(4):
+            V([], ["C256_%d" % d], "ms", T.C256[:, 16 * d:16 * d + 16], 256.0 * d)
+        for t in range(3):
+            V(["FR"], ["MREF%d" % t], "cp", T.MREF[:, 64 * t:64 * t + 64], T.FR[:, 256 * t + 192:256 * t + 256])
+
+    def constants_s(part):
+        if part == 0:
+            SA(["BLK", "ROW"], ["SEL0"], blk("SEL", 0), T.BLK[:], scale=T.ROW[:, 0:1])
+            mm(["SEL0", "KB"], "b7", T.b7[:, 200:201], blk("SEL", 0), T.KB[:, 1:2], True, True)
+        if part == 1:
+            for r in range(1, 16):
+                SA(["BLK", "ROW"], ["SEL%d" % r], blk("SEL", r), T.BLK[:], scale=T.ROW[:, r:r + 1])
+        if part == 2:
+            for i in range(16):
+                SA(MRK, ["MXR%d" % i], T.MXR[:, i::16], T.MREF[:])
+            wr_["MXR"] = [n for i in range(16) for n in wr_["MXR%d" % i]]
+        if part == 3:
+            for r in range(16):
+                SA(["MS%d" % r, "TRC"], ["TRI%d" % r], blk("TRI", r), blk("MS", r), scale=T.TRC[:, r:r + 1])
+    C256K = ["C256_%d" % d for d in range(4)]
+    MRK = ["MREF0", "MREF1", "MREF2"]
+
+    def merge(a, b):
+        ta = tb = 0.0
+        a, b = list(a), list(b)
+        while a or b:
+            if b and (not a or tb + b[0][0] <= ta + a[0][0]):
+                tb += b[0][0]
+                b.pop(0)[1]()
+            else:
+                ta += a[0][0]
+                a.pop(0)[1]()
+
+    def pipe(chunks, gather, diff, post, after, ahead=0):
+        out, n = [], len(chunks)
+
+        def g1(k):
+            if k >= ahead:
+                gather(chunks[k])
+            diff(chunks[k], "b%d" % (5 + k % 2))
+
+        def p1(k):
+            post(chunks[k], "b%d" % (5 + k % 2))
+            after(chunks[k])
+        for k in range(n + 1):
+            if k < n:
+                out.append((EST["sG"], lambda k=k: g1(k)))
+            if k > 0:
+                out.append((EST["sP"], lambda k=k: p1(k - 1)))
+        return out
+
+    def share(sc):
+        return [(c, c + 2) for c in range(0, 16, 2) if (c, c + 2) not in sc]
+
+    def sums(bank, sel, c0, c1, done):
+        done.update(range(c0, c1))
+        k = c0 // 4 * 4
+        if not all(c in done for c in range(k, k + 4)):
+            return
+        for r in range(16):
+            mm(["FL%d" % c for c in range(k, k + 4)] + ([sel] if sel == "VN" else ["MS%d" % r]), bank, T[bank][:, 16 * k:16 * k + 64], blk(sel, r),
+               T.FL[:, k:k + 4, 16 * r:16 * r + 16], False, bool(len(done) == 16 and r == 15))
+
+    def spread_keys():
+        V(["KEY"], ["KPa"], "ts", T.KP[:, 0:16], P["KEY"], 8160, None, A.bitwise_and)
+        V(["KEY"], ["KPb"], "ts", T.KP[:, 16:32], P["KEY"], 31, None, A.bitwise_and)
+        V(["KPa", "KPb"], ["KPB"], "cp", T.KPB[:], T.KP[:])
+        V(["KEY"], ["NKF"], "ts", T.NKF[:], P["KEY"], -1.0, None, A.mult)
+        for r in range(16):
+            mm(["SEL%d" % r, "KPB"], "b3", T.b3[:, r:256:16], blk("SEL", r), T.KPB[:, 0:16], True, False)
+            mm(["SEL%d" % r, "KPB"], "b3", T.b3[:, r:256:16], blk("SEL", r), T.KPB[:, 16:32], False, True)
+        ops(("cp", "KF", "KEY"))
+
+    def equal_pairs(first_s):
+        V(["b3"], ["KR"], "cp", T.KR[:], T.b3[:, 0:256])
+        off = 0
+        for c in range(first_s, 16):
+            n = 256 - 16 * c
+            SA(["b3", "NKF"], ["EQT%d" % c], T.EQT[:, off:off + n], T.b3[:, 16 * c:256], F.Abs, bias=T.NKF[:, c:c + 1])
+            SA(["EQT%d" % c], ["EQ%d" % c], T.EQ[:, 272 * c:256 * c + 256], T.EQT[:, off:off + n], F.Relu, bias=1.0, scale=-1.0)
+            off += n
+        mm(["IDN", "ZER"], "b4", T.b4[:, 0:256], T.IDN[:], T.ZER[:], True, False)
+        for c in range(16):
+            if c < first_s:
+                V(["KR", "KF"], ["EQ%d" % c], "ts", T.EQ[:, 272 * c:256 * c + 256], T.KR[:, 16 * c:256], T.KF[:, c:c + 1], None, A.is_equal)
+            if c < 15:
+                mm(["BLK", "EQ%d" % c], "b4", T.b4[:, 16 * c + 16:256], T.BLK[:], T.EQ[:, 272 * c + 16:256 * c + 256], False, c == 14)
+
+    def earlier_lanes():
+        SA(["b4"], ["DUPS"], T.DUPS[:], T.b4[:, 0:256])
+
+    def count_earlier():
+        for r in range(16):
+            mm(["TRI%d" % r] + ["EQ%d" % c for c in range(16)], "b7", T.b7[:, 128:144], blk("TRI", r), T.EQ[:, r::272], r == 0, False)
+        for r in range(16):
+            mm(["MS%d" % r, "DUPS"], "b7", T.b7[:, 128:144], blk("MS", r), T.DUPS[:, r::16], False, r == 15)
+
+    def winners():
+        V(["KF", "L6"], ["A1"], "tt", P["A1"], T.KF[:], P["L6"], A.subtract)
+        V(["b7"], ["WIN"], "ts", P["WIN"], T.b7[:, 128:144], 0.0, None, A.is_equal)
+        ops(("tt", "A2", "A1", "WIN", A.mult))
+
+    LM, SNW = T.TAB[:, 4096:6144], T.TAB[:, 0:4096]
+    MXK, ZXK = ["MX%d" % i for i in range(16)], ["ZX%d" % i for i in range(16)]
+    RK = ["R%d" % c for c in range(16)] + ["Rm"]
+
+    for t in range(4):
+        m = T.M[:, 256 * t:256 * t + 256]
+        nx = 256 * (t + 1)
+        mk = ["M0"] if t == 0 else ["M%d%s" % (t, x) for x in "rof"]
+        LS = L_S if t else L_S0
+
+        def lsrc(c0, c1):
+            if t and c0 >= 12:
+                o = 64 * (t - 1) + 16 * (c0 - 12)
+                return (T.LSTR[:, o:o + 16 * (c1 - c0)], T.MXR[:, 16 * o:16 * o + 256 * (c1 - c0)], ["LSTR"], ["MXR"])
+            return (T.LST[:, 16 * c0:16 * c1], T.MX[:, 256 * c0:256 * c1], ["LST"], MXK)
+
+        def lgather(ch):
+            o, mx, k1, k2 = lsrc(*ch)
+            SA(["LM"] + k1, ["X%d" % ch[0]], T.X[:, 256 * ch[0]:256 * ch[1]], LM.indirect(o))
+
+        def ldiff(ch, b):
+            o, mx, k1, k2 = lsrc(*ch)
+            mm(["IDN", "X%d" % ch[0]], b, T[b][:], T.IDN[:], T.X[:, 256 * ch[0]:256 * ch[1]], True, False)
+            mm(["IDM"] + k2, b, T[b][:], T.IDM[:], mx, False, True)
+
+        def lpost(ch, b):
+            for c in range(ch[0], ch[1]):
+                o = 256 * (c - ch[0])
+                SA([b], ["FL%d" % c], T.FL[:, c, :], T[b][:, o:o + 256], F.Relu)
+        mm(["BLK", "RHK"], "b3", T.b3[:, 0:256], T.BLK[:], T.RHK[:], True, False)
+        mm(["IDN", "JC"], "b3", T.b3[:, 0:256], T.IDN[:], T.JC[:], False, False)
+        lst8 = set()
+        vp = share(LS)
+        st = pipe(LS, lgather, ldiff, lpost, lambda ch: sums("b3", "VN", ch[0], ch[1], lst8))
+        for k, w in ((0, "WU"), (16, "WV")):
+            for r in range(16):
+                mm([w] + mk, "b2", T.b2[:, k:k + 16], blk(w, r), T.M[:, 256 * t + r:256 * t + 256:16], r == 0, r == 15)
+        vt = []
+        for c in [c for p in vp for c in range(*p)]:
+            def lv(c=c):
+                o, mx, k1, k2 = lsrc(c, c + 1)
+                V(["LM"] + k1 + k2, ["FL%d" % c], "tt", T.FL[:, c, :], LM.indirect(o), mx, A.is_gt)
+                sums("b3", "VN", c, c + 1, lst8)
+            vt.append((EST["vL"] + (1.0 if t and not vt else 0.0), lv))
+        merge(vt, st)
+        V(["b2"], ["TUI"], "ts", T.TUI[:], T.b2[:, 0:32], -1.0, None, A.mult)
+        ops(("ts", "TUI", "TUI", 4095, None, A.bitwise_and))
+        V(["TUI"], ["TPR"], "tt", P["TPR"], T.TUI[:, 0:16], T.TUI[:, 16:32], A.mult)
+        ops(("ts", "TAL", "TPR", 5, 2047, A.arith_shift_right, A.bitwise_and))
+        if t == 0:
+            constants_2()
+            SA(["SN"], ["SN"], T.TAB[:, 0:4096], T.TAB[:, 0:4096], F.Identity, bias=255.0, scale=-1.0)
+        V(["SEG", "b3"], ["SC"], "scan", T.SC[:], T.SEG[:], T.b3[:, 0:256], 0.0, A.mult, A.max)
+        V(["SC"], ["KK"], "cp", P["KK"], T.SC[:, 15::16])
+        ops(("ts", "KK", "KK", 127, None, A.bitwise_and))
+        V(["KK", "TUI"], ["KC"], "tt", P["KC"], P["KK"], T.TUI[:, 0:16], A.mult)
+        ops(("tt", "KC", "KC", "TAL", A.add), ("ts", "KC", "KC", 2047, None, A.bitwise_and), ("cp", "GL", "KC"))
+        V(["TL", "GL"], ["TG"], "cp", T.TG[:], T.TL[:, 0:2048].indirect(P["GL"]))
+        V(["LM", "GL", "MN"], ["ZQ"], "tt", T.ZQ[:], LM.indirect(P["GL"]), T.MN[:], A.add)
+        SA(mk, ["Rm"], T.R[:, 4096:4352], m)
+        if t == 3:
+            V(["TUI", "K0"], ["C0T"], "ts", P["C0T"], T.TUI[:, 0:16], T.K0[:], None, A.mult)
+            V(["SC"], ["NOH"], "ts", P["NOH"], T.SC[:, 15::16], 128.0, None, A.is_lt)
+            ops(("tt", "C0T", "C0T", "TAL", A.add), ("ts", "C0I", "C0T", 2047, None, A.bitwise_and), ("tt", "A1", "C0I", "L2", A.subtract),
+                ("tt", "A2", "A1", "NOH", A.mult), ("tt", "KEY", "A2", "L6", A.add))
+            spread_keys()
+
+        def pgather(ch):
+            SA(["MO", "TG"], ["X%d" % ch[0]], T.X[:, 256 * ch[0]:256 * ch[1]], T.MO[:].indirect(T.TG[:, 16 * ch[0]:16 * ch[1]]))
+        pgather(P_S[0])
+        pgather(P_S[1])
+        for i in range(16):
+            if i < ZX_S:
+                SA(["ZQ"], ["ZX%d" % i], T.ZX[:, i::16], T.ZQ[:])
+            else:
+                V(["ZQ"], ["ZX%d" % i], "cp", T.ZX[:, i::16], T.ZQ[:])
+        for b in ("b0", "b1"):
+            mm(["IDN", "ZER"], b, T[b][:, 0:256], T.IDN[:], T.ZER[:], True, False)
+            mm(["WBU", "C255"], b, T[b][:, 0:128], T.WBU[:], T.C255[:, 0:128], False, False)
+            mm(["WBV", "C255"], b, T[b][:, 128:256], T.WBV[:], T.C255[:, 0:128], False, False)
+        if t == 3:
+            equal_pairs(16)
+        nh, done = [0, 0], {}
+
+        def hsum(ch):
+            for c in range(*ch):
+                done[c] = True
+            k = ch[0] // 4 * 4
+            if not all(c in done for c in range(k, k + 4)):
+                return
+            c0, c1, h = k, k + 4, k // 8
+            b, l0, n = "b%d" % h, 16 * c0 - 128 * h, 64
+            nh[h] += 4
+            for o, w in ((0, "WU"), (128, "WV")):
+                for i in range(16):
+                    mm(["R%d" % c for c in range(c0, c1)] + [w], b, T[b][:, o + l0:o + l0 + n], blk(w, i),
+                       T.R[:, 256 * c0 + i:256 * c1:16], False, bool(nh[h] == 8 and o and i == 15))
+
+        def pdiff(ch, b):
+            mm(["IDN", "X%d" % ch[0]], b, T[b][:], T.IDN[:], T.X[:, 256 * ch[0]:256 * ch[1]], True, False)
+            mm(["IDM"] + ZXK, b, T[b][:], T.IDM[:], T.ZX[:, 256 * ch[0]:256 * ch[1]], False, True)
+
+        def ppost(ch, b):
+            SA([b], ["R%d" % c for c in range(*ch)], T.R[:, 256 * ch[0]:256 * ch[1]], T[b][:], F.Relu, scale=-1.0)
+        vt = []
+        for ch in P_V:
+            def pv1(ch=ch):
+                c0, c1 = ch
+                V(["MO", "TG"] + ZXK, ["TT%d" % c0], "tt", T.TT[:, 256 * c0:256 * c1], T.MO[:].indirect(T.TG[:, 16 * c0:16 * c1]),
+                  T.ZX[:, 256 * c0:256 * c1], A.subtract)
+
+            def pv2(ch=ch):
+                c0, c1 = ch
+                V(["TT%d" % c0], ["R%d" % c for c in range(c0, c1)], "ts", T.R[:, 256 * c0:256 * c1], T.TT[:, 256 * c0:256 * c1], -1.0, 0.0, A.mult, A.max)
+                hsum(ch)
+            n = (ch[1] - ch[0]) / 2
+            vt += [(EST["vT"] * n, pv1), (EST["vR"] * n, pv2)]
+        st = pipe(P_S, pgather, pdiff, ppost, hsum, 2)
+        st[0] = (0.2, st[0][1])
+        st[1] = (0.2, st[1][1])
+        if t == 0:
+            constants_s(0)
+        merge(vt, st)
+        if t == 3:
+            earlier_lanes()
+            count_earlier()
+        if t == 0:
+            constants_s(1)
+        if t < 3:
+            SA(["TL", "GL"], ["TGF"], T.TGF[:], T.TL[:, 0:2048].indirect(P["GL"]), F.Identity, bias=8192.0)
+            SA(["TL", "NBC0", "NBC1"], ["NB"], T.NB[:], T.TL[:, 0:256], F.Identity, bias=T.NBC[:, 1:2], scale=T.NBC[:, 0:1])
+
+        def hashes(h):
+            b = "b%d" % h
+            o = slice(128 * h, 128 * h + 128)
+            V([b], ["UI"], "cp", T.UI[:, 0:256], T[b][:, 0:256])
+            V(["UI"], ["UI"], "ts", T.UI[:, 0:256], T.UI[:, 0:256], 4095, None, A.bitwise_and)
+            V(["UI"], ["PRD"], "tt", T.PRD[:, 0:128], T.UI[:, 0:128], T.UI[:, 128:256], A.mult)
+            V(["PRD"], ["HP"], "ts", T.HP[:, o], T.PRD[:, 0:128], 5, None, A.arith_shift_right)
+            V(["HP", b], ["HP"], "tt", T.HP[:, o], T.HP[:, o], T[b][:, 0:128], A.add)
+            V(["HP"], ["HI"], "ts", T.HI[:, o], T.HP[:, o], 4095, None, A.bitwise_and)
+            V(["HI"], ["HL%d" % h], "cp", T.HL[:, o], T.HI[:, o])
+        hashes(0)
+        mm(["IDN", "ZER"], "b4", T.b4[:, 0:256], T.IDN[:], T.ZER[:], True, False)
+        sst = set()
+
+        def sgather(ch):
+            SA(["SN", "HL%d" % (ch[0] // 8)], ["X%d" % ch[0]], T.X[:, 256 * ch[0]:256 * ch[1]], SNW.indirect(T.HL[:, 16 * ch[0]:16 * ch[1]]))
+
+        def sdiff(ch, b):
+            mm(["IDN", "X%d" % ch[0]], b, T[b][:], T.IDN[:], T.X[:, 256 * ch[0]:256 * ch[1]], True, False)
+            mm(["IDM"] + ["R%d" % c for c in range(*ch)], b, T[b][:], T.IDM[:], T.R[:, 256 * ch[0]:256 * ch[1]], False, True)
+
+        def spost(ch, b):
+            for c in range(ch[0], ch[1]):
+                o = 256 * (c - ch[0])
+                SA([b], ["FL%d" % c], T.FL[:, c, :], T[b][:, o:o + 256], F.Square)
+        vt = []
+        for c in [c for p in share(S_S) for c in range(*p)]:
+            def sv(c=c):
+                V(["SN", "HL%d" % (c // 8), "R%d" % c], ["FL%d" % c], "tt", T.FL[:, c, :], SNW.indirect(T.HL[:, 16 * c:16 * c + 16]),
+                  T.R[:, 256 * c:256 * c + 256], A.not_equal)
+                sums("b4", "MS", c, c + 1, sst)
+            vt.append((EST["vL"], sv))
+        vt.insert(2, (1.3, lambda: hashes(1)))
+        merge(vt, pipe(S_S, sgather, sdiff, spost, lambda ch: sums("b4", "MS", ch[0], ch[1], sst)))
+        V(["SC"], ["HASF"], "ts", P["HASF"], T.SC[:, 15::16], 128.0, 16.0, A.is_ge, A.mult)
+        V(["SC"], ["NOH"], "ts", P["NOH"], T.SC[:, 15::16], 128.0, None, A.is_lt)
+        V(["b4", "CAP"], ["YY"], "tt", T.YY[:], T.b4[:, 0:256], T.CAP[:], A.min)
+        V(["YY", "SEG"], ["SC"], "scan", T.SC[:], T.SEG[:], T.YY[:], 0.0, A.mult, A.max)
+        V(["SC", "HASF"], ["VH"], "tt", P["VH"], T.SC[:, 15::16], P["HASF"], A.mult)
+        ops(("tt", "PLF", "BASE", "VH", A.subtract), ("cp", "PL", "PLF"))
+        SA(["PL"] + RK, ["PCB"], T.PCB[:], T.R[:].indirect(P["PL"]), F.Identity, bias=255.0, scale=-1.0)
+        for k, w in ((0, "WU"), (16, "WV")):
+            for r in range(16):
+                mm([w, "PCB"], "b2", T.b2[:, k:k + 16], blk(w, r), T.PCB[:, r::16], r == 0, r == 15)
+        if t == 3:
+            winners()
+            ops(("tt", "A3", "A2", "L2", A.add), ("cp", "LLb", "A3"))
+            V(["LLb"] + mk, ["LM"], "cp", T.TAB[:, 4096:6400].indirect(P["LLb"]), m)
+            dma("y", "dyl", T.yl[:], T.TAB[:, 4096:6144], ["LM"], [])
+        if t < 3:
+            ops(("cp", "LSEL", "VH"))
+            src = T.NB
+            sk = ["NB"]
+            if t:
+                V(["NB", "LT%dr" % t, "LT%do" % t, "LT%df" % t], ["MT"], "tt", T.MT[:], T.LT[:, 256 * t - 256:256 * t], T.NB[:], A.max)
+                src, sk = T.MT, ["MT"]
+            SA(["LSEL", "SELM"], ["SELG"], T.SELG[:], T.SELM[:].indirect(P["LSEL"]))
+            SA(sk, ["MT1"], T.MT1[:], src[:], F.Abs, bias=-8192.0)
+            SA(["MT1"], ["MT1"], T.MT1[:], T.MT1[:], F.Abs, bias=-4096.0)
+            SA(["MT1"], ["MK"], T.MK[:], T.MT1[:], F.Relu, bias=1.0, scale=-1.0)
+            SA(["MT1"], ["MT1"], T.MT1[:], T.MT1[:], F.Abs, bias=-2048.0)
+            SA(["MT1"], ["MT2"], T.MT2[:], T.MT1[:], F.Identity, bias=2048.0, scale=-1.0)
+        ops(("ts", "NONE", "VH", 0.0, None, A.is_equal), ("ts", "N8", "VH", 0.0, 8.0, A.is_equal, A.mult), ("tt", "NN", "NONE", "L1", A.mult))
+        if t == 0:
+            V(["b7"], ["K0"], "cp", T.K0[:], T.b7[:, 200:201])
+        if t < 3:
+            V(["TUI", "K0"], ["C0T"], "ts", P["C0T"], T.TUI[:, 0:16], T.K0[:], None, A.mult)
+            ops(("tt", "NA", "NOH", "BD", A.mult), ("tt", "C0T", "C0T", "TAL", A.add), ("tt", "PLB", "NA", "PLF", A.add),
+                ("ts", "C0I", "C0T", 2047, None, A.bitwise_and), ("cp", "PL2", "PLB"), ("tt", "A1", "C0I", "L2", A.subtract),
+                ("ts", "CH", "VH", 0.0, None, A.is_gt), ("tt", "A3", "NONE", "L6", A.mult), ("tt", "A2", "A1", "NOH", A.mult), ("tt", "KA", "A2", "A3", A.add))
+            SA(["PL2"] + RK, ["VAL"], T.VAL[:], T.R[:].indirect(P["PL2"]))
+        if t == 0:
+            candidates(192, T.MREF[:], MRK, T.LSTR[:], "LSTR", T.ARF[:], "ARF")
+            constants_s(2)
+        V(["b2"], ["CUI"], "ts", T.CUI[:], T.b2[:, 0:32], -1.0, None, A.mult)
+        ops(("ts", "CUI", "CUI", 4095, None, A.bitwise_and))
+        V(["CUI"], ["CPR"], "tt", P["CPR"], T.CUI[:, 0:16], T.CUI[:, 16:32], A.mult)
+        ops(("ts", "CPR", "CPR", 5, None, A.arith_shift_right))
+        V(["CPR", "CUI"], ["CPS"], "tt", P["CPS"], P["CPR"], T.CUI[:, 0:16], A.add)
+        ops(("ts", "DI", "CPS", 3, None, A.bitwise_and), ("tt", "DD", "DI", "N8", A.add))
+        for d in range(4):
+            V(["DD"], ["E%d" % d], "ts", T.E[:, 16 * d:16 * d + 16], P["DD"], float(d), None, A.is_equal)
+        EK = ["E%d" % d for d in range(4)]
+        mm(["IDN"] + C256K, "b7", T.b7[:, 64:128], T.IDN[:], T.C256[:], True, False)
+        mm(["NTR"] + EK, "b7", T.b7[:, 64:128], T.NTR[:], T.E[:], False, False)
+        V(["SEG"] + EK, ["CS"], "scan", T.CS[:], T.SEG[:, 0:64], T.E[:], 0.0, A.mult, A.add)
+        mm(["BLK", "CS"], "b7", T.b7[:, 64:128], T.BLK[:], T.CS[:], False, True)
+        if t < 3:
+            ops(("ts", "CHH", "CPS", 4095, None, A.bitwise_and), ("tt", "KH", "CHH", "CH", A.mult), ("tt", "KEY", "KH", "KA", A.add))
+        V(["b7"] + EK, ["SL"], "tt", T.SL[:], T.b7[:, 64:128], T.E[:], A.mult)
+        V(["SL"], ["S2"], "tt", T.S2[:], T.SL[:, 0:32], T.SL[:, 32:64], A.add)
+        V(["S2"], ["S3"], "tt", P["S3"], T.S2[:, 0:16], T.S2[:, 16:32], A.add)
+        ops(("tt", "S4", "S3", "NN", A.add), ("cp", "SLOT", "S4"))
+        sm = T["SM%d" % t]
+        V(["SLOT", "PCB", "SM%dp" % t, "SM%do" % t], ["SM%d" % t], "cp", sm[:].indirect(P["SLOT"]), T.PCB[:])
+        send("fm%d" % (t + 1), lambda p: (T.M[:, nx + 48 * rank:nx + 48 * rank + 48], sm[:, 256 * p:256 * p + 48]), ["SM%d" % t])
+        SA(["SM%d" % t], ["M%do" % (t + 1)], T.M[:, nx + 48 * rank:nx + 48 * rank + 48], sm[:, 256 * rank:256 * rank + 48])
+        if t == 0:
+            constants_s(3)
+        if t < 3:
+            spread_keys()
+            stt = T["ST%d" % t]
+            V(["SLOT", "SELG", "TGF"] + ["ST%d_%d" % (t, d) for d in range(4)], ["ST%d" % t], "tt", stt[:].indirect(P["SLOT"]), T.SELG[:], T.TGF[:], A.max)
+            send("ft%d" % (t + 1), lambda p: (T.LT[:, 256 * t + 48 * rank:256 * t + 48 * rank + 48], stt[:, 256 * p:256 * p + 48]), ["ST%d" % t])
+            equal_pairs(EQ_S)
+            SA(["ST%d" % t], ["LT%do" % (t + 1)], T.LT[:, 256 * t + 48 * rank:256 * t + 48 * rank + 48], stt[:, 256 * rank:256 * rank + 48])
+            earlier_lanes()
+        if t == 0:
+            V(["MK", "AR"], ["MKAa", "MKAb"], "tt", T.MKA[:], T.MK[:], T.AR[:], A.mult)
+        elif t < 3:
+            V(["MK", "AR"], ["MKAa"], "tt", T.MKA[:, 0:192], T.MK[:, 0:192], T.AR[:, 0:192], A.mult)
+            V(["MK", "ARF"], ["MKAb"], "tt", T.MKA[:, 192:256], T.MK[:, 192:256], T.ARF[:, 64 * t - 64:64 * t], A.mult)
+        if t < 3:
+            nk = ["M%dr" % (t + 1), "M%do" % (t + 1)]
+            candidates(192, T.M[:, nx:nx + 192], nk, T.LST[:, 0:192], "LST", T.AR[:, 0:192], "AR")
+            for i in range(16):
+                SA(nk, ["MX%d" % i], T.MX[:, i:3072:16], T.M[:, nx:nx + 192])
+            count_earlier()
+            winners()
+            ops(("tt", "A3", "A2", "L6", A.add), ("cp", "LLa", "A3"))
+            V(["LLa", "VAL"], ["LM", "SN"], "cp", T.TAB[:].indirect(P["LLa"]), T.VAL[:])
+            ops(("tt", "A1", "A2", "NOH", A.mult), ("tt", "A3", "A1", "L2", A.add), ("cp", "LLb", "A3"))
+            V(["LLb", "MT2", "MKAa", "MKAb"], ["TL"], "tt", T.TL[:].indirect(P["LLb"]), T.MT2[:], T.MKA[:], A.max)
+            SA(["M%d%s" % (t + 1, x) for x in "rof"], ["MN"], T.MN[:], T.M[:, nx:nx + 256], F.Identity, bias=255.0, scale=-1.0)
+    dma("s", "dyf", T.yf[:], T.M[:, 1024:1280], ["M4r", "M4o", "M4f"], [])
+    issue()
+    for s in SEMAPHORES:
+        if cnt[s] and known["y"].get(s, 0) < cnt[s]:
+            g.sync.wait_ge(S[s], cnt[s])

@@ -1,52 +1,49 @@
+import numpy as np
 from concourse.bass import DstId, RemoteDMATransfer
 from concourse.mybir import AluOpType as A, ActivationFunctionType as F
 
 BF, FP, I32, U16 = "bfloat16", "float32", "int32", "uint16"
-POOLS = {
-    "PLFP": ["LANE", "BASE", "BD", "L1", "L2", "L6", "HASF", "NOH", "VH", "PLF", "S3", "S4", "NN", "NONE", "N8", "CH", "A1", "A2",
-             "A3", "KA", "KH", "WIN", "DD", "NA", "PLB"],
-    "PLI": ["TPR", "TAL", "KK", "KC", "C0T", "C0I", "CPR", "CHH", "DI", "KEY", "CPS"],
-    "PLU": ["GL", "LSEL", "PL", "SLOT", "PL2", "LLa", "LLb"],
-}
+BLOCKS = [(12, 16), (0, 6), (6, 12)]
+PLAN = {"L": ["vvss", "vvvs", "vvvs"], "L0": ["vvss", "vvvs", "vvvs"], "PG": ["ss", "svs", "svs"], "PP": ["ss", "sss", "sss"],
+        "S": ["vs", "vvs", "vvs"], "NEG": "svsvsvsv", "EQ": 13}
 SIZES = {
-    BF: {"TAB": 6400, "MO": 2048, "FR": 1024, "M": 1280, "BLK": 128, "IDN": 128, "Z": 128, "NTR": 128, "ONES": 128, "DK": 128, "WBU": 128,
-         "WBV": 128, "KUH": 128, "KUL": 128, "IDM": 128, "RHK": 256, "JC": 256, "KB": 2, "SEG": 256, "C255": 256, "ZER": 256, "C256": 64,
-         "WU": 2048, "WV": 2048, "VN": 2048, "MS": 2048, "SEL": 2048, "TRI": 2048, "MREF": 192, "MX": 4096, "MXR": 3072, "X": 4096,
-         "MN": 256, "ZQ": 256, "ZX": 4096, "R": 4352, "TT": 4096, "PCB": 256, "E": 64, "CS": 64, "KPB": 32, "EQ": 4096, "DUPS": 256,
-         "VAL": 256, "SM0": 1280, "SM1": 1280, "SM2": 1280, "SM3": 1280},
-    FP: {"TL": 2304, "PF": 4, "WF": 4, "WN": 4, "K0": 1, "CAP": 256, "TRC": 16, "ROW": 16, "SELM": 32, "NBC": 2, "COLF": 32, "SC": 256,
-         "YY": 256, "SL": 64, "S2": 32, "TGF": 256, "SELG": 256, "LT": 768, "NB": 256, "MT": 256, "MK": 256, "MT1": 256, "MT2": 256,
-         "MKA": 256, "KF": 16, "NKF": 16, "EQT": 1280, "ST0": 1280, "ST1": 1280, "ST2": 1280},
-    I32: {"TLI": 2048, "WKI": 3, "CI": 256, "CM": 256, "PI": 1, "PR": 1, "PG": 1, "CG": 128, "KWI": 128, "KWT": 128, "UI": 512, "PRD": 256,
-          "AR": 256, "ARF": 192, "CT": 256, "TUI": 32, "HP": 256, "HI": 256, "CUI": 32, "KP": 32},
-    U16: {"LST": 256, "LSTR": 192, "TG": 256, "HL": 256, "KR": 256},
+    BF: {"TAB": 6400, "MO": 2048, "FR": 1024, "M": 1280, "MD": 2048, "ONES": 2048, "BLK": 128, "IDN": 128, "IDM": 128, "Z": 128, "DK": 16,
+         "WBU": 128, "WBV": 128, "BD": 128, "Z4": 128, "ZK": 128, "C255": 128, "JC": 384, "WU": 2048, "WV": 2048, "VN": 2048, "MS": 2048,
+         "SEL": 2048, "TRI": 2048, "CUM": 2048, "EX": 2048, "X": 4096, "FL": 4096, "R": 4352, "LG": 256, "QT": 384, "HASR": 256, "ZB": 256,
+         "TD": 256, "TH": 512, "E": 256, "CS": 256, "SL": 256, "CAPC": 256, "PCB": 256, "VAL": 256, "KPB": 64, "EQ": 4096, "DUPS": 256,
+         "SM0": 1280, "SM1": 1280, "SM2": 1280, "SM3": 1280},
+    FP: {"TL": 2304, "PF": 8, "WF": 4, "WN": 4, "KJ": 16, "LF": 192, "LANE": 16, "BASE": 16, "L4": 16, "HASB": 16, "B2": 16, "PLF": 16,
+         "K1": 16, "KF": 16, "NKF": 16, "XK": 16, "X2": 16, "LTC": 256, "LT": 512, "MT": 256, "TA": 256, "TB": 256, "TY": 256, "TGF": 256,
+         "MSK": 256, "EQT": 640, "ST0": 1280, "ST1": 1280},
+    I32: {"TLI": 2048, "WKI": 3, "CI": 128, "CM": 128, "CG": 128, "PI": 4, "LI": 256, "CT": 1024, "SC": 256, "SCM": 16, "GI": 16, "KP": 64,
+          "UI": 512, "PRD": 256, "HP": 256, "HI": 256, "D3": 256, "HH": 512},
+    U16: {"LST": 1024, "TG": 256, "HL": 256, "KR": 256, "GL": 16, "PL": 16, "SLOT": 16, "LLA": 16, "LLB": 16},
 }
-SCRATCH = {"FL": ("sbuf", [128, 16, 256], BF)}
+SCRATCH, WIDTH, DTYPE = {}, {}, {}
 for _d in SIZES:
     for _n in SIZES[_d]:
         SCRATCH[_n] = ("sbuf", [128, SIZES[_d][_n]], _d)
-for _n, _d in (("PLFP", FP), ("PLI", I32), ("PLU", U16)):
-    SCRATCH[_n] = ("sbuf", [128, 16 * len(POOLS[_n])], _d)
-for _b in range(8):
-    SCRATCH["b%d" % _b] = ("psum", [128, 512], FP)
-_DMAS = ["wk", "fm", "fr", "lm", "tl", "mo", "sn", "rf", "yl", "yf"]
+        WIDTH[_n], DTYPE[_n] = SIZES[_d][_n], _d
+BANKS = ["b0", "b1", "b2", "d0", "d1", "m0", "m1", "m2"]
+for _b in BANKS:
+    SCRATCH[_b] = ("psum", [128, 512], FP)
+    WIDTH[_b], DTYPE[_b] = 512, FP
+_DMAS = ["wk", "fm", "fr", "lm", "tl", "mo", "sn", "yl", "yf"]
 SEMAPHORES = (["sv", "ss", "st", "sg", "loc"] + ["d" + x for x in _DMAS]
-              + ["pre%d" % t for t in range(4)] + ["fm%d" % t for t in range(1, 5)] + ["ft%d" % t for t in range(1, 4)])
-L_S0 = [(12, 14), (14, 16), (8, 10)]
-L_S = [(12, 14), (14, 16), (8, 10)]
-P_S = [(4, 6), (6, 8), (12, 14), (14, 16)]
-P_V = [(0, 4), (8, 12)]
-S_S = [(4, 6), (6, 8), (14, 16)]
-ZX_S, EQ_S = 4, 10
-EST = {"vL": 0.47, "vT": 0.68, "vR": 0.26, "sG": 0.70, "sP": 0.53}
+              + ["pre%d" % t for t in range(4)] + ["fm%d" % t for t in range(1, 5)] + ["ft%d" % t for t in range(1, 3)])
+CYC, PEC, WAKE, HOP, SLACK = 0.0009, 0.00046, 0.12, 3.0, 0.2
 
-US = {"v": {"FL": 0.45, "TT": 1.35, "R": 0.48, "ZX": 0.16, "UI": 0.3, "PRD": 0.28, "AR": 0.2, "CT": 0.2, "LST": 0.2, "LSTR": 0.2, "SC": 0.26,
-            "YY": 0.26, "TG": 0.42, "ZQ": 0.42, "SM": 0.9, "ST": 0.9, "LM": 0.9, "TL": 1.3, "MT": 0.45, "MKAa": 0.4, "KR": 0.26, "EQ": 0.12,
-            "VN": 0.9, "ARF": 0.2, "HP": 0.15, "HI": 0.15, "HL": 0.15},
-      "s": {"X": 0.72, "FL": 0.26, "R": 0.48, "MX": 0.21, "MXR": 0.21, "ZX": 0.26, "WU": 1.75, "WV": 1.75, "SN": 3.4, "TGF": 0.42, "NB": 0.26,
-            "PCB": 0.42, "SELG": 0.42, "VAL": 0.42, "MT": 0.26, "MK": 0.26, "DUPS": 0.26, "MN": 0.26, "Rm": 0.26, "EQT": 0.13}}
-LOADED = {"dlm": 6.0, "dtl": 10.0, "dmo": 13.0, "dfr": 14.0, "dsn": 18.0, "drf": 19.0}
-WINDOW, WAKE = {"v": 60, "s": 4, "t": 60, "g": 1, "y": 1}, 0.1
+
+def X(name, a=0, b=None, s=1, p=None):
+    return (name, a, WIDTH[name] if b is None else b, s, p)
+
+
+def IX(win, off):
+    return ("*", win, off)
+
+
+def cols(x):
+    return 16 * cols(x[2]) if x[0] == "*" else len(range(x[1], x[2], x[3]))
 
 
 def rank_program(g, core, T, topo):
@@ -57,611 +54,538 @@ def rank_program(g, core, T, topo):
     S = T.sem
     Q = {"v": g.vector, "s": g.scalar, "t": g.tensor, "g": g, "y": g.sync}
     SN = {"v": "sv", "s": "ss", "t": "st", "g": "sg"}
-    cnt = {k: 0 for k in SEMAPHORES}
-    known = {e: {} for e in Q}
-    snap, wr_, rd_, ps_ = {}, {}, {}, {}
-    P = {}
-    for pn in POOLS:
-        for i, n in enumerate(POOLS[pn]):
-            P[n] = T[pn][:, 16 * i:16 * i + 16]
 
-    def is_bank(k):
-        return k[0] == "b" and k[1:].isdigit()
-
-    def sync(e, toks):
-        need = {}
-        for s, v in toks:
-            if known[e].get(s, 0) < v:
-                need[s] = max(need.get(s, 0), v)
-        drop = [s for s in need if any(s2 != s and snap.get((s2, need[s2]), {}).get(s, 0) >= need[s] for s2 in need)]
-        for s, v in need.items():
-            if s not in drop:
-                Q[e].wait_ge(S[s], v)
-        for s, v in need.items():
-            known[e][s] = max(known[e].get(s, 0), v)
-            for a, b in snap.get((s, v), {}).items():
-                known[e][a] = max(known[e].get(a, 0), b)
+    def ap(x):
+        if not isinstance(x, tuple):
+            return x
+        if x[0] == "*":
+            return ap(x[1]).indirect(ap(x[2]))
+        rows = slice(None) if x[4] is None else slice(0, x[4])
+        return T[x[0]][rows, x[1]:x[2]] if x[3] == 1 else T[x[0]][rows, x[1]:x[2]:x[3]]
 
     rec = []
+    writer = {n: np.full(WIDTH[n], -1) for n in WIDTH}
+    readers = {n: [] for n in WIDTH}
+    bank = {}
 
-    def add(e, sem, inc, rd, wr, cost, late, call):
-        n, before, order = len(rec), set(), set()
-        for k in list(rd) + list(wr):
-            if is_bank(k):
-                cur = ps_.setdefault(k, [None, [], []])
+    def add(e, sem, inc, rd, wr, cost, late, call, follow=()):
+        n, before, order = len(rec), set(), set(follow)
+        rd = [y for x in rd if isinstance(x, tuple) for y in (x[1:] if x[0] == "*" else [x])] + [x[2] for x in wr if x[0] == "*"]
+        wr = [x[1] if x[0] == "*" else x for x in wr]
+        for x in rd + wr:
+            if x[0] in BANKS:
+                cur = bank.setdefault(x[0], [None, [], []])
                 if cur[0] != e:
-                    ps_[k] = cur = [e, [], cur[1]]
+                    bank[x[0]] = cur = [e, [], cur[1]]
                 before.update(cur[2])
                 if e == "t":
                     order.update(cur[1][-1:])
                 cur[1].append(n)
-            elif k in rd:
-                before.update(wr_.get(k, []))
-        for k in wr:
-            if not is_bank(k):
-                before.update(wr_.get(k, []) + rd_.get(k, []))
-        for k in rd:
-            rd_.setdefault(k, []).append(n)
-        for k in wr:
-            wr_[k], rd_[k] = [n], []
-        before.discard(n)
-        rec.append((e, sem, inc, before, order, cost, late, call))
+            else:
+                before.update(np.unique(writer[x[0]][x[1]:x[2]:x[3]]).tolist())
+        for x in wr:
+            if x[0] not in BANKS:
+                keep = []
+                for i, mask in readers[x[0]]:
+                    if mask[x[1]:x[2]:x[3]].any():
+                        before.add(i)
+                        mask[x[1]:x[2]:x[3]] = False
+                    if mask.any():
+                        keep.append((i, mask))
+                readers[x[0]] = keep
+                writer[x[0]][x[1]:x[2]:x[3]] = n
+        for x in rd:
+            if x[0] not in BANKS:
+                mask = np.zeros(WIDTH[x[0]], bool)
+                mask[x[1]:x[2]:x[3]] = True
+                readers[x[0]].append((n, mask))
+        before -= {n, -1}
+        order.discard(n)
+        rec.append([e, sem, inc, before, order, cost, late, call])
         return n
 
-    def op(e, rd, wr, name, *a, **kw):
-        f = {"cp": lambda: g.vector.tensor_copy, "tt": lambda: g.vector.tensor_tensor, "ts": lambda: g.vector.tensor_scalar,
-             "scan": lambda: g.vector.tensor_tensor_scan, "ms": lambda: g.vector.memset, "act": lambda: g.scalar.activation,
-             "mm": lambda: g.tensor.matmul, "iota": lambda: g.iota}[name]()
-        key = wr[0].rstrip("0123456789")
-        c = (0.3 if wr[0] in ("b5", "b6") else 0.045) if e == "t" else US[e].get(key, 0.11) if e in US else 0.3
-        add(e, SN[e], 1, rd, wr, c, 0.0, lambda: f(*a, **kw))
+    def us(out, ins, two=False):
+        if out[0] == "*":
+            return 0.05 + 3.8 * CYC * cols(out)
+        if ins and ins[0][0] == "*":
+            return 0.06 + 1.56 * CYC * cols(out)
+        r = 0.5 if all(DTYPE[x[0]] in (BF, U16) for x in [out] + ins) else 1.0
+        if two and not any(x[0] in BANKS for x in ins):
+            r *= 2
+        return max(70, r * cols(out)) * CYC
 
-    def dma(e, sem, out, in_, rd, wr):
-        return add(e, sem, 16, rd, wr, 0.1, LOADED.get(sem, 2.5), lambda: Q[e].dma_start(out, in_))
+    def call(e, f, out, args, cost, **kw):
+        ins = [x for x in list(args) + list(kw.values()) if isinstance(x, tuple)]
+        return add(e, SN[e], 1, ins, [out], cost, 0.0, lambda: f(ap(out), *[ap(x) for x in args], **{k: ap(kw[k]) for k in kw}))
 
-    def issue():
-        todo = {e: [i for i in range(len(rec)) if rec[i][0] == e] for e in Q}
-        now, fin = {e: 0.0 for e in Q}, {}
-        for i in range(len(rec)):
-            if rec[i][0] is None:
-                fin[i] = None
-        left, pos = sum(len(x) for x in todo.values()), {}
-        while left:
-            best = None
-            for e in Q:
-                head = pick = None
-                for i in todo[e][:WINDOW[e]]:
-                    st = now[e]
-                    for d in rec[i][3] | rec[i][4]:
-                        f = fin.get(d)
-                        if rec[d][0] is None:
-                            f = fin.get(rec[d][3])
-                            f = None if f is None else f + 2.0
-                        if f is None:
-                            st = None
-                            break
-                        if d in rec[i][3] and f > now[e] - WAKE:
-                            st = max(st, f + WAKE)
-                    if head is None:
-                        head = (st, i)
-                        if st is not None:
-                            pick = (st, i)
-                    elif st is not None and (pick is None or (st < pick[0] and (head[0] is None or st + rec[i][5] <= head[0] + 0.04))):
-                        pick = (st, i)
-                if pick is not None and (best is None or pick[0] < best[0]):
-                    best = (pick[0], e, pick[1])
-            st, e, i = best
-            _, sem, inc, before, order, cost, late, call = rec[i]
-            todo[e].remove(i)
-            left -= 1
-            now[e] = st + cost
-            fin[i] = st + cost + late
-            toks = []
-            for d in before:
-                if not (e == "t" and rec[d][0] == "t"):
-                    toks.append(pos[d] if rec[d][0] is not None else (rec[d][1], rec[d][2]))
-            sync(e, toks)
-            cnt[sem] += inc
-            pos[i] = (sem, cnt[sem])
-            ins = call()
-            if sem != "loc":
-                ins.then_inc(S[sem], inc)
-            snap[pos[i]] = dict(known[e])
+    def cp(out, a):
+        call("v", g.vector.tensor_copy, out, [a], us(out, [a]))
 
-    def V(rd, wr, name, *a):
-        op("v", rd, wr, name, *a)
+    def tt(out, a, b, op):
+        call("v", g.vector.tensor_tensor, out, [a, b, op], us(out, [a, b], True))
 
-    def ops(*rows):
-        for r in rows:
-            name, out, ins = r[0], r[1], [x for x in r[2:] if isinstance(x, str)]
-            V(ins, [out], name, *[ap(x) if isinstance(x, str) else x for x in r[1:]])
+    def ts(out, a, s1, op0, s2=None, op1=None):
+        call("v", g.vector.tensor_scalar, out, [a, s1, s2, op0] + ([] if op1 is None else [op1]), us(out, [a]))
 
-    def ap(n):
-        return P[n] if n in P else T[n][:]
+    def fill(out, v):
+        call("v", g.vector.memset, out, [v], us(out, []))
 
-    def SA(rd, wr, out, in_, fn=F.Copy, **kw):
-        op("s", rd, wr, "act", out, in_, fn, **kw)
+    def act(out, a, fn=F.Copy, **kw):
+        call("s", g.scalar.activation, out, [a, fn], us(out, [a]) if a[0] == "*" else max(70, cols(out)) * CYC, **kw)
 
-    def mm(rd, bank, out, lhsT, rhs, start, stop):
-        op("t", rd, [bank], "mm", out, lhsT, rhs, start, stop)
+    def mm(out, lhsT, rhs, start, stop):
+        call("t", g.tensor.matmul, out, [lhsT, rhs, start, stop], max(64, cols(rhs)) * PEC)
 
-    def blk(name, r):
-        return T[name][:, 128 * r:128 * (r + 1)]
+    def iota(out, pat, base, cm):
+        kw = {} if DTYPE[out[0]] == I32 else {"allow_small_or_imprecise_dtypes": True}
+        call("g", g.iota, out, [pat, base, cm], 0.15 + 2 * CYC * cols(out), **kw)
 
-    lands = {}
+    def select(out, a, pat, op, base, cm):
+        call("g", g.affine_select, out, [a, pat, op, 0.0, base, cm], 0.2 + 2 * CYC * cols(out))
 
-    def land(key, sem):
-        cnt[sem] += 12
-        lands[sem] = len(rec)
-        wr_[key] = [len(rec)]
-        rec.append((None, sem, 12, None, set(), 0.0, 0.0, None))
+    loaded = [1.8]
 
-    def send(sem, pieces, rd):
+    def load(e, sem, out, src):
+        loaded[0] += 0.4 + cols(out) * (2 if DTYPE[out[0]] == BF else 4) * 0.0004
+        add(e, sem, 16, [], [out], 0.1, loaded[0], lambda: Q[e].dma_start(ap(out), src), follow=last[e])
+        last[e] = [len(rec) - 1]
+
+    def store(e, sem, dst, a):
+        add(e, sem, 16, [a], [], 0.1, 3.0, lambda: Q[e].dma_start(dst, ap(a)))
+
+    lands, last = {}, {"send": [], "y": [], "s": []}
+
+    def land(sem, name, at):
+        lands[sem] = add(None, sem, 12, [], [X(name, at(p), at(p) + 48) for p in peers], 0.0, HOP, None)
+
+    def send(sem, dst, to, src, at):
         tr = []
         for n, p in enumerate(peers):
             rid, pid, _ = topo.addr(T.cores[p])
-            dst, src = pieces(p)
             eng = topo.engines(core, T.cores[p])
             tr.append(RemoteDMATransfer(dst_ids=[DstId(rid=rid, pnc=pid)], dma_engine_mask=sum(1 << x for x in eng[4 * n:4 * n + 4]),
-                                        remote_sem=S[sem], src=src, dst=dst))
-        n = add("g", "loc", 12, rd, [], 0.3, 1.0, lambda: g.remote_dma_fused(tr, local_sem=S.loc))
-        rec[lands[sem]] = (None, sem, 12, n, set(), 0.0, 0.0, None)
+                                        remote_sem=S[sem], src=T[src][:, at(p):at(p) + 48], dst=T[dst][:, to:to + 48]))
+        n = add("g", "loc", 12, [X(src, at(p), at(p) + 48) for p in peers], [], 0.3, 1.0, lambda: g.remote_dma_fused(tr, local_sem=S.loc), follow=last["send"])
+        last["send"] = [n]
+        rec[lands[sem]][4].add(n)
+
+    def issue():
+        n = len(rec)
+        nxt, left = [[] for _ in rec], [0] * n
+        for i in range(n):
+            for d in rec[i][3] | rec[i][4]:
+                nxt[d].append(i)
+                left[i] += 1
+        seq, deg = [i for i in range(n) if not left[i]], list(left)
+        for i in seq:
+            for k in nxt[i]:
+                deg[k] -= 1
+                if not deg[k]:
+                    seq.append(k)
+        tail = [0.0] * n
+        for i in reversed(seq):
+            tail[i] = rec[i][5] + rec[i][6] + max([0.0] + [tail[k] + (WAKE if rec[k][0] != "t" or rec[i][0] != "t" else 0.0) for k in nxt[i]])
+        ready, now, fin, can = {e: [] for e in Q}, {e: 0.0 for e in Q}, [0.0] * n, [0.0] * n
+        cnt, known, snap, pos = {k: 0 for k in SEMAPHORES}, {e: {} for e in Q}, {}, {}
+
+        def done(i):
+            for k in nxt[i]:
+                left[k] -= 1
+                soft = i not in rec[k][3] or (rec[k][0] == "t" and rec[i][0] == "t")
+                can[k] = max(can[k], fin[i] - rec[i][6] if soft else fin[i] + WAKE)
+                if not left[k]:
+                    free(k)
+
+        def free(k):
+            if rec[k][0] is None:
+                fin[k] = can[k] + rec[k][6]
+                cnt[rec[k][1]] += rec[k][2]
+                pos[k] = (rec[k][1], rec[k][2])
+                done(k)
+            else:
+                ready[rec[k][0]].append(k)
+        for k in [i for i in range(n) if not left[i]]:
+            free(k)
+        while any(ready.values()):
+            best = None
+            for e in Q:
+                if ready[e]:
+                    k = min(ready[e], key=lambda i: (max(now[e], can[i]), -tail[i]))
+                    t0 = max(now[e], can[k])
+                    k = max([i for i in ready[e] if can[i] <= t0 + min(SLACK, 0.6 * rec[k][5])], key=lambda i: tail[i])
+                    if best is None or max(now[e], can[k]) < best[0]:
+                        best = (max(now[e], can[k]), e, k)
+            st, e, i = best
+            _, sem, inc, before, _, cost, late, fn = rec[i]
+            ready[e].remove(i)
+            now[e], fin[i] = st + cost, st + cost + late
+            need = {}
+            for d in before:
+                if not (e == "t" and rec[d][0] == "t") and known[e].get(pos[d][0], 0) < pos[d][1]:
+                    need[pos[d][0]] = max(need.get(pos[d][0], 0), pos[d][1])
+            for s, v in need.items():
+                if not any(s2 != s and snap.get((s2, need[s2]), {}).get(s, 0) >= v for s2 in need):
+                    Q[e].wait_ge(S[s], v)
+            for s, v in need.items():
+                known[e][s] = max(known[e].get(s, 0), v)
+                for a, b in snap.get((s, v), {}).items():
+                    known[e][a] = max(known[e].get(a, 0), b)
+            cnt[sem] += inc
+            pos[i] = (sem, cnt[sem])
+            ins = fn()
+            if sem != "loc":
+                ins.then_inc(S[sem], inc)
+            snap[pos[i]] = dict(known[e])
+            done(i)
+        for s in SEMAPHORES:
+            if cnt[s] and known["y"].get(s, 0) < cnt[s]:
+                g.sync.wait_ge(S[s], cnt[s])
+
+    def blk(name, r):
+        return X(name, 128 * r, 128 * r + 128)
+
+    def lists(out, w, src, start=True, stop=True):
+        for r in range(16):
+            mm(out, blk(w, r), X(src[0], src[1] + r, src[2], 16), start and r == 0, stop and r == 15)
+
+    LM, SNW, TLW = X("TAB", 256, 2304), X("TAB", 2304, 6400), X("TL", 256, 2304)
 
     for t in range(4):
-        land("SM%dp" % t, "pre%d" % t)
-    for t in range(1, 5):
-        land("M%dr" % t, "fm%d" % t)
-    for t in range(1, 4):
-        land("LT%dr" % t, "ft%d" % t)
-    dma("y", "dwk", T.WKI[:], T.wk[:], [], ["WKI"])
-    dma("s", "dfm", T.M[:, 0:256], T.fm[:], [], ["M0"])
-    dma("y", "dlm", T.TAB[:, 4096:6144], T.lm[:], [], ["LM"])
-    dma("y", "dtl", T.TLI[:], T.tl[:], [], ["TLI"])
-    dma("y", "dmo", T.MO[:], T.mo[:], [], ["MO"])
-    dma("y", "dfr", T.FR[:], T.fr[:], [], ["FR"])
-    dma("y", "dsn", T.TAB[:, 0:4096], T.sn[:], [], ["SN"])
-    rf = []
-    for t in range(4):
-        rf.append(dma("y", "drf", T["SM%d" % t][:, 256 * rank:256 * rank + 48], T.fr[:, 256 * t + 48 * rank:256 * t + 48 * rank + 48], [], ["SM%do" % t]))
-        rf.append(dma("y", "drf", T.M[:, 256 * t + 448:256 * t + 512], T.fr[:, 256 * t + 192:256 * t + 256], [], ["M%df" % (t + 1)]))
-    for t in range(4):
-        wr_["SM%do" % t], wr_["M%df" % (t + 1)] = list(rf), list(rf)
+        land("pre%d" % t, "SM%d" % t, lambda p: 256 * p)
+        land("fm%d" % (t + 1), "M", lambda p: 256 * t + 256 + 48 * p)
+    for t in range(2):
+        land("ft%d" % (t + 1), "LT", lambda p: 256 * t + 48 * p)
+    load("y", "dwk", X("WKI"), T.wk[:])
+    load("s", "dfm", X("M", 0, 256), T.fm[:])
+    load("y", "dlm", LM, T.lm[:])
+    load("y", "dtl", X("TLI"), T.tl[:])
+    load("y", "dmo", X("MO"), T.mo[:])
+    load("y", "dsn", SNW, T.sn[:])
+    load("y", "dfr", X("FR"), T.fr[:])
 
-    op("g", [], ["CI"], "iota", T.CI[:], [[1, 256]], 0, 0)
-    op("g", [], ["PI"], "iota", T.PI[:], [[0, 1]], 0, 1)
-    for t in range(3):
-        for d in range(4):
-            op("g", [], ["ST%d_%d" % (t, d)], "iota", T["ST%d" % t][:, 256 * d:256 * d + 48], [[0, 48]], 0, 0, allow_small_or_imprecise_dtypes=True)
-        op("g", [], ["LT%df" % (t + 1)], "iota", T.LT[:, 256 * t + 192:256 * t + 256], [[0, 64]], 0, 0, allow_small_or_imprecise_dtypes=True)
-    for t in range(4):
-        send("pre%d" % t, lambda p: (T["SM%d" % t][:, 256 * rank:256 * rank + 48], T.FR[:, 256 * t + 48 * p:256 * t + 48 * p + 48]), ["FR"])
-    rp, gp, pf = T.PF[:, 0:1], T.PF[:, 1:2], T.PF[:, 2:3]
-    wc, kc = T.WF[:, 0:1], T.WF[:, 2:3]
-    V([], ["ONES"], "ms", T.ONES[:], 1.0)
-    ops(("ts", "CM", "CI", 15, None, A.bitwise_and), ("ts", "PR", "PI", 15, None, A.bitwise_and), ("ts", "PG", "PI", 4, None, A.arith_shift_right))
-    V(["CI"], ["CG"], "ts", T.CG[:], T.CI[:, 0:128], 4, None, A.arith_shift_right)
-    V(["PR"], ["PF0"], "cp", rp, T.PR[:])
-    V(["PG"], ["PF1"], "cp", gp, T.PG[:])
-    V(["PI"], ["PF2"], "cp", pf, T.PI[:])
-    V(["CG", "PF1"], ["BLK"], "ts", T.BLK[:], T.CG[:], gp, None, A.is_equal)
-    V(["CI", "PF2"], ["IDN"], "ts", T.IDN[:], T.CI[:, 0:128], pf, None, A.is_equal)
-    V(["WKI"], ["WF"], "cp", T.WF[:, 0:3], T.WKI[:])
-    V(["IDN", "WF"], ["DK"], "ts", T.DK[:], T.IDN[:], kc, None, A.mult)
-    mm(["ONES", "DK"], "b0", T.b0[:, 0:128], T.ONES[:], T.DK[:], True, True)
-    V(["BLK", "WF"], ["WBU"], "ts", T.WBU[:], T.BLK[:], wc, None, A.mult)
-    V(["BLK", "WF"], ["WBV"], "ts", T.WBV[:], T.BLK[:], T.WF[:, 1:2], None, A.mult)
-    V(["WKI"], ["WN"], "ts", T.WN[:, 0:3], T.WKI[:], -1.0, None, A.mult)
-    V(["b0", "WF"], ["KWI"], "ts", T.KWI[:], T.b0[:, 0:128], wc, None, A.mult)
-    ops(("ts", "KWT", "KWI", 2040, None, A.bitwise_and), ("tt", "KUH", "KWT", "BLK", A.mult),
-        ("ts", "KWT", "KWI", 7, None, A.bitwise_and), ("tt", "KUL", "KWT", "BLK", A.mult))
-
-    def candidates(n, src, key, lst, lkey, ar, akey):
-        mm(["WBU"] + key, "b0", T.b0[:, 0:n], T.WBU[:], src, True, True)
-        mm(["WBV"] + key, "b0", T.b0[:, n:2 * n], T.WBV[:], src, True, True)
-        mm(["KUH"] + key, "b1", T.b1[:, 0:n], T.KUH[:], src, True, False)
-        mm(["KUL"] + key, "b1", T.b1[:, 0:n], T.KUL[:], src, False, True)
-        V(["b0"], ["UI"], "cp", T.UI[:, 0:2 * n], T.b0[:, 0:2 * n])
-        V(["UI"], ["UI"], "ts", T.UI[:, 0:2 * n], T.UI[:, 0:2 * n], 4095, None, A.bitwise_and)
-        V(["UI"], ["PRD"], "tt", T.PRD[:, 0:n], T.UI[:, 0:n], T.UI[:, n:2 * n], A.mult)
-        V(["PRD"], [akey], "ts", ar, T.PRD[:, 0:n], 5, 2047, A.arith_shift_right, A.bitwise_and)
-        V([akey, "b1"], ["CT"], "tt", T.CT[:, 0:n], ar, T.b1[:, 0:n], A.add)
-        V(["CT"], ["CT"], "ts", T.CT[:, 0:n], T.CT[:, 0:n], 2047, None, A.bitwise_and)
-        V(["CT"], [lkey], "cp", lst, T.CT[:, 0:n])
-
-    for i in range(16):
-        SA(["M0"], ["MX%d" % i], T.MX[:, i::16], T.M[:, 0:256])
-    candidates(256, T.M[:, 0:256], ["M0"], T.LST[:], "LST", T.AR[:], "AR")
-
-    V(["CM"], ["Z"], "ts", T.Z[:], T.CM[:, 0:128], -99.0, None, A.add)
-    ops(("tt", "Z", "Z", "BLK", A.mult), ("ts", "Z", "Z", 99.0, None, A.add))
+    rp, gp, pf, ecol, ini, cap, row0 = [X("PF", k, k + 1) for k in range(7)]
+    iota(X("CI"), [[1, 128]], 0, 0)
+    iota(X("PI", 0, 1), [[0, 1]], 0, 1)
+    jc, at = {}, 0
+    for c0, c1 in BLOCKS:
+        if c1 - c0 not in jc:
+            jc[c1 - c0] = X("JC", at, at + 16 * (c1 - c0))
+            iota(jc[c1 - c0], [[-2048, 16], [0, c1 - c0]], 32768, 0)
+            at += 16 * (c1 - c0)
+    fill(X("ONES"), 1.0)
+    fill(X("C255"), 255.0)
+    ts(X("CM"), X("CI"), 15, A.bitwise_and)
+    ts(X("CG"), X("CI"), 4, A.arith_shift_right)
+    ts(X("PI", 1, 2), X("PI", 0, 1), 15, A.bitwise_and)
+    ts(X("PI", 2, 3), X("PI", 0, 1), 4, A.arith_shift_right)
+    ts(X("PI", 3, 4), X("PI", 0, 1), 7, A.bitwise_and)
+    cp(rp, X("PI", 1, 2))
+    cp(gp, X("PI", 2, 3))
+    cp(pf, X("PI", 0, 1))
+    ts(X("BLK"), X("CG"), gp, A.is_equal)
+    ts(X("IDN"), X("CI"), pf, A.is_equal)
+    ts(X("IDM"), X("CI"), pf, A.is_equal, -1.0, A.mult)
+    cp(X("WF", 0, 3), X("WKI"))
+    ts(X("WN", 0, 3), X("WKI"), -1.0, A.mult)
+    ts(X("Z"), X("CM"), 99.0, A.add)
+    tt(X("Z"), X("Z"), X("BLK"), A.mult)
     for r in range(16):
-        V(["Z"], ["MS%d" % r], "ts", blk("MS", r), T.Z[:], float(r), None, A.is_equal)
-    MSK = ["MS%d" % r for r in range(16)]
-    V(MSK, ["VN"], "ts", T.VN[:], T.MS[:], -4096.0, None, A.mult)
-    SA(MSK + ["WN"], ["WU"], T.WU[:], T.MS[:], scale=T.WN[:, 0:1])
-    SA(MSK + ["WN"], ["WV"], T.WV[:], T.MS[:], scale=T.WN[:, 1:2])
-    V(["CI", "PF2"], ["IDM"], "ts", T.IDM[:], T.CI[:, 0:128], pf, -1.0, A.is_equal, A.mult)
-    ops(("ts", "SEG", "CM", 0.0, None, A.is_gt), ("ts", "CAP", "CM", -0.0625, 1.0, A.mult, A.add), ("ts", "JC", "CAP", 2048.0, None, A.mult))
-    V(["CM", "PF0", "WF"], ["RHK"], "ts", T.RHK[:], T.CM[:], rp, kc, A.is_equal, A.mult)
-    V([], ["C255"], "ms", T.C255[:], 255.0)
-    V([], ["ZER"], "ms", T.ZER[:], 0.0)
-    V(["TLI"], ["TL"], "cp", T.TL[:, 0:2048], T.TLI[:])
-    V(["M0"], ["MN"], "ts", T.MN[:], T.M[:, 0:256], -1.0, 255.0, A.mult, A.add)
-
-    def constants_2():
-        V(["CI", "PF0"], ["ROW"], "ts", T.ROW[:], T.CI[:, 0:16], rp, None, A.is_equal)
-        V(["CI", "PF0"], ["TRC"], "ts", T.TRC[:], T.CI[:, 0:16], rp, None, A.is_gt)
-        V(["WF"], ["KB"], "cp", T.KB[:], T.WF[:, 1:3])
-        V(["CM", "PF0"], ["NTR"], "ts", T.NTR[:], T.CM[:, 0:128], rp, -1.0, A.is_le, A.mult)
-        ops(("tt", "NTR", "NTR", "BLK", A.mult))
-        V(["CI", "PF0"], ["COLF"], "ts", T.COLF[:], T.CI[:, 0:32], rp, None, A.add)
-        ops(("ts", "SELM", "COLF", 16.0, 12288.0, A.is_equal, A.mult))
-        V(["CI"], ["LANE"], "ts", P["LANE"], T.CI[:, 0:16], 16.0, None, A.mult)
-        V(["LANE", "PF0"], ["LANE"], "ts", P["LANE"], P["LANE"], rp, None, A.add)
-        ops(("ts", "BASE", "LANE", 16.0, 16.0, A.mult, A.add), ("ts", "BD", "LANE", -15.0, 4080.0, A.mult, A.add),
-            ("ts", "L1", "LANE", 1024.0, None, A.add), ("ts", "L2", "LANE", 2048.0, None, A.add), ("ts", "L6", "LANE", 6144.0, None, A.add))
-        V(["PF0"], ["NBC0"], "ts", T.NBC[:, 0:1], rp, 0.0, None, A.is_gt)
-        V(["PF0"], ["NBC1"], "ts", T.NBC[:, 1:2], rp, 0.0, 4096.0, A.is_equal, A.mult)
+        ts(blk("MS", r), X("Z"), 99.0 + r, A.is_equal)
+    for h in range(4):
+        o = (512 * h, 512 * h + 512)
+        ts(X("WU", *o), X("MS", *o), X("WN", 0, 1), A.mult)
+        act(X("WV", *o), X("MS", *o), scale=X("WN", 1, 2))
+        act(X("VN", *o), X("MS", *o), scale=-65536.0)
+    ts(X("DK"), X("CI", 0, 16), rp, A.is_equal, X("WF", 2, 3), A.mult)
+    mm(X("m1", 0, 16), X("BLK"), X("DK"), True, True)
+    cp(X("KJ"), X("m1", 0, 16))
+    act(X("WBU"), X("BLK"), scale=X("WF", 0, 1))
+    act(X("WBV"), X("BLK"), scale=X("WF", 1, 2))
+    select(X("EX"), X("ONES"), [[-1, 128], [0, 16]], A.is_equal, 0, 1)
+    select(X("SEL"), X("ONES"), [[-1, 16], [-16, 8], [0, 16]], A.is_equal, 0, 1)
+    for i in range(16):
+        select(blk("CUM", i), X("BLK"), [[0, 8], [1, 16]], A.is_ge, -i, 0)
+    select(X("TRI"), X("VN"), [[0, 16], [16, 8], [1, 16]], A.is_gt, 0, -1)
+    select(X("BD"), X("BLK"), [[1, 128]], A.is_equal, -1, -1)
+    tt(X("BD"), X("IDN"), X("BD"), A.subtract)
+    act(X("Z4"), blk("SEL", 15), scale=-4.0)
+    act(X("ZK"), blk("SEL", 15), scale=2304.0)
+    ts(X("LANE"), X("CI", 0, 16), 16.0, A.mult, rp, A.add)
+    ts(X("BASE"), X("LANE"), 16.0, A.mult, 16.0, A.add)
+    ts(X("L4"), X("LANE"), 4096.0, A.add)
+    ts(ecol, X("PI", 3, 4), -4.0, A.add)
+    ts(ini, rp, -8.0, A.add, 0.0, A.max)
+    ts(ini, ini, 256.0, A.mult)
+    ts(cap, rp, 8.0, A.is_lt, 256.0, A.mult)
+    ts(X("CAPC"), X("ONES", 0, 256), cap, A.mult, ini, A.max)
+    ts(row0, rp, 0.0, A.is_equal, 8192.0, A.mult)
+    act(X("LTC"), X("ONES", 0, 256), scale=row0)
+    for t in range(2):
+        act(X("LT", 256 * t + 192, 256 * t + 256), X("LTC", 0, 64))
         for d in range(4):
-            V([], ["C256_%d" % d], "ms", T.C256[:, 16 * d:16 * d + 16], 256.0 * d)
-        for t in range(3):
-            V(["FR"], ["MREF%d" % t], "cp", T.MREF[:, 64 * t:64 * t + 64], T.FR[:, 256 * t + 192:256 * t + 256])
-
-    def constants_s(part):
-        if part == 0:
-            SA(["BLK", "ROW"], ["SEL0"], blk("SEL", 0), T.BLK[:], scale=T.ROW[:, 0:1])
-            mm(["SEL0", "KB"], "b7", T.b7[:, 200:201], blk("SEL", 0), T.KB[:, 1:2], True, True)
-        if part == 1:
-            for r in range(1, 16):
-                SA(["BLK", "ROW"], ["SEL%d" % r], blk("SEL", r), T.BLK[:], scale=T.ROW[:, r:r + 1])
-        if part == 2:
-            for i in range(16):
-                SA(MRK, ["MXR%d" % i], T.MXR[:, i::16], T.MREF[:])
-            wr_["MXR"] = [n for i in range(16) for n in wr_["MXR%d" % i]]
-        if part == 3:
-            for r in range(16):
-                SA(["MS%d" % r, "TRC"], ["TRI%d" % r], blk("TRI", r), blk("MS", r), scale=T.TRC[:, r:r + 1])
-    C256K = ["C256_%d" % d for d in range(4)]
-    MRK = ["MREF0", "MREF1", "MREF2"]
-
-    def merge(a, b):
-        ta = tb = 0.0
-        a, b = list(a), list(b)
-        while a or b:
-            if b and (not a or tb + b[0][0] <= ta + a[0][0]):
-                tb += b[0][0]
-                b.pop(0)[1]()
-            else:
-                ta += a[0][0]
-                a.pop(0)[1]()
-
-    def pipe(chunks, gather, diff, post, after, ahead=0):
-        out, n = [], len(chunks)
-
-        def g1(k):
-            if k >= ahead:
-                gather(chunks[k])
-            diff(chunks[k], "b%d" % (5 + k % 2))
-
-        def p1(k):
-            post(chunks[k], "b%d" % (5 + k % 2))
-            after(chunks[k])
-        for k in range(n + 1):
-            if k < n:
-                out.append((EST["sG"], lambda k=k: g1(k)))
-            if k > 0:
-                out.append((EST["sP"], lambda k=k: p1(k - 1)))
-        return out
-
-    def share(sc):
-        return [(c, c + 2) for c in range(0, 16, 2) if (c, c + 2) not in sc]
-
-    def sums(bank, sel, c0, c1, done):
-        done.update(range(c0, c1))
-        k = c0 // 4 * 4
-        if not all(c in done for c in range(k, k + 4)):
-            return
-        for r in range(16):
-            mm(["FL%d" % c for c in range(k, k + 4)] + ([sel] if sel == "VN" else ["MS%d" % r]), bank, T[bank][:, 16 * k:16 * k + 64], blk(sel, r),
-               T.FL[:, k:k + 4, 16 * r:16 * r + 16], False, bool(len(done) == 16 and r == 15))
-
-    def spread_keys():
-        V(["KEY"], ["KPa"], "ts", T.KP[:, 0:16], P["KEY"], 8160, None, A.bitwise_and)
-        V(["KEY"], ["KPb"], "ts", T.KP[:, 16:32], P["KEY"], 31, None, A.bitwise_and)
-        V(["KPa", "KPb"], ["KPB"], "cp", T.KPB[:], T.KP[:])
-        V(["KEY"], ["NKF"], "ts", T.NKF[:], P["KEY"], -1.0, None, A.mult)
-        for r in range(16):
-            mm(["SEL%d" % r, "KPB"], "b3", T.b3[:, r:256:16], blk("SEL", r), T.KPB[:, 0:16], True, False)
-            mm(["SEL%d" % r, "KPB"], "b3", T.b3[:, r:256:16], blk("SEL", r), T.KPB[:, 16:32], False, True)
-        ops(("cp", "KF", "KEY"))
-
-    def equal_pairs(first_s):
-        V(["b3"], ["KR"], "cp", T.KR[:], T.b3[:, 0:256])
-        off = 0
-        for c in range(first_s, 16):
-            n = 256 - 16 * c
-            SA(["b3", "NKF"], ["EQT%d" % c], T.EQT[:, off:off + n], T.b3[:, 16 * c:256], F.Abs, bias=T.NKF[:, c:c + 1])
-            SA(["EQT%d" % c], ["EQ%d" % c], T.EQ[:, 272 * c:256 * c + 256], T.EQT[:, off:off + n], F.Relu, bias=1.0, scale=-1.0)
-            off += n
-        mm(["IDN", "ZER"], "b4", T.b4[:, 0:256], T.IDN[:], T.ZER[:], True, False)
-        for c in range(16):
-            if c < first_s:
-                V(["KR", "KF"], ["EQ%d" % c], "ts", T.EQ[:, 272 * c:256 * c + 256], T.KR[:, 16 * c:256], T.KF[:, c:c + 1], None, A.is_equal)
-            if c < 15:
-                mm(["BLK", "EQ%d" % c], "b4", T.b4[:, 16 * c + 16:256], T.BLK[:], T.EQ[:, 272 * c + 16:256 * c + 256], False, c == 14)
-
-    def earlier_lanes():
-        SA(["b4"], ["DUPS"], T.DUPS[:], T.b4[:, 0:256])
-
-    def count_earlier():
-        for r in range(16):
-            mm(["TRI%d" % r] + ["EQ%d" % c for c in range(16)], "b7", T.b7[:, 128:144], blk("TRI", r), T.EQ[:, r::272], r == 0, False)
-        for r in range(16):
-            mm(["MS%d" % r, "DUPS"], "b7", T.b7[:, 128:144], blk("MS", r), T.DUPS[:, r::16], False, r == 15)
-
-    def winners():
-        V(["KF", "L6"], ["A1"], "tt", P["A1"], T.KF[:], P["L6"], A.subtract)
-        V(["b7"], ["WIN"], "ts", P["WIN"], T.b7[:, 128:144], 0.0, None, A.is_equal)
-        ops(("tt", "A2", "A1", "WIN", A.mult))
-
-    LM, SNW = T.TAB[:, 4096:6144], T.TAB[:, 0:4096]
-    MXK, ZXK = ["MX%d" % i for i in range(16)], ["ZX%d" % i for i in range(16)]
-    RK = ["R%d" % c for c in range(16)] + ["Rm"]
-
+            act(X("ST%d" % t, 256 * d, 256 * d + 48), X("LTC", 0, 48))
+    for h in range(4):
+        ts(X("TL", 256 + 512 * h, 768 + 512 * h), X("TLI", 512 * h, 512 * h + 512), -1.0, A.mult, 4096.0, A.add)
+    for h in range(8):
+        o = X("TAB", 2304 + 512 * h, 2816 + 512 * h)
+        if PLAN["NEG"][h] == "s":
+            act(o, o, F.Identity, bias=255.0, scale=-1.0)
+        else:
+            ts(o, o, -1.0, A.mult, 255.0, A.add)
     for t in range(4):
-        m = T.M[:, 256 * t:256 * t + 256]
-        nx = 256 * (t + 1)
-        mk = ["M0"] if t == 0 else ["M%d%s" % (t, x) for x in "rof"]
-        LS = L_S if t else L_S0
+        send("pre%d" % t, "SM%d" % t, 256 * rank, "FR", lambda p: 256 * t + 48 * p)
+        act(X("SM%d" % t, 256 * rank, 256 * rank + 48), X("FR", 256 * t + 48 * rank, 256 * t + 48 * rank + 48))
+        act(X("M", 256 * t + 448, 256 * t + 512), X("FR", 256 * t + 192, 256 * t + 256))
 
-        def lsrc(c0, c1):
-            if t and c0 >= 12:
-                o = 64 * (t - 1) + 16 * (c0 - 12)
-                return (T.LSTR[:, o:o + 16 * (c1 - c0)], T.MXR[:, 16 * o:16 * o + 256 * (c1 - c0)], ["LSTR"], ["MXR"])
-            return (T.LST[:, 16 * c0:16 * c1], T.MX[:, 256 * c0:256 * c1], ["LST"], MXK)
+    def candidates(t, c0, c1):
+        n, li, lf = c1 - c0, 64 * t, 48 * t
+        src = X("M", 256 * t + 16 * c0, 256 * t + 16 * c1)
+        lists(X("m2", 0, n), "WU", src, True, False)
+        lists(X("m2", 16, 16 + n), "WV", src, False, True)
+        if n > 8:
+            c1 = c0 + n
+            ts(X("LI", li + c0, li + c1), X("m2", 0, n), -1.0, A.mult)
+            ts(X("LI", li + 16 + c0, li + 16 + c1), X("m2", 16, 16 + n), -1.0, A.mult)
+        else:
+            ts(X("LI", li + c0, li + c1), X("m2", 0, n), -1.0, A.mult)
+            ts(X("LI", li + 16 + c0, li + 16 + c1), X("m2", 16, 16 + n), -1.0, A.mult)
+        u, v, a = [X("LI", li + 16 * k + c0, li + 16 * k + c1) for k in range(3)]
+        ts(u, u, 4095, A.bitwise_and)
+        ts(v, v, 4095, A.bitwise_and)
+        tt(a, u, v, A.mult)
+        cp(X("LF", lf + c0, lf + c1), u)
+        ts(a, a, 5, A.arith_shift_right, 2047, A.bitwise_and)
+        cp(X("LF", lf + 16 + c0, lf + 16 + c1), a)
+        for b0, b1 in BLOCKS:
+            if c0 <= b0 < c1:
+                for c in range(b0, b1):
+                    ts(X("CT", 256 * t + 16 * b0 + c - b0, 256 * t + 16 * b1, b1 - b0), X("KJ"), X("LF", lf + c, lf + c + 1), A.mult,
+                       X("LF", lf + 16 + c, lf + 17 + c), A.add)
+                for k in range(4):
+                    o = 1024 * (t % 2) + 64 * b0 + 16 * (b1 - b0) * k
+                    act(X("MD", o, o + 16 * (b1 - b0)), X("M", 256 * t + 16 * b0, 256 * t + 16 * b1))
+        o = (256 * t + 16 * c0, 256 * t + 16 * c1)
+        ts(X("CT", *o), X("CT", *o), 2047, A.bitwise_and)
+        cp(X("LST", *o), X("CT", *o))
 
-        def lgather(ch):
-            o, mx, k1, k2 = lsrc(*ch)
-            SA(["LM"] + k1, ["X%d" % ch[0]], T.X[:, 256 * ch[0]:256 * ch[1]], LM.indirect(o))
+    pp = [0]
 
-        def ldiff(ch, b):
-            o, mx, k1, k2 = lsrc(*ch)
-            mm(["IDN", "X%d" % ch[0]], b, T[b][:], T.IDN[:], T.X[:, 256 * ch[0]:256 * ch[1]], True, False)
-            mm(["IDM"] + k2, b, T[b][:], T.IDM[:], mx, False, True)
+    def dbank():
+        pp[0] += 1
+        return "d%d" % (pp[0] % 2)
 
-        def lpost(ch, b):
-            for c in range(ch[0], ch[1]):
-                o = 256 * (c - ch[0])
-                SA([b], ["FL%d" % c], T.FL[:, c, :], T[b][:, o:o + 256], F.Relu)
-        mm(["BLK", "RHK"], "b3", T.b3[:, 0:256], T.BLK[:], T.RHK[:], True, False)
-        mm(["IDN", "JC"], "b3", T.b3[:, 0:256], T.IDN[:], T.JC[:], False, False)
-        lst8 = set()
-        vp = share(LS)
-        st = pipe(LS, lgather, ldiff, lpost, lambda ch: sums("b3", "VN", ch[0], ch[1], lst8))
-        for k, w in ((0, "WU"), (16, "WV")):
-            for r in range(16):
-                mm([w] + mk, "b2", T.b2[:, k:k + 16], blk(w, r), T.M[:, 256 * t + r:256 * t + 256:16], r == 0, r == 15)
-        vt = []
-        for c in [c for p in vp for c in range(*p)]:
-            def lv(c=c):
-                o, mx, k1, k2 = lsrc(c, c + 1)
-                V(["LM"] + k1 + k2, ["FL%d" % c], "tt", T.FL[:, c, :], LM.indirect(o), mx, A.is_gt)
-                sums("b3", "VN", c, c + 1, lst8)
-            vt.append((EST["vL"] + (1.0 if t and not vt else 0.0), lv))
-        merge(vt, st)
-        V(["b2"], ["TUI"], "ts", T.TUI[:], T.b2[:, 0:32], -1.0, None, A.mult)
-        ops(("ts", "TUI", "TUI", 4095, None, A.bitwise_and))
-        V(["TUI"], ["TPR"], "tt", P["TPR"], T.TUI[:, 0:16], T.TUI[:, 16:32], A.mult)
-        ops(("ts", "TAL", "TPR", 5, 2047, A.arith_shift_right, A.bitwise_and))
-        if t == 0:
-            constants_2()
-            SA(["SN"], ["SN"], T.TAB[:, 0:4096], T.TAB[:, 0:4096], F.Identity, bias=255.0, scale=-1.0)
-        V(["SEG", "b3"], ["SC"], "scan", T.SC[:], T.SEG[:], T.b3[:, 0:256], 0.0, A.mult, A.max)
-        V(["SC"], ["KK"], "cp", P["KK"], T.SC[:, 15::16])
-        ops(("ts", "KK", "KK", 127, None, A.bitwise_and))
-        V(["KK", "TUI"], ["KC"], "tt", P["KC"], P["KK"], T.TUI[:, 0:16], A.mult)
-        ops(("tt", "KC", "KC", "TAL", A.add), ("ts", "KC", "KC", 2047, None, A.bitwise_and), ("cp", "GL", "KC"))
-        V(["TL", "GL"], ["TG"], "cp", T.TG[:], T.TL[:, 0:2048].indirect(P["GL"]))
-        V(["LM", "GL", "MN"], ["ZQ"], "tt", T.ZQ[:], LM.indirect(P["GL"]), T.MN[:], A.add)
-        SA(mk, ["Rm"], T.R[:, 4096:4352], m)
-        if t == 3:
-            V(["TUI", "K0"], ["C0T"], "ts", P["C0T"], T.TUI[:, 0:16], T.K0[:], None, A.mult)
-            V(["SC"], ["NOH"], "ts", P["NOH"], T.SC[:, 15::16], 128.0, None, A.is_lt)
-            ops(("tt", "C0T", "C0T", "TAL", A.add), ("ts", "C0I", "C0T", 2047, None, A.bitwise_and), ("tt", "A1", "C0I", "L2", A.subtract),
-                ("tt", "A2", "A1", "NOH", A.mult), ("tt", "KEY", "A2", "L6", A.add))
-            spread_keys()
-
-        def pgather(ch):
-            SA(["MO", "TG"], ["X%d" % ch[0]], T.X[:, 256 * ch[0]:256 * ch[1]], T.MO[:].indirect(T.TG[:, 16 * ch[0]:16 * ch[1]]))
-        pgather(P_S[0])
-        pgather(P_S[1])
-        for i in range(16):
-            if i < ZX_S:
-                SA(["ZQ"], ["ZX%d" % i], T.ZX[:, i::16], T.ZQ[:])
+    def leaders(t, k):
+        c0, c1 = BLOCKS[k]
+        nc, n, b = c1 - c0, 16 * (c1 - c0), "b%d" % k
+        md = X("MD", 1024 * (t % 2) + 64 * c0, 1024 * (t % 2) + 64 * c1)
+        mm(X(b, 0, n), X("IDN"), jc[nc], True, False)
+        step = 2 if nc >= 8 else 4
+        for u in range(4):
+            off = X("LST", 256 * t + 16 * c0 + 4 * nc * u, 256 * t + 16 * c0 + 4 * nc * (u + 1))
+            o = (256 * c0 + 4 * n * u, 256 * c0 + 4 * n * (u + 1))
+            if PLAN["L" if t else "L0"][k][u] == "v":
+                tt(X("FL", *o), IX(LM, off), md, A.is_gt)
             else:
-                V(["ZQ"], ["ZX%d" % i], "cp", T.ZX[:, i::16], T.ZQ[:])
-        for b in ("b0", "b1"):
-            mm(["IDN", "ZER"], b, T[b][:, 0:256], T.IDN[:], T.ZER[:], True, False)
-            mm(["WBU", "C255"], b, T[b][:, 0:128], T.WBU[:], T.C255[:, 0:128], False, False)
-            mm(["WBV", "C255"], b, T[b][:, 128:256], T.WBV[:], T.C255[:, 0:128], False, False)
-        if t == 3:
-            equal_pairs(16)
-        nh, done = [0, 0], {}
+                d = X(dbank(), 0, 4 * n)
+                act(X("X", *o), IX(LM, off))
+                mm(d, X("IDN"), X("X", *o), True, False)
+                mm(d, X("IDM"), md, False, True)
+                act(X("FL", *o), d, F.Relu)
+            if u % step == step - 1:
+                u0 = u + 1 - step
+                lists(X(b, 4 * nc * u0, 4 * nc * (u + 1)), "VN", X("FL", 256 * c0 + 4 * n * u0, o[1]), False, u == 3)
+        s = 16 * c0
+        tt(X("SC", s, s + n), X(b, 0, n), X("CT", 256 * t + s, 256 * t + s + n), A.add)
+        for h in (8, 4, 2, 1):
+            tt(X("SC", s, s + h * nc) if h > 1 else X("SCM", c0, c1), X("SC", s, s + h * nc), X("SC", s + h * nc, s + 2 * h * nc), A.max)
+        ts(X("GI", c0, c1), X("SCM", c0, c1), 2047, A.bitwise_and)
+        cp(X("GL", c0, c1), X("GI", c0, c1))
 
-        def hsum(ch):
-            for c in range(*ch):
-                done[c] = True
-            k = ch[0] // 4 * 4
-            if not all(c in done for c in range(k, k + 4)):
-                return
-            c0, c1, h = k, k + 4, k // 8
-            b, l0, n = "b%d" % h, 16 * c0 - 128 * h, 64
-            nh[h] += 4
-            for o, w in ((0, "WU"), (128, "WV")):
+    def products(t, k):
+        c0, c1 = BLOCKS[k]
+        n, b, s, gl = 16 * (c1 - c0), "b%d" % k, 16 * c0, X("GL", c0, c1)
+        if t:
+            ts(X("TG", s, s + n), IX(TLW, gl), -1.0, A.mult, 4096.0, A.add)
+        else:
+            cp(X("TG", s, s + n), IX(X("TLI"), gl))
+        act(X("LG", s, s + n), IX(LM, gl))
+        mm(X(b, 0, 128, 1, n), X("M", 256 * t + s, 256 * t + s + n), X("IDN"), True, False)
+        mm(X(b, 0, 128, 1, n), X("LG", s, s + n), X("IDM"), False, True)
+        qt = X("QT", 128 * k, 128 * k + 128, 1, n)
+        act(qt, X(b, 0, 128, 1, n), F.Identity, bias=-255.0)
+        mm(X(b, 0, n), X("WBU"), X("C255", 0, n), True, False)
+        mm(X(b, n, 2 * n), X("WBV"), X("C255", 0, n), False, False)
+        run = 2 if n % 64 == 0 else n // 32
+        for u in range(n // 32):
+            l0 = s + 32 * u
+            o, src = (16 * l0, 16 * l0 + 512), IX(X("MO"), X("TG", l0, l0 + 32))
+            d = X(dbank())
+            if PLAN["PG"][k][u] == "v":
+                cp(X("X", *o), src)
+            else:
+                act(X("X", *o), src)
+            mm(d, X("IDN"), X("X", *o), True, False)
+            mm(d, qt, X("EX", 512 * u, 512 * u + 512, 1, n), False, True)
+            if PLAN["PP"][k][u] == "v":
+                ts(X("R", *o), d, -1.0, A.mult, 0.0, A.max)
+            else:
+                act(X("R", *o), d, F.Relu, scale=-1.0)
+            if u % run == run - 1:
+                a = 32 * (u + 1 - run)
+                for h, w in ((0, "WU"), (n, "WV")):
+                    for i in range(16):
+                        mm(X(b, h + a, h + 32 * u + 32), blk(w, i), X("R", 16 * (s + a) + i, o[1], 16), False, bool(h and i == 15 and 32 * u + 32 == n))
+        ui, hp = X("UI", 2 * s, 2 * s + 2 * n), X("HP", s, s + n)
+        cp(ui, X(b, 0, 2 * n))
+        ts(ui, ui, 4095, A.bitwise_and)
+        tt(X("PRD", s, s + n), X("UI", 2 * s, 2 * s + n), X("UI", 2 * s + n, 2 * s + 2 * n), A.mult)
+        ts(hp, X("PRD", s, s + n), 5, A.arith_shift_right)
+        tt(hp, hp, X(b, 0, n), A.add)
+        ts(X("HI", s, s + n), hp, 4095, A.bitwise_and)
+        cp(X("HL", s, s + n), X("HI", s, s + n))
+
+    def seen(t, k):
+        c0, c1 = BLOCKS[k]
+        n, b, s = 16 * (c1 - c0), "b%d" % k, 16 * c0
+        run = 2 if n % 64 == 0 else n // 32
+        for u in range(n // 32):
+            l0 = s + 32 * u
+            o, src = (16 * l0, 16 * l0 + 512), IX(SNW, X("HL", l0, l0 + 32))
+            if PLAN["S"][k][u] == "v":
+                tt(X("FL", *o), src, X("R", *o), A.not_equal)
+            else:
+                d = X(dbank())
+                act(X("X", *o), src)
+                mm(d, X("IDN"), X("X", *o), True, False)
+                mm(d, X("IDM"), X("R", *o), False, True)
+                act(X("FL", *o), d, F.Square)
+            if u % run == run - 1:
+                a = 32 * (u + 1 - run)
                 for i in range(16):
-                    mm(["R%d" % c for c in range(c0, c1)] + [w], b, T[b][:, o + l0:o + l0 + n], blk(w, i),
-                       T.R[:, 256 * c0 + i:256 * c1:16], False, bool(nh[h] == 8 and o and i == 15))
+                    mm(X(b, a, 32 * u + 32), blk("CUM", i), X("FL", 16 * (s + a) + i, o[1], 16), a == 0 and i == 0, i == 15 and 32 * u + 32 == n)
+        tt(X("ZB", s, s + n), X(b, 0, n), X("HASR", s, s + n), A.min)
 
-        def pdiff(ch, b):
-            mm(["IDN", "X%d" % ch[0]], b, T[b][:], T.IDN[:], T.X[:, 256 * ch[0]:256 * ch[1]], True, False)
-            mm(["IDM"] + ZXK, b, T[b][:], T.IDM[:], T.ZX[:, 256 * ch[0]:256 * ch[1]], False, True)
-
-        def ppost(ch, b):
-            SA([b], ["R%d" % c for c in range(*ch)], T.R[:, 256 * ch[0]:256 * ch[1]], T[b][:], F.Relu, scale=-1.0)
-        vt = []
-        for ch in P_V:
-            def pv1(ch=ch):
-                c0, c1 = ch
-                V(["MO", "TG"] + ZXK, ["TT%d" % c0], "tt", T.TT[:, 256 * c0:256 * c1], T.MO[:].indirect(T.TG[:, 16 * c0:16 * c1]),
-                  T.ZX[:, 256 * c0:256 * c1], A.subtract)
-
-            def pv2(ch=ch):
-                c0, c1 = ch
-                V(["TT%d" % c0], ["R%d" % c for c in range(c0, c1)], "ts", T.R[:, 256 * c0:256 * c1], T.TT[:, 256 * c0:256 * c1], -1.0, 0.0, A.mult, A.max)
-                hsum(ch)
-            n = (ch[1] - ch[0]) / 2
-            vt += [(EST["vT"] * n, pv1), (EST["vR"] * n, pv2)]
-        st = pipe(P_S, pgather, pdiff, ppost, hsum, 2)
-        st[0] = (0.2, st[0][1])
-        st[1] = (0.2, st[1][1])
-        if t == 0:
-            constants_s(0)
-        merge(vt, st)
-        if t == 3:
-            earlier_lanes()
-            count_earlier()
-        if t == 0:
-            constants_s(1)
-        if t < 3:
-            SA(["TL", "GL"], ["TGF"], T.TGF[:], T.TL[:, 0:2048].indirect(P["GL"]), F.Identity, bias=8192.0)
-            SA(["TL", "NBC0", "NBC1"], ["NB"], T.NB[:], T.TL[:, 0:256], F.Identity, bias=T.NBC[:, 1:2], scale=T.NBC[:, 0:1])
-
-        def hashes(h):
-            b = "b%d" % h
-            o = slice(128 * h, 128 * h + 128)
-            V([b], ["UI"], "cp", T.UI[:, 0:256], T[b][:, 0:256])
-            V(["UI"], ["UI"], "ts", T.UI[:, 0:256], T.UI[:, 0:256], 4095, None, A.bitwise_and)
-            V(["UI"], ["PRD"], "tt", T.PRD[:, 0:128], T.UI[:, 0:128], T.UI[:, 128:256], A.mult)
-            V(["PRD"], ["HP"], "ts", T.HP[:, o], T.PRD[:, 0:128], 5, None, A.arith_shift_right)
-            V(["HP", b], ["HP"], "tt", T.HP[:, o], T.HP[:, o], T[b][:, 0:128], A.add)
-            V(["HP"], ["HI"], "ts", T.HI[:, o], T.HP[:, o], 4095, None, A.bitwise_and)
-            V(["HI"], ["HL%d" % h], "cp", T.HL[:, o], T.HI[:, o])
-        hashes(0)
-        mm(["IDN", "ZER"], "b4", T.b4[:, 0:256], T.IDN[:], T.ZER[:], True, False)
-        sst = set()
-
-        def sgather(ch):
-            SA(["SN", "HL%d" % (ch[0] // 8)], ["X%d" % ch[0]], T.X[:, 256 * ch[0]:256 * ch[1]], SNW.indirect(T.HL[:, 16 * ch[0]:16 * ch[1]]))
-
-        def sdiff(ch, b):
-            mm(["IDN", "X%d" % ch[0]], b, T[b][:], T.IDN[:], T.X[:, 256 * ch[0]:256 * ch[1]], True, False)
-            mm(["IDM"] + ["R%d" % c for c in range(*ch)], b, T[b][:], T.IDM[:], T.R[:, 256 * ch[0]:256 * ch[1]], False, True)
-
-        def spost(ch, b):
-            for c in range(ch[0], ch[1]):
-                o = 256 * (c - ch[0])
-                SA([b], ["FL%d" % c], T.FL[:, c, :], T[b][:, o:o + 256], F.Square)
-        vt = []
-        for c in [c for p in share(S_S) for c in range(*p)]:
-            def sv(c=c):
-                V(["SN", "HL%d" % (c // 8), "R%d" % c], ["FL%d" % c], "tt", T.FL[:, c, :], SNW.indirect(T.HL[:, 16 * c:16 * c + 16]),
-                  T.R[:, 256 * c:256 * c + 256], A.not_equal)
-                sums("b4", "MS", c, c + 1, sst)
-            vt.append((EST["vL"], sv))
-        vt.insert(2, (1.3, lambda: hashes(1)))
-        merge(vt, pipe(S_S, sgather, sdiff, spost, lambda ch: sums("b4", "MS", ch[0], ch[1], sst)))
-        V(["SC"], ["HASF"], "ts", P["HASF"], T.SC[:, 15::16], 128.0, 16.0, A.is_ge, A.mult)
-        V(["SC"], ["NOH"], "ts", P["NOH"], T.SC[:, 15::16], 128.0, None, A.is_lt)
-        V(["b4", "CAP"], ["YY"], "tt", T.YY[:], T.b4[:, 0:256], T.CAP[:], A.min)
-        V(["YY", "SEG"], ["SC"], "scan", T.SC[:], T.SEG[:], T.YY[:], 0.0, A.mult, A.max)
-        V(["SC", "HASF"], ["VH"], "tt", P["VH"], T.SC[:, 15::16], P["HASF"], A.mult)
-        ops(("tt", "PLF", "BASE", "VH", A.subtract), ("cp", "PL", "PLF"))
-        SA(["PL"] + RK, ["PCB"], T.PCB[:], T.R[:].indirect(P["PL"]), F.Identity, bias=255.0, scale=-1.0)
-        for k, w in ((0, "WU"), (16, "WV")):
+    def keys(t):
+        ka = X("LI", 64 * t + 48, 64 * t + 64)
+        ts(X("HASB"), X("SCM"), 2048.0, A.is_ge, 8192.0, A.mult)
+        for c0, c1 in BLOCKS:
+            tt(X("K1", c0, c1), X("CT", 256 * t + 16 * c0, 256 * t + 15 * c0 + c1), X("HASB", c0, c1), A.subtract)
+        ts(ka, X("K1"), 256.0, A.add, 0.0, A.max)
+        both = X("LI", 64 * t + 32, 64 * t + 64)
+        ts(X("KP", 0, 32), both, 8160, A.bitwise_and)
+        ts(X("KP", 32, 64), both, 31, A.bitwise_and)
+        cp(X("KPB"), X("KP"))
+        for h in range(2):
             for r in range(16):
-                mm([w, "PCB"], "b2", T.b2[:, k:k + 16], blk(w, r), T.PCB[:, r::16], r == 0, r == 15)
+                mm(X("m0", r, 512, 16), blk("SEL", r), X("KPB", 32 * h, 32 * h + 32), h + r == 0, h + r == 16)
+        for h in range(2 if t < 3 else 0):
+            for r in range(16):
+                mm(X("m1", 256 + r, 512, 16), blk("SEL", r), X("KPB", 32 * h + 16, 32 * h + 32), h + r == 0, False)
+        act(X("HASR"), X("m0", 256, 512), F.Relu, bias=1.0, scale=-1.0)
+        tt(X("B2"), X("L4"), X("HASB"), A.subtract)
+        tt(X("B2"), X("B2"), X("BASE"), A.max)
+
+    def winners(kb):
+        first = PLAN["EQ"]
+        cp(X("KR"), X(kb, 256, 512))
+        if first < 16:
+            act(X("NKF"), X("KF"), scale=-1.0)
+        at = 0
+        for c in range(first, 16):
+            n = 256 - 16 * c
+            act(X("EQT", at, at + n), X(kb, 256 + 16 * c, 512), F.Abs, bias=X("NKF", c, c + 1))
+            act(X("EQ", 272 * c, 256 * c + 256), X("EQT", at, at + n), F.Relu, bias=1.0, scale=-1.0)
+            at += n
+        for c in range(16):
+            if c < first:
+                ts(X("EQ", 272 * c, 256 * c + 256), X("KR", 16 * c, 256), X("KF", c, c + 1), A.is_equal)
+            if c < 15:
+                mm(X("d0", 16 * c + 16, 256), X("BLK"), X("EQ", 272 * c + 16, 256 * c + 256), c == 0, c == 14)
+        act(X("DUPS", 16, 256), X("d0", 16, 256), scale=-65536.0)
+        for r in range(16):
+            mm(X("d1", 0, 16), blk("TRI", r), X("EQ", r, 4096, 272), r == 0, False)
+        lists(X("d1", 1, 16), "MS", X("DUPS", 16, 256), False, True)
+        tt(X("XK"), X("d1", 0, 16), X("KF"), A.add)
+
+    candidates(0, 0, 16)
+    for t in range(4):
+        m, nx = X("M", 256 * t, 256 * t + 256), 256 * t + 256
+        for k in range(len(BLOCKS)):
+            leaders(t, k)
+        if t < 3:
+            candidates(t + 1, 12, 16)
+        keys(t)
+        act(X("R", 4096, 4352), m)
+        products(t, 0)
         if t == 3:
-            winners()
-            ops(("tt", "A3", "A2", "L2", A.add), ("cp", "LLb", "A3"))
-            V(["LLb"] + mk, ["LM"], "cp", T.TAB[:, 4096:6400].indirect(P["LLb"]), m)
-            dma("y", "dyl", T.yl[:], T.TAB[:, 4096:6144], ["LM"], [])
+            cp(X("KF"), X("LI", 64 * t + 48, 64 * t + 64))
+        for k in range(1, len(BLOCKS)):
+            products(t, k)
+        if t == 3:
+            winners("m0")
+            tt(X("X2"), X("XK"), X("LANE"), A.max)
+            cp(X("LLA"), X("X2"))
+            cp(IX(X("TAB", 0, 2304), X("LLA")), m)
+            store("y", "dyl", T.yl[:], LM)
+        else:
+            tt(X("MT"), X("LT", 256 * t - 256, 256 * t) if t else X("LTC"), X("TL", 256, 512), A.max)
+            act(X("TA"), X("MT"), F.Abs, bias=-4096.0)
+            act(X("TB"), X("TA"), F.Identity, bias=4096.0, scale=-1.0)
+            tt(X("TY"), X("TA"), X("m0", 0, 256), A.subtract)
+        if t < 2:
+            act(X("TGF"), IX(TLW, X("GL")), F.Identity, bias=8192.0, scale=-1.0)
+        ts(X("D3"), X("HP"), 3, A.bitwise_and)
         if t < 3:
-            ops(("cp", "LSEL", "VH"))
-            src = T.NB
-            sk = ["NB"]
-            if t:
-                V(["NB", "LT%dr" % t, "LT%do" % t, "LT%df" % t], ["MT"], "tt", T.MT[:], T.LT[:, 256 * t - 256:256 * t], T.NB[:], A.max)
-                src, sk = T.MT, ["MT"]
-            SA(["LSEL", "SELM"], ["SELG"], T.SELG[:], T.SELM[:].indirect(P["LSEL"]))
-            SA(sk, ["MT1"], T.MT1[:], src[:], F.Abs, bias=-8192.0)
-            SA(["MT1"], ["MT1"], T.MT1[:], T.MT1[:], F.Abs, bias=-4096.0)
-            SA(["MT1"], ["MK"], T.MK[:], T.MT1[:], F.Relu, bias=1.0, scale=-1.0)
-            SA(["MT1"], ["MT1"], T.MT1[:], T.MT1[:], F.Abs, bias=-2048.0)
-            SA(["MT1"], ["MT2"], T.MT2[:], T.MT1[:], F.Identity, bias=2048.0, scale=-1.0)
-        ops(("ts", "NONE", "VH", 0.0, None, A.is_equal), ("ts", "N8", "VH", 0.0, 8.0, A.is_equal, A.mult), ("tt", "NN", "NONE", "L1", A.mult))
-        if t == 0:
-            V(["b7"], ["K0"], "cp", T.K0[:], T.b7[:, 200:201])
+            ts(X("HH", 0, 256), X("HP"), 4080, A.bitwise_and)
+            ts(X("HH", 256, 512), X("HP"), 15, A.bitwise_and)
+        for k in range(len(BLOCKS)):
+            seen(t, k)
+        mask = X("m0", 0, 256)
+        mm(mask, X("BD"), X("ZB"), True, True)
+        mm(X("b0", 0, 256), X("Z4"), X("ZB"), True, False)
+        lists(X("m2", 0, 16), "MS", X("ZB"))
+        tt(X("TD"), mask, X("D3"), A.mult)
+        mm(X("b0", 0, 256), X("BLK"), X("TD"), False, True)
+        tt(X("PLF"), X("B2"), X("m2", 0, 16), A.subtract)
+        cp(X("PL"), X("PLF"))
+        act(X("PCB"), IX(X("R"), X("PL")), F.Identity, bias=255.0, scale=-1.0)
+        ts(X("E"), X("b0", 0, 256), ecol, A.is_equal)
+        call("v", g.vector.tensor_tensor_scan, X("CS"), [X("E"), X("CAPC"), ini, A.add, A.min], us(X("CS"), [X("E")]))
+        tt(X("SL"), X("CS"), X("E"), A.mult)
+        lists(X("b1", 0, 16), "MS", X("SL"))
+        ts(X("SLOT"), X("b1", 0, 16), -1.0, A.add)
+        sm = "SM%d" % t
+        cp(IX(X(sm), X("SLOT")), X("PCB"))
+        send("fm%d" % (t + 1), "M", nx + 48 * rank, sm, lambda p: 256 * p)
+        act(X("M", nx + 48 * rank, nx + 48 * rank + 48), X(sm, 256 * rank, 256 * rank + 48))
+        if t < 2:
+            act(X("MSK"), mask, scale=8192.0)
         if t < 3:
-            V(["TUI", "K0"], ["C0T"], "ts", P["C0T"], T.TUI[:, 0:16], T.K0[:], None, A.mult)
-            ops(("tt", "NA", "NOH", "BD", A.mult), ("tt", "C0T", "C0T", "TAL", A.add), ("tt", "PLB", "NA", "PLF", A.add),
-                ("ts", "C0I", "C0T", 2047, None, A.bitwise_and), ("cp", "PL2", "PLB"), ("tt", "A1", "C0I", "L2", A.subtract),
-                ("ts", "CH", "VH", 0.0, None, A.is_gt), ("tt", "A3", "NONE", "L6", A.mult), ("tt", "A2", "A1", "NOH", A.mult), ("tt", "KA", "A2", "A3", A.add))
-            SA(["PL2"] + RK, ["VAL"], T.VAL[:], T.R[:].indirect(P["PL2"]))
-        if t == 0:
-            candidates(192, T.MREF[:], MRK, T.LSTR[:], "LSTR", T.ARF[:], "ARF")
-            constants_s(2)
-        V(["b2"], ["CUI"], "ts", T.CUI[:], T.b2[:, 0:32], -1.0, None, A.mult)
-        ops(("ts", "CUI", "CUI", 4095, None, A.bitwise_and))
-        V(["CUI"], ["CPR"], "tt", P["CPR"], T.CUI[:, 0:16], T.CUI[:, 16:32], A.mult)
-        ops(("ts", "CPR", "CPR", 5, None, A.arith_shift_right))
-        V(["CPR", "CUI"], ["CPS"], "tt", P["CPS"], P["CPR"], T.CUI[:, 0:16], A.add)
-        ops(("ts", "DI", "CPS", 3, None, A.bitwise_and), ("tt", "DD", "DI", "N8", A.add))
-        for d in range(4):
-            V(["DD"], ["E%d" % d], "ts", T.E[:, 16 * d:16 * d + 16], P["DD"], float(d), None, A.is_equal)
-        EK = ["E%d" % d for d in range(4)]
-        mm(["IDN"] + C256K, "b7", T.b7[:, 64:128], T.IDN[:], T.C256[:], True, False)
-        mm(["NTR"] + EK, "b7", T.b7[:, 64:128], T.NTR[:], T.E[:], False, False)
-        V(["SEG"] + EK, ["CS"], "scan", T.CS[:], T.SEG[:, 0:64], T.E[:], 0.0, A.mult, A.add)
-        mm(["BLK", "CS"], "b7", T.b7[:, 64:128], T.BLK[:], T.CS[:], False, True)
+            tt(X("TH", 0, 256), mask, X("HH", 0, 256), A.mult)
+            tt(X("TH", 256, 512), mask, X("HH", 256, 512), A.mult)
+            mm(X("m1", 256, 512), X("ZK"), X("ZB"), False, False)
+            mm(X("m1", 256, 512), X("BLK"), X("TH", 0, 256), False, False)
+            mm(X("m1", 256, 512), X("BLK"), X("TH", 256, 512), False, True)
+            lists(X("b2", 0, 32), "MS", X("TH"))
+            ts(X("K1"), X("m2", 0, 16), 0.0, A.is_gt, 2304.0, A.mult)
+            tt(X("K1"), X("K1"), X("LI", 64 * t + 48, 64 * t + 64), A.add)
+            tt(X("K1"), X("K1"), X("b2", 0, 16), A.add)
+            tt(X("KF"), X("K1"), X("b2", 16, 32), A.add)
+            act(X("VAL"), IX(X("R"), X("PL")))
+            winners("m1")
+            tt(X("X2"), X("XK"), X("LANE"), A.max)
+            cp(X("LLA"), X("X2"))
+            cp(IX(X("TAB"), X("LLA")), X("VAL"))
+            tt(X("X2"), X("XK"), X("HASB"), A.subtract)
+            tt(X("X2"), X("X2"), X("LANE"), A.max)
+            cp(X("LLB"), X("X2"))
+            tt(IX(X("TL"), X("LLB")), X("TB"), X("TY"), A.max)
+        if t < 2:
+            st = "ST%d" % t
+            tt(IX(X(st), X("SLOT")), X("MSK"), X("TGF"), A.max)
+            send("ft%d" % (t + 1), "LT", 256 * t + 48 * rank, st, lambda p: 256 * p)
+            act(X("LT", 256 * t + 48 * rank, 256 * t + 48 * rank + 48), X(st, 256 * rank, 256 * rank + 48))
         if t < 3:
-            ops(("ts", "CHH", "CPS", 4095, None, A.bitwise_and), ("tt", "KH", "CHH", "CH", A.mult), ("tt", "KEY", "KH", "KA", A.add))
-        V(["b7"] + EK, ["SL"], "tt", T.SL[:], T.b7[:, 64:128], T.E[:], A.mult)
-        V(["SL"], ["S2"], "tt", T.S2[:], T.SL[:, 0:32], T.SL[:, 32:64], A.add)
-        V(["S2"], ["S3"], "tt", P["S3"], T.S2[:, 0:16], T.S2[:, 16:32], A.add)
-        ops(("tt", "S4", "S3", "NN", A.add), ("cp", "SLOT", "S4"))
-        sm = T["SM%d" % t]
-        V(["SLOT", "PCB", "SM%dp" % t, "SM%do" % t], ["SM%d" % t], "cp", sm[:].indirect(P["SLOT"]), T.PCB[:])
-        send("fm%d" % (t + 1), lambda p: (T.M[:, nx + 48 * rank:nx + 48 * rank + 48], sm[:, 256 * p:256 * p + 48]), ["SM%d" % t])
-        SA(["SM%d" % t], ["M%do" % (t + 1)], T.M[:, nx + 48 * rank:nx + 48 * rank + 48], sm[:, 256 * rank:256 * rank + 48])
-        if t == 0:
-            constants_s(3)
-        if t < 3:
-            spread_keys()
-            stt = T["ST%d" % t]
-            V(["SLOT", "SELG", "TGF"] + ["ST%d_%d" % (t, d) for d in range(4)], ["ST%d" % t], "tt", stt[:].indirect(P["SLOT"]), T.SELG[:], T.TGF[:], A.max)
-            send("ft%d" % (t + 1), lambda p: (T.LT[:, 256 * t + 48 * rank:256 * t + 48 * rank + 48], stt[:, 256 * p:256 * p + 48]), ["ST%d" % t])
-            equal_pairs(EQ_S)
-            SA(["ST%d" % t], ["LT%do" % (t + 1)], T.LT[:, 256 * t + 48 * rank:256 * t + 48 * rank + 48], stt[:, 256 * rank:256 * rank + 48])
-            earlier_lanes()
-        if t == 0:
-            V(["MK", "AR"], ["MKAa", "MKAb"], "tt", T.MKA[:], T.MK[:], T.AR[:], A.mult)
-        elif t < 3:
-            V(["MK", "AR"], ["MKAa"], "tt", T.MKA[:, 0:192], T.MK[:, 0:192], T.AR[:, 0:192], A.mult)
-            V(["MK", "ARF"], ["MKAb"], "tt", T.MKA[:, 192:256], T.MK[:, 192:256], T.ARF[:, 64 * t - 64:64 * t], A.mult)
-        if t < 3:
-            nk = ["M%dr" % (t + 1), "M%do" % (t + 1)]
-            candidates(192, T.M[:, nx:nx + 192], nk, T.LST[:, 0:192], "LST", T.AR[:, 0:192], "AR")
-            for i in range(16):
-                SA(nk, ["MX%d" % i], T.MX[:, i:3072:16], T.M[:, nx:nx + 192])
-            count_earlier()
-            winners()
-            ops(("tt", "A3", "A2", "L6", A.add), ("cp", "LLa", "A3"))
-            V(["LLa", "VAL"], ["LM", "SN"], "cp", T.TAB[:].indirect(P["LLa"]), T.VAL[:])
-            ops(("tt", "A1", "A2", "NOH", A.mult), ("tt", "A3", "A1", "L2", A.add), ("cp", "LLb", "A3"))
-            V(["LLb", "MT2", "MKAa", "MKAb"], ["TL"], "tt", T.TL[:].indirect(P["LLb"]), T.MT2[:], T.MKA[:], A.max)
-            SA(["M%d%s" % (t + 1, x) for x in "rof"], ["MN"], T.MN[:], T.M[:, nx:nx + 256], F.Identity, bias=255.0, scale=-1.0)
-    dma("s", "dyf", T.yf[:], T.M[:, 1024:1280], ["M4r", "M4o", "M4f"], [])
+            candidates(t + 1, 0, 12)
+    store("s", "dyf", T.yf[:], X("M", 1024, 1280))
     issue()
-    for s in SEMAPHORES:
-        if cnt[s] and known["y"].get(s, 0) < cnt[s]:
-            g.sync.wait_ge(S[s], cnt[s])

@@ -3,20 +3,21 @@ from concourse.bass import DstId, RemoteDMATransfer
 from concourse.mybir import AluOpType as A, ActivationFunctionType as F
 
 BF, FP, I32, U16 = "bfloat16", "float32", "int32", "uint16"
-BLOCKS = [(12, 16), (0, 6), (6, 12)]
-PLAN = {"L": ["vvss", "vvvs", "vvvs"], "L0": ["vvss", "vvvs", "vvvs"], "PG": ["ss", "svs", "svs"], "PP": ["ss", "sss", "sss"],
-        "S": ["vs", "vvs", "vvs"], "NEG": "svsvsvsv", "EQ": 13}
+BLOCKS = [(0, 8), (8, 16)]
+PLAN = {"L": ["svsv", "sv", "vv", "ss"], "L0": ["vv", "vs", "sv", "sv"], "PG": ["svsv", "svss"], "PP": ["vsss", "ssss"],
+        "S": ["ssvs", "vvvs"], "NEG": "vvvvvvvv", "EQ": 10, "Q": [3, 0, 1, 2],
+        "ORDER": "L3 L0 L1 L2 P0 P1 C K S0 S1 W", "D": ["d0", "d1", "b2"]}
 SIZES = {
-    BF: {"TAB": 6400, "MO": 2048, "FR": 1024, "M": 1280, "MD": 2048, "ONES": 2048, "BLK": 128, "IDN": 128, "IDM": 128, "Z": 128, "DK": 16,
-         "WBU": 128, "WBV": 128, "BD": 128, "Z4": 128, "ZK": 128, "C255": 128, "JC": 384, "WU": 2048, "WV": 2048, "VN": 2048, "MS": 2048,
-         "SEL": 2048, "TRI": 2048, "CUM": 2048, "EX": 2048, "X": 4096, "FL": 4096, "R": 4352, "LG": 256, "QT": 384, "HASR": 256, "ZB": 256,
-         "TD": 256, "TH": 512, "E": 256, "CS": 256, "SL": 256, "CAPC": 256, "PCB": 256, "VAL": 256, "KPB": 64, "EQ": 4096, "DUPS": 256,
+    BF: {"TAB": 6400, "MO": 2048, "FR": 1024, "M": 1280, "MD": 4096, "ONES": 2048, "BLK": 128, "IDN": 128, "IDM": 128, "Z": 128, "DK": 16,
+         "WBU": 128, "WBV": 128, "BD": 128, "Z4": 128, "ZK": 128, "NBL": 128, "C255": 128, "C20": 32, "JC": 128, "WU": 2048, "WV": 2048, "VN": 2048, "MS": 2048,
+         "SEL": 2048, "TRI": 2048, "CUM": 2048, "EX": 2048, "X": 4096, "FL": 4096, "R": 4352, "LG": 256, "QT": 256, "NG": 256, "ZB": 256,
+         "TD": 256, "DIAG": 256, "SEG": 256, "E": 256, "CS": 256, "SL": 256, "CAPC": 256, "PCB": 256, "VAL": 256, "KPB": 64, "EQ": 4096, "DUPS": 256,
          "SM0": 1280, "SM1": 1280, "SM2": 1280, "SM3": 1280},
     FP: {"TL": 2304, "PF": 8, "WF": 4, "WN": 4, "KJ": 16, "LF": 192, "LANE": 16, "BASE": 16, "L4": 16, "HASB": 16, "B2": 16, "PLF": 16,
-         "K1": 16, "KF": 16, "NKF": 16, "XK": 16, "X2": 16, "LTC": 256, "LT": 512, "MT": 256, "TA": 256, "TB": 256, "TY": 256, "TGF": 256,
-         "MSK": 256, "EQT": 640, "ST0": 1280, "ST1": 1280},
+         "K1": 16, "KF": 16, "NKF": 16, "XK": 16, "X2": 16, "LT": 384, "MT": 256, "TA": 256, "TB": 256, "TY": 256, "TGF": 256,
+         "MSK": 256, "EQT": 1024, "TH": 256, "KD": 256, "KS": 256, "BLF": 128, "ST0": 1280, "ST1": 1280},
     I32: {"TLI": 2048, "WKI": 3, "CI": 128, "CM": 128, "CG": 128, "PI": 4, "LI": 256, "CT": 1024, "SC": 256, "SCM": 16, "GI": 16, "KP": 64,
-          "UI": 512, "PRD": 256, "HP": 256, "HI": 256, "D3": 256, "HH": 512},
+          "UI": 512, "PRD": 256, "HP": 256, "HI": 256, "D3": 256},
     U16: {"LST": 1024, "TG": 256, "HL": 256, "KR": 256, "GL": 16, "PL": 16, "SLOT": 16, "LLA": 16, "LLB": 16},
 }
 SCRATCH, WIDTH, DTYPE = {}, {}, {}
@@ -31,7 +32,7 @@ for _b in BANKS:
 _DMAS = ["wk", "fm", "fr", "lm", "tl", "mo", "sn", "yl", "yf"]
 SEMAPHORES = (["sv", "ss", "st", "sg", "loc"] + ["d" + x for x in _DMAS]
               + ["pre%d" % t for t in range(4)] + ["fm%d" % t for t in range(1, 5)] + ["ft%d" % t for t in range(1, 3)])
-CYC, PEC, WAKE, HOP, SLACK = 0.0009, 0.00046, 0.12, 3.0, 0.2
+CYC, PEC, WAKE, HOP, SLACK, PASSES = 0.0009, 0.00046, 0.12, 3.0, 0.2, 3
 
 
 def X(name, a=0, b=None, s=1, p=None):
@@ -134,7 +135,7 @@ def rank_program(g, core, T, topo):
         call("s", g.scalar.activation, out, [a, fn], us(out, [a]) if a[0] == "*" else max(70, cols(out)) * CYC, **kw)
 
     def mm(out, lhsT, rhs, start, stop):
-        call("t", g.tensor.matmul, out, [lhsT, rhs, start, stop], max(64, cols(rhs)) * PEC)
+        call("t", g.tensor.matmul, out, [lhsT, rhs, start, stop], max(64, cols(rhs)) * PEC * (4 if DTYPE[rhs[0]] == FP else 1))
 
     def iota(out, pat, base, cm):
         kw = {} if DTYPE[out[0]] == I32 else {"allow_small_or_imprecise_dtypes": True}
@@ -171,54 +172,59 @@ def rank_program(g, core, T, topo):
 
     def issue():
         n = len(rec)
-        nxt, left = [[] for _ in rec], [0] * n
-        for i in range(n):
-            for d in rec[i][3] | rec[i][4]:
-                nxt[d].append(i)
-                left[i] += 1
-        seq, deg = [i for i in range(n) if not left[i]], list(left)
-        for i in seq:
-            for k in nxt[i]:
-                deg[k] -= 1
-                if not deg[k]:
-                    seq.append(k)
-        tail = [0.0] * n
-        for i in reversed(seq):
-            tail[i] = rec[i][5] + rec[i][6] + max([0.0] + [tail[k] + (WAKE if rec[k][0] != "t" or rec[i][0] != "t" else 0.0) for k in nxt[i]])
-        ready, now, fin, can = {e: [] for e in Q}, {e: 0.0 for e in Q}, [0.0] * n, [0.0] * n
-        cnt, known, snap, pos = {k: 0 for k in SEMAPHORES}, {e: {} for e in Q}, {}, {}
-
-        def done(i):
-            for k in nxt[i]:
-                left[k] -= 1
+        ahead, back = [[] for _ in rec], [[] for _ in rec]
+        for k in range(n):
+            for i in rec[k][3] | rec[k][4]:
                 soft = i not in rec[k][3] or (rec[k][0] == "t" and rec[i][0] == "t")
-                can[k] = max(can[k], fin[i] - rec[i][6] if soft else fin[i] + WAKE)
-                if not left[k]:
-                    free(k)
+                gap = 0.0 if soft else rec[i][6] + WAKE
+                ahead[i].append((k, gap))
+                back[k].append((i, gap))
 
-        def free(k):
-            if rec[k][0] is None:
-                fin[k] = can[k] + rec[k][6]
-                cnt[rec[k][1]] += rec[k][2]
-                pos[k] = (rec[k][1], rec[k][2])
-                done(k)
-            else:
-                ready[rec[k][0]].append(k)
-        for k in [i for i in range(n) if not left[i]]:
-            free(k)
-        while any(ready.values()):
-            best = None
-            for e in Q:
-                if ready[e]:
-                    k = min(ready[e], key=lambda i: (max(now[e], can[i]), -tail[i]))
-                    t0 = max(now[e], can[k])
-                    k = max([i for i in ready[e] if can[i] <= t0 + min(SLACK, 0.6 * rec[k][5])], key=lambda i: tail[i])
-                    if best is None or max(now[e], can[k]) < best[0]:
-                        best = (max(now[e], can[k]), e, k)
-            st, e, i = best
-            _, sem, inc, before, _, cost, late, fn = rec[i]
-            ready[e].remove(i)
-            now[e], fin[i] = st + cost, st + cost + late
+        def plan(nxt, prv, weight):
+            left, can, end, order = [len(x) for x in prv], [0.0] * n, [0.0] * n, []
+            ready, now = {e: [] for e in Q}, {e: 0.0 for e in Q}
+
+            def done(i):
+                for k, gap in nxt[i]:
+                    left[k] -= 1
+                    can[k] = max(can[k], end[i] + gap)
+                    if not left[k]:
+                        free(k)
+
+            def free(k):
+                if rec[k][0] is None:
+                    end[k] = can[k]
+                    done(k)
+                else:
+                    ready[rec[k][0]].append(k)
+            for k in [i for i in range(n) if not left[i]]:
+                free(k)
+            while any(ready.values()):
+                best = None
+                for e in Q:
+                    if ready[e]:
+                        k = min(ready[e], key=lambda i: (max(now[e], can[i]), -weight[i]))
+                        t0 = max(now[e], can[k]) + min(SLACK, 0.6 * rec[k][5])
+                        k = max([i for i in ready[e] if can[i] <= t0], key=lambda i: weight[i])
+                        if best is None or max(now[e], can[k]) < best[0]:
+                            best = (max(now[e], can[k]), e, k)
+                st, e, i = best
+                ready[e].remove(i)
+                now[e] = end[i] = st + rec[i][5]
+                order.append(i)
+                done(i)
+            return order, end
+        order, end = plan(ahead, back, [-i for i in range(n)])
+        best = (max(end), order)
+        for _ in range(PASSES):
+            order, end = plan(ahead, back, plan(back, ahead, end)[1])
+            best = min(best, (max(end), order))
+        cnt, known, snap, pos = {k: 0 for k in SEMAPHORES}, {e: {} for e in Q}, {}, {}
+        for i in lands.values():
+            cnt[rec[i][1]] += rec[i][2]
+            pos[i] = (rec[i][1], rec[i][2])
+        for i in best[1]:
+            e, sem, inc, before, _, cost, late, fn = rec[i]
             need = {}
             for d in before:
                 if not (e == "t" and rec[d][0] == "t") and known[e].get(pos[d][0], 0) < pos[d][1]:
@@ -236,7 +242,6 @@ def rank_program(g, core, T, topo):
             if sem != "loc":
                 ins.then_inc(S[sem], inc)
             snap[pos[i]] = dict(known[e])
-            done(i)
         for s in SEMAPHORES:
             if cnt[s] and known["y"].get(s, 0) < cnt[s]:
                 g.sync.wait_ge(S[s], cnt[s])
@@ -254,7 +259,7 @@ def rank_program(g, core, T, topo):
         land("pre%d" % t, "SM%d" % t, lambda p: 256 * p)
         land("fm%d" % (t + 1), "M", lambda p: 256 * t + 256 + 48 * p)
     for t in range(2):
-        land("ft%d" % (t + 1), "LT", lambda p: 256 * t + 48 * p)
+        land("ft%d" % (t + 1), "LT", lambda p: 192 * t + 48 * p)
     load("y", "dwk", X("WKI"), T.wk[:])
     load("s", "dfm", X("M", 0, 256), T.fm[:])
     load("y", "dlm", LM, T.lm[:])
@@ -263,17 +268,13 @@ def rank_program(g, core, T, topo):
     load("y", "dsn", SNW, T.sn[:])
     load("y", "dfr", X("FR"), T.fr[:])
 
-    rp, gp, pf, ecol, ini, cap, row0 = [X("PF", k, k + 1) for k in range(7)]
+    rp, gp, pf, ecol, ini, cap, row0, not0 = [X("PF", k, k + 1) for k in range(8)]
     iota(X("CI"), [[1, 128]], 0, 0)
     iota(X("PI", 0, 1), [[0, 1]], 0, 1)
-    jc, at = {}, 0
-    for c0, c1 in BLOCKS:
-        if c1 - c0 not in jc:
-            jc[c1 - c0] = X("JC", at, at + 16 * (c1 - c0))
-            iota(jc[c1 - c0], [[-2048, 16], [0, c1 - c0]], 32768, 0)
-            at += 16 * (c1 - c0)
+    iota(X("JC"), [[-2048, 16], [0, 8]], 32768, 0)
     fill(X("ONES"), 1.0)
     fill(X("C255"), 255.0)
+    fill(X("C20"), -16 * 65536.0)
     ts(X("CM"), X("CI"), 15, A.bitwise_and)
     ts(X("CG"), X("CI"), 4, A.arith_shift_right)
     ts(X("PI", 1, 2), X("PI", 0, 1), 15, A.bitwise_and)
@@ -310,6 +311,10 @@ def rank_program(g, core, T, topo):
     tt(X("BD"), X("IDN"), X("BD"), A.subtract)
     act(X("Z4"), blk("SEL", 15), scale=-4.0)
     act(X("ZK"), blk("SEL", 15), scale=2304.0)
+    act(X("BLF"), X("BLK"))
+    for h in range(2):
+        ts(X("DIAG", 128 * h, 128 * h + 128), X("CM"), rp, A.is_equal)
+        ts(X("SEG", 128 * h, 128 * h + 128), X("CM"), 0.0, A.is_gt)
     ts(X("LANE"), X("CI", 0, 16), 16.0, A.mult, rp, A.add)
     ts(X("BASE"), X("LANE"), 16.0, A.mult, 16.0, A.add)
     ts(X("L4"), X("LANE"), 4096.0, A.add)
@@ -319,11 +324,11 @@ def rank_program(g, core, T, topo):
     ts(cap, rp, 8.0, A.is_lt, 256.0, A.mult)
     ts(X("CAPC"), X("ONES", 0, 256), cap, A.mult, ini, A.max)
     ts(row0, rp, 0.0, A.is_equal, 8192.0, A.mult)
-    act(X("LTC"), X("ONES", 0, 256), scale=row0)
+    ts(not0, rp, 0.0, A.is_gt, -1.0, A.mult)
+    act(X("NBL"), X("BLK"), scale=-2.0 ** 30)
     for t in range(2):
-        act(X("LT", 256 * t + 192, 256 * t + 256), X("LTC", 0, 64))
         for d in range(4):
-            act(X("ST%d" % t, 256 * d, 256 * d + 48), X("LTC", 0, 48))
+            act(X("ST%d" % t, 256 * d, 256 * d + 48), X("ONES", 0, 48), scale=row0)
     for h in range(4):
         ts(X("TL", 256 + 512 * h, 768 + 512 * h), X("TLI", 512 * h, 512 * h + 512), -1.0, A.mult, 4096.0, A.add)
     for h in range(8):
@@ -340,66 +345,62 @@ def rank_program(g, core, T, topo):
     def candidates(t, c0, c1):
         n, li, lf = c1 - c0, 64 * t, 48 * t
         src = X("M", 256 * t + 16 * c0, 256 * t + 16 * c1)
-        lists(X("m2", 0, n), "WU", src, True, False)
-        lists(X("m2", 16, 16 + n), "WV", src, False, True)
-        if n > 8:
-            c1 = c0 + n
-            ts(X("LI", li + c0, li + c1), X("m2", 0, n), -1.0, A.mult)
-            ts(X("LI", li + 16 + c0, li + 16 + c1), X("m2", 16, 16 + n), -1.0, A.mult)
-        else:
-            ts(X("LI", li + c0, li + c1), X("m2", 0, n), -1.0, A.mult)
-            ts(X("LI", li + 16 + c0, li + 16 + c1), X("m2", 16, 16 + n), -1.0, A.mult)
-        u, v, a = [X("LI", li + 16 * k + c0, li + 16 * k + c1) for k in range(3)]
-        ts(u, u, 4095, A.bitwise_and)
-        ts(v, v, 4095, A.bitwise_and)
+        lists(X("m2", 256, 256 + n), "WU", src, True, False)
+        lists(X("m2", 256 + n, 256 + 2 * n), "WV", src, False, True)
+        uv, u, v = X("LI", li + 2 * c0, li + 2 * c1), X("LI", li + 2 * c0, li + c0 + c1), X("LI", li + c0 + c1, li + 2 * c1)
+        a = X("LI", li + 32 + c0, li + 32 + c1)
+        ts(uv, X("m2", 256, 256 + 2 * n), -1.0, A.mult)
+        ts(uv, uv, 4095, A.bitwise_and)
         tt(a, u, v, A.mult)
         cp(X("LF", lf + c0, lf + c1), u)
         ts(a, a, 5, A.arith_shift_right, 2047, A.bitwise_and)
         cp(X("LF", lf + 16 + c0, lf + 16 + c1), a)
-        for b0, b1 in BLOCKS:
-            if c0 <= b0 < c1:
-                for c in range(b0, b1):
-                    ts(X("CT", 256 * t + 16 * b0 + c - b0, 256 * t + 16 * b1, b1 - b0), X("KJ"), X("LF", lf + c, lf + c + 1), A.mult,
-                       X("LF", lf + 16 + c, lf + 17 + c), A.add)
-                for k in range(4):
-                    o = 1024 * (t % 2) + 64 * b0 + 16 * (b1 - b0) * k
-                    act(X("MD", o, o + 16 * (b1 - b0)), X("M", 256 * t + 16 * b0, 256 * t + 16 * b1))
-        o = (256 * t + 16 * c0, 256 * t + 16 * c1)
-        ts(X("CT", *o), X("CT", *o), 2047, A.bitwise_and)
-        cp(X("LST", *o), X("CT", *o))
+        for q in [q for q in PLAN["Q"] if c0 <= 4 * q < c1]:
+            o = 256 * t + 128 * (q // 2)
+            for c in range(4 * q, 4 * q + 4):
+                ts(X("CT", o + 2 * (c % 4) + q % 2, o + 128, 8), X("KJ"), X("LF", lf + c, lf + c + 1), A.mult, X("LF", lf + 16 + c, lf + 17 + c), A.add)
+            ct = X("CT", o + q % 2, o + 128, 2)
+            ts(ct, ct, 2047, A.bitwise_and)
+            cp(X("LST", 256 * t + 64 * q, 256 * t + 64 * q + 64), ct)
+            o = 2048 * (t % 2) + 512 * q
+            act(X("MD", o, o + 64), X("M", 256 * t + 64 * q, 256 * t + 64 * q + 64))
+            for w in (64, 128, 256)[:4 - len(PLAN["L" if t else "L0"][q]) // 2]:
+                act(X("MD", o + w, o + 2 * w), X("MD", o, o + w))
 
     pp = [0]
 
     def dbank():
         pp[0] += 1
-        return "d%d" % (pp[0] % 2)
+        return PLAN["D"][pp[0] % len(PLAN["D"])]
 
-    def leaders(t, k):
-        c0, c1 = BLOCKS[k]
-        nc, n, b = c1 - c0, 16 * (c1 - c0), "b%d" % k
-        md = X("MD", 1024 * (t % 2) + 64 * c0, 1024 * (t % 2) + 64 * c1)
-        mm(X(b, 0, n), X("IDN"), jc[nc], True, False)
-        step = 2 if nc >= 8 else 4
-        for u in range(4):
-            off = X("LST", 256 * t + 16 * c0 + 4 * nc * u, 256 * t + 16 * c0 + 4 * nc * (u + 1))
-            o = (256 * c0 + 4 * n * u, 256 * c0 + 4 * n * (u + 1))
-            if PLAN["L" if t else "L0"][k][u] == "v":
+    def leaders(t, q):
+        k, who = q // 2, PLAN["L" if t else "L0"][q]
+        b, n, second = "b%d" % k, 1024 // len(who), PLAN["Q"].index(q) > PLAN["Q"].index(q ^ 1)
+        md = X("MD", 2048 * (t % 2) + 512 * q, 2048 * (t % 2) + 512 * q + n)
+        if not second:
+            mm(X(b, 0, 128), X("IDN"), X("JC"), True, False)
+        for u in range(len(who)):
+            off = X("LST", 256 * t + 64 * q + n // 16 * u, 256 * t + 64 * q + n // 16 * (u + 1))
+            o = (1024 * q + n * u, 1024 * q + n * (u + 1))
+            if who[u] == "v":
                 tt(X("FL", *o), IX(LM, off), md, A.is_gt)
             else:
-                d = X(dbank(), 0, 4 * n)
+                d = X(dbank(), 0, n)
                 act(X("X", *o), IX(LM, off))
                 mm(d, X("IDN"), X("X", *o), True, False)
                 mm(d, X("IDM"), md, False, True)
-                act(X("FL", *o), d, F.Relu)
-            if u % step == step - 1:
-                u0 = u + 1 - step
-                lists(X(b, 4 * nc * u0, 4 * nc * (u + 1)), "VN", X("FL", 256 * c0 + 4 * n * u0, o[1]), False, u == 3)
-        s = 16 * c0
-        tt(X("SC", s, s + n), X(b, 0, n), X("CT", 256 * t + s, 256 * t + s + n), A.add)
-        for h in (8, 4, 2, 1):
-            tt(X("SC", s, s + h * nc) if h > 1 else X("SCM", c0, c1), X("SC", s, s + h * nc), X("SC", s + h * nc, s + 2 * h * nc), A.max)
-        ts(X("GI", c0, c1), X("SCM", c0, c1), 2047, A.bitwise_and)
-        cp(X("GL", c0, c1), X("GI", c0, c1))
+                act(X("FL", *o), d, F.Sign, bias=-0.5)
+                mm(X(b, q % 2 + n // 8 * u, n // 8 * (u + 1), 2), X("IDN"), X("C20", 0, n // 16), False, False)
+        lists(X(b, q % 2, 128, 2), "VN", X("FL", 1024 * q, 1024 * q + 1024), False, second)
+        if second:
+            s, c0 = 128 * k, 8 * k
+            tt(X("SC", s, s + 128), X(b, 0, 128), X("CT", 256 * t + s, 256 * t + s + 128), A.add)
+            for h in (64, 32, 16):
+                tt(X("SC", s, s + h), X("SC", s, s + h), X("SC", s + h, s + 2 * h), A.max)
+            for h in range(2):
+                tt(X("SCM", c0 + 4 * h, c0 + 4 * h + 4), X("SC", s + h, s + 8, 2), X("SC", s + 8 + h, s + 16, 2), A.max)
+            ts(X("GI", c0, c0 + 8), X("SCM", c0, c0 + 8), 2047, A.bitwise_and)
+            cp(X("GL", c0, c0 + 8), X("GI", c0, c0 + 8))
 
     def products(t, k):
         c0, c1 = BLOCKS[k]
@@ -443,11 +444,14 @@ def rank_program(g, core, T, topo):
         tt(hp, hp, X(b, 0, n), A.add)
         ts(X("HI", s, s + n), hp, 4095, A.bitwise_and)
         cp(X("HL", s, s + n), X("HI", s, s + n))
+        ts(X("D3", s, s + n), hp, 3, A.bitwise_and)
+        tt(X("NG", s, s + n), X("LG", s, s + n), X("M", 256 * t + s, 256 * t + s + n), A.is_gt)
 
     def seen(t, k):
         c0, c1 = BLOCKS[k]
         n, b, s = 16 * (c1 - c0), "b%d" % k, 16 * c0
         run = 2 if n % 64 == 0 else n // 32
+        mm(X(b, 0, n), X("NBL"), X("NG", s, s + n), True, False)
         for u in range(n // 32):
             l0 = s + 32 * u
             o, src = (16 * l0, 16 * l0 + 512), IX(SNW, X("HL", l0, l0 + 32))
@@ -462,14 +466,20 @@ def rank_program(g, core, T, topo):
             if u % run == run - 1:
                 a = 32 * (u + 1 - run)
                 for i in range(16):
-                    mm(X(b, a, 32 * u + 32), blk("CUM", i), X("FL", 16 * (s + a) + i, o[1], 16), a == 0 and i == 0, i == 15 and 32 * u + 32 == n)
-        tt(X("ZB", s, s + n), X(b, 0, n), X("HASR", s, s + n), A.min)
+                    mm(X(b, a, 32 * u + 32), blk("CUM", i), X("FL", 16 * (s + a) + i, o[1], 16), False, i == 15 and 32 * u + 32 == n)
+        o = (s, s + n)
+        ts(X("ZB", *o), X(b, 0, n), 0.0, A.is_gt)
+        mm(X("m1", *o), X("BD"), X("ZB", *o), True, True)
+        mm(X("m2", *o), X("Z4"), X("ZB", *o), True, False)
+        tt(X("TD", *o), X("m1", *o), X("D3", *o), A.mult)
+        mm(X("m2", *o), X("BLK"), X("TD", *o), False, True)
 
     def keys(t):
         ka = X("LI", 64 * t + 48, 64 * t + 64)
         ts(X("HASB"), X("SCM"), 2048.0, A.is_ge, 8192.0, A.mult)
-        for c0, c1 in BLOCKS:
-            tt(X("K1", c0, c1), X("CT", 256 * t + 16 * c0, 256 * t + 15 * c0 + c1), X("HASB", c0, c1), A.subtract)
+        for q in range(4):
+            o = 256 * t + 128 * (q // 2)
+            tt(X("K1", 4 * q, 4 * q + 4), X("CT", o + q % 2, o + 8, 2), X("HASB", 4 * q, 4 * q + 4), A.subtract)
         ts(ka, X("K1"), 256.0, A.add, 0.0, A.max)
         both = X("LI", 64 * t + 32, 64 * t + 64)
         ts(X("KP", 0, 32), both, 8160, A.bitwise_and)
@@ -477,19 +487,15 @@ def rank_program(g, core, T, topo):
         cp(X("KPB"), X("KP"))
         for h in range(2):
             for r in range(16):
-                mm(X("m0", r, 512, 16), blk("SEL", r), X("KPB", 32 * h, 32 * h + 32), h + r == 0, h + r == 16)
-        for h in range(2 if t < 3 else 0):
-            for r in range(16):
-                mm(X("m1", 256 + r, 512, 16), blk("SEL", r), X("KPB", 32 * h + 16, 32 * h + 32), h + r == 0, False)
-        act(X("HASR"), X("m0", 256, 512), F.Relu, bias=1.0, scale=-1.0)
+                mm(X("m0", r, 512, 16), blk("SEL", r), X("KPB", 32 * h, 32 * h + 32), h + r == 0, h + r == 16 and t == 3)
         tt(X("B2"), X("L4"), X("HASB"), A.subtract)
         tt(X("B2"), X("B2"), X("BASE"), A.max)
 
-    def winners(kb):
+    def winners(kb, kf):
         first = PLAN["EQ"]
         cp(X("KR"), X(kb, 256, 512))
         if first < 16:
-            act(X("NKF"), X("KF"), scale=-1.0)
+            act(X("NKF"), kf, scale=-1.0)
         at = 0
         for c in range(first, 16):
             n = 256 - 16 * c
@@ -498,58 +504,48 @@ def rank_program(g, core, T, topo):
             at += n
         for c in range(16):
             if c < first:
-                ts(X("EQ", 272 * c, 256 * c + 256), X("KR", 16 * c, 256), X("KF", c, c + 1), A.is_equal)
+                ts(X("EQ", 272 * c, 256 * c + 256), X("KR", 16 * c, 256), X(kf[0], kf[1] + c * kf[3], kf[1] + c * kf[3] + 1), A.is_equal)
             if c < 15:
                 mm(X("d0", 16 * c + 16, 256), X("BLK"), X("EQ", 272 * c + 16, 256 * c + 256), c == 0, c == 14)
         act(X("DUPS", 16, 256), X("d0", 16, 256), scale=-65536.0)
         for r in range(16):
             mm(X("d1", 0, 16), blk("TRI", r), X("EQ", r, 4096, 272), r == 0, False)
         lists(X("d1", 1, 16), "MS", X("DUPS", 16, 256), False, True)
-        tt(X("XK"), X("d1", 0, 16), X("KF"), A.add)
+        tt(X("XK"), X("d1", 0, 16), kf, A.add)
 
     candidates(0, 0, 16)
     for t in range(4):
         m, nx = X("M", 256 * t, 256 * t + 256), 256 * t + 256
-        for k in range(len(BLOCKS)):
-            leaders(t, k)
-        if t < 3:
-            candidates(t + 1, 12, 16)
-        keys(t)
         act(X("R", 4096, 4352), m)
-        products(t, 0)
-        if t == 3:
-            cp(X("KF"), X("LI", 64 * t + 48, 64 * t + 64))
-        for k in range(1, len(BLOCKS)):
-            products(t, k)
-        if t == 3:
-            winners("m0")
-            tt(X("X2"), X("XK"), X("LANE"), A.max)
-            cp(X("LLA"), X("X2"))
-            cp(IX(X("TAB", 0, 2304), X("LLA")), m)
-            store("y", "dyl", T.yl[:], LM)
-        else:
-            tt(X("MT"), X("LT", 256 * t - 256, 256 * t) if t else X("LTC"), X("TL", 256, 512), A.max)
-            act(X("TA"), X("MT"), F.Abs, bias=-4096.0)
+        for step in PLAN["ORDER"].split():
+            if step[0] in "LPS":
+                {"L": leaders, "P": products, "S": seen}[step[0]](t, int(step[1]))
+            elif step == "K":
+                keys(t)
+            elif step == "C" and t < 3:
+                candidates(t + 1, 12, 16)
+            elif step == "W" and t == 3:
+                cp(X("KF"), X("LI", 64 * t + 48, 64 * t + 64))
+                winners("m0", X("KF"))
+                tt(X("X2"), X("XK"), X("LANE"), A.max)
+                cp(X("LLA"), X("X2"))
+                cp(IX(X("TAB", 0, 2304), X("LLA")), m)
+                store("y", "dyl", T.yl[:], LM)
+        if t < 3:
+            n = 192 if t else 0
+            if n:
+                tt(X("MT", 0, n), X("LT", 192 * t - 192, 192 * t), X("TL", 256, 256 + n), A.max)
+                act(X("TA", 0, n), X("MT", 0, n), F.Abs, bias=-4096.0)
+            act(X("TA", n, 256), X("TL", 256 + n, 512), F.Identity, bias=4096.0, scale=not0)
             act(X("TB"), X("TA"), F.Identity, bias=4096.0, scale=-1.0)
-            tt(X("TY"), X("TA"), X("m0", 0, 256), A.subtract)
         if t < 2:
             act(X("TGF"), IX(TLW, X("GL")), F.Identity, bias=8192.0, scale=-1.0)
-        ts(X("D3"), X("HP"), 3, A.bitwise_and)
-        if t < 3:
-            ts(X("HH", 0, 256), X("HP"), 4080, A.bitwise_and)
-            ts(X("HH", 256, 512), X("HP"), 15, A.bitwise_and)
-        for k in range(len(BLOCKS)):
-            seen(t, k)
-        mask = X("m0", 0, 256)
-        mm(mask, X("BD"), X("ZB"), True, True)
-        mm(X("b0", 0, 256), X("Z4"), X("ZB"), True, False)
-        lists(X("m2", 0, 16), "MS", X("ZB"))
-        tt(X("TD"), mask, X("D3"), A.mult)
-        mm(X("b0", 0, 256), X("BLK"), X("TD"), False, True)
-        tt(X("PLF"), X("B2"), X("m2", 0, 16), A.subtract)
+        mask = X("m1", 0, 256)
+        lists(X("b0", 0, 16), "MS", X("ZB"))
+        tt(X("PLF"), X("B2"), X("b0", 0, 16), A.subtract)
         cp(X("PL"), X("PLF"))
         act(X("PCB"), IX(X("R"), X("PL")), F.Identity, bias=255.0, scale=-1.0)
-        ts(X("E"), X("b0", 0, 256), ecol, A.is_equal)
+        ts(X("E"), X("m2", 0, 256), ecol, A.is_equal)
         call("v", g.vector.tensor_tensor_scan, X("CS"), [X("E"), X("CAPC"), ini, A.add, A.min], us(X("CS"), [X("E")]))
         tt(X("SL"), X("CS"), X("E"), A.mult)
         lists(X("b1", 0, 16), "MS", X("SL"))
@@ -561,18 +557,14 @@ def rank_program(g, core, T, topo):
         if t < 2:
             act(X("MSK"), mask, scale=8192.0)
         if t < 3:
-            tt(X("TH", 0, 256), mask, X("HH", 0, 256), A.mult)
-            tt(X("TH", 256, 512), mask, X("HH", 256, 512), A.mult)
-            mm(X("m1", 256, 512), X("ZK"), X("ZB"), False, False)
-            mm(X("m1", 256, 512), X("BLK"), X("TH", 0, 256), False, False)
-            mm(X("m1", 256, 512), X("BLK"), X("TH", 256, 512), False, True)
-            lists(X("b2", 0, 32), "MS", X("TH"))
-            ts(X("K1"), X("m2", 0, 16), 0.0, A.is_gt, 2304.0, A.mult)
-            tt(X("K1"), X("K1"), X("LI", 64 * t + 48, 64 * t + 64), A.add)
-            tt(X("K1"), X("K1"), X("b2", 0, 16), A.add)
-            tt(X("KF"), X("K1"), X("b2", 16, 32), A.add)
+            tt(X("TH"), mask, X("HI"), A.mult)
+            mm(X("m0", 256, 512), X("ZK"), X("ZB"), False, False)
+            mm(X("m0", 256, 512), X("BLF"), X("TH"), False, True)
+            tt(X("KD"), X("m0", 256, 512), X("DIAG"), A.mult)
+            call("v", g.vector.tensor_tensor_scan, X("KS"), [X("SEG"), X("KD"), 0.0, A.mult, A.add], us(X("KS"), [X("KD")]))
             act(X("VAL"), IX(X("R"), X("PL")))
-            winners("m1")
+            winners("m0", X("KS", 15, 256, 16))
+            tt(X("TY"), X("TA"), X("m0", 0, 256), A.subtract)
             tt(X("X2"), X("XK"), X("LANE"), A.max)
             cp(X("LLA"), X("X2"))
             cp(IX(X("TAB"), X("LLA")), X("VAL"))
@@ -583,8 +575,8 @@ def rank_program(g, core, T, topo):
         if t < 2:
             st = "ST%d" % t
             tt(IX(X(st), X("SLOT")), X("MSK"), X("TGF"), A.max)
-            send("ft%d" % (t + 1), "LT", 256 * t + 48 * rank, st, lambda p: 256 * p)
-            act(X("LT", 256 * t + 48 * rank, 256 * t + 48 * rank + 48), X(st, 256 * rank, 256 * rank + 48))
+            send("ft%d" % (t + 1), "LT", 192 * t + 48 * rank, st, lambda p: 256 * p)
+            act(X("LT", 192 * t + 48 * rank, 192 * t + 48 * rank + 48), X(st, 256 * rank, 256 * rank + 48))
         if t < 3:
             candidates(t + 1, 0, 12)
     store("s", "dyf", T.yf[:], X("M", 1024, 1280))

@@ -4,27 +4,35 @@ from concourse.mybir import AluOpType as A, ActivationFunctionType as F
 
 BF, FP, I32, U16 = "bfloat16", "float32", "int32", "uint16"
 BLOCKS = [(0, 8), (8, 16)]
-PLAN = {"L": ["svsv", "sv", "vv", "ss"], "L0": ["vv", "vs", "sv", "sv"], "PG": ["svsv", "svss"], "PP": ["vsss", "ssss"],
-        "S": ["ssvs", "vvvs"], "NEG": "vvvvvvvv", "EQ": 10, "Q": [3, 0, 1, 2],
-        "ORDER": "L3 L0 L1 L2 P0 P1 C K S0 S1 W", "D": ["d0", "d1", "b2"]}
+PLAN = {"L": ["ss", "vvsv", "vvvv", "ssss"], "L0": ["sv", "vvss", "vv", "vsss"], "PG": ["vxxx", "xvxx"], "PP": ["svss", "ssxv"],
+        "S": ["vvsv", "sssvvsvv"], "NEG": "xxxxxxxx", "EQ": 9, "EQ3": 4, "MOD": "ss", "NG": ["s", "v"], "F": ["sssxs"], "ST": "s", "GATE": 1, "TWO": 0,
+        "Q": [3, 2, 0, 1], "ORDER": "L3 L2 L0 L1 P1 P0 S1 C S0 K W", "D": ["d0", "d1", "b2"]}
 SIZES = {
-    BF: {"TAB": 6400, "MO": 2048, "FR": 1024, "M": 1280, "MD": 4096, "ONES": 2048, "BLK": 128, "IDN": 128, "IDM": 128, "Z": 128, "DK": 16,
-         "WBU": 128, "WBV": 128, "BD": 128, "Z4": 128, "ZK": 128, "NBL": 128, "C255": 128, "C20": 32, "JC": 128, "WU": 2048, "WV": 2048, "VN": 2048, "MS": 2048,
-         "SEL": 2048, "TRI": 2048, "CUM": 2048, "EX": 2048, "X": 4096, "FL": 4096, "R": 4352, "LG": 256, "QT": 256, "NG": 256, "ZB": 256,
+    BF: {"TAB": 6400, "MO": 2048, "FR": 1024, "MD": 4096, "ONES": 512, "BLK": 128, "IDN": 128, "IDM": 128, "Z": 128, "Z4C": 128, "OWN": 128, "W4": 1024, "SEN": 128, "DK": 256, "SGN": 64, "C12": 512, "BD6": 128, "C21": 128, "C19": 256, "UF": 512,
+         "WB": 256, "MR": 192, "EQT": 2176, "W2": 16, "HF": 256, "BD": 128, "Z4": 128, "ZK": 128, "NBL": 128, "C255": 128, "C20": 32, "JC": 128, "VN": 2048,
+         "SEL": 2048, "TRI": 2048, "CUM": 2048, "EX": 2048, "X": 4096, "FL": 4096, "R": 5376, "LG": 256, "QT": 256, "NG": 256, "ZB": 256,
          "TD": 256, "DIAG": 256, "SEG": 256, "E": 256, "CS": 256, "SL": 256, "CAPC": 256, "PCB": 256, "VAL": 256, "KPB": 64, "EQ": 4096, "DUPS": 256,
          "SM0": 1280, "SM1": 1280, "SM2": 1280, "SM3": 1280},
-    FP: {"TL": 2304, "PF": 8, "WF": 4, "WN": 4, "KJ": 16, "LF": 192, "LANE": 16, "BASE": 16, "L4": 16, "HASB": 16, "B2": 16, "PLF": 16,
+    FP: {"TL": 6400, "PF": 12, "WF": 4, "WN": 4, "KJ": 256, "KU": 256, "LF": 32, "IDF": 128, "HY": 256, "U4": 128, "U2": 64, "NDF": 128, "SC": 256, "SP": 256, "SX": 256, "LANE": 16, "BASE": 16, "L4": 64, "HASB": 16, "B2": 16, "PLF": 16,
          "K1": 16, "KF": 16, "NKF": 16, "XK": 16, "X2": 16, "LT": 384, "MT": 256, "TA": 256, "TB": 256, "TY": 256, "TGF": 256,
-         "MSK": 256, "EQT": 1024, "TH": 256, "KD": 256, "KS": 256, "BLF": 128, "ST0": 1280, "ST1": 1280},
-    I32: {"TLI": 2048, "WKI": 3, "CI": 128, "CM": 128, "CG": 128, "PI": 4, "LI": 256, "CT": 1024, "SC": 256, "SCM": 16, "GI": 16, "KP": 64,
+         "MSK": 256, "KRF": 256, "TH": 256, "KD": 256, "KS": 256, "BLF": 128, "ST0": 1280, "ST1": 1280},
+    I32: {"TLI": 2048, "WKI": 3, "CI": 128, "CM": 128, "CG": 128, "PI": 8, "LI": 320, "CT": 1216, "GI": 16, "KP": 64,
           "UI": 512, "PRD": 256, "HP": 256, "HI": 256, "D3": 256},
-    U16: {"LST": 1024, "TG": 256, "HL": 256, "KR": 256, "GL": 16, "PL": 16, "SLOT": 16, "LLA": 16, "LLB": 16},
+    U16: {"LST": 1216, "TG": 256, "HL": 256, "KR": 256, "GL": 16, "PL": 16, "SLOT": 16, "LLA": 16, "LC": 32},
 }
-SCRATCH, WIDTH, DTYPE = {}, {}, {}
+SCRATCH, WIDTH, DTYPE, SMALL = {}, {}, {}, {}
 for _d in SIZES:
-    for _n in SIZES[_d]:
-        SCRATCH[_n] = ("sbuf", [128, SIZES[_d][_n]], _d)
-        WIDTH[_n], DTYPE[_n] = SIZES[_d][_n], _d
+    _p = "small_" + _d
+    WIDTH[_p], DTYPE[_p] = 0, _d
+    for _n, _w in SIZES[_d].items():
+        if _w <= 128:
+            SMALL[_n] = (_p, WIDTH[_p], _w)
+            WIDTH[_p] += -(-_w // 16) * 16
+        else:
+            WIDTH[_n], DTYPE[_n] = _w, _d
+SMALL["M"] = ("R", 4096, 1280)
+for _n in WIDTH:
+    SCRATCH[_n] = ("sbuf", [128, WIDTH[_n]], DTYPE[_n])
 BANKS = ["b0", "b1", "b2", "d0", "d1", "m0", "m1", "m2"]
 for _b in BANKS:
     SCRATCH[_b] = ("psum", [128, 512], FP)
@@ -32,10 +40,15 @@ for _b in BANKS:
 _DMAS = ["wk", "fm", "fr", "lm", "tl", "mo", "sn", "yl", "yf"]
 SEMAPHORES = (["sv", "ss", "st", "sg", "loc"] + ["d" + x for x in _DMAS]
               + ["pre%d" % t for t in range(4)] + ["fm%d" % t for t in range(1, 5)] + ["ft%d" % t for t in range(1, 3)])
-CYC, PEC, WAKE, HOP, SLACK, PASSES = 0.0009, 0.00046, 0.12, 3.0, 0.2, 3
+CYC, FIX, PEC, WAKE, HOP, SLACK, PASSES, SHAKE, LOAD, OWN = 0.00094, 0.0, 0.00048, 0.15, 2.5, 0.35, 3, 0.5, 0.0006, 1.0
+
+TRIES, PLANNED, CROSS, FIRST = 0, {}, 0.15, 10.0
 
 
 def X(name, a=0, b=None, s=1, p=None):
+    if name in SMALL:
+        name, at, w = SMALL[name]
+        return (name, at + a, at + (w if b is None else b), s, p)
     return (name, a, WIDTH[name] if b is None else b, s, p)
 
 
@@ -68,9 +81,10 @@ def rank_program(g, core, T, topo):
     writer = {n: np.full(WIDTH[n], -1) for n in WIDTH}
     readers = {n: [] for n in WIDTH}
     bank = {}
+    gate = {}
 
     def add(e, sem, inc, rd, wr, cost, late, call, follow=()):
-        n, before, order = len(rec), set(), set(follow)
+        n, before, order = len(rec), set(), set(follow) | set(gate.pop(e, ()))
         rd = [y for x in rd if isinstance(x, tuple) for y in (x[1:] if x[0] == "*" else [x])] + [x[2] for x in wr if x[0] == "*"]
         wr = [x[1] if x[0] == "*" else x for x in wr]
         for x in rd + wr:
@@ -105,15 +119,15 @@ def rank_program(g, core, T, topo):
         rec.append([e, sem, inc, before, order, cost, late, call])
         return n
 
-    def us(out, ins, two=False):
+    def us(out, ins, two=False, first=0.063):
         if out[0] == "*":
-            return 0.05 + 3.8 * CYC * cols(out)
+            return first + 3.8 * CYC * cols(out)
         if ins and ins[0][0] == "*":
-            return 0.06 + 1.56 * CYC * cols(out)
+            return first + 1.56 * CYC * cols(out)
         r = 0.5 if all(DTYPE[x[0]] in (BF, U16) for x in [out] + ins) else 1.0
         if two and not any(x[0] in BANKS for x in ins):
             r *= 2
-        return max(70, r * cols(out)) * CYC
+        return FIX + max(64, r * cols(out)) * CYC
 
     def call(e, f, out, args, cost, **kw):
         ins = [x for x in list(args) + list(kw.values()) if isinstance(x, tuple)]
@@ -128,11 +142,28 @@ def rank_program(g, core, T, topo):
     def ts(out, a, s1, op0, s2=None, op1=None):
         call("v", g.vector.tensor_scalar, out, [a, s1, s2, op0] + ([] if op1 is None else [op1]), us(out, [a]))
 
+    def scan(out, a, b, first, op0, op1):
+        call("v", g.vector.tensor_tensor_scan, out, [a, b, first, op0, op1], us(out, [a, b]))
+
     def fill(out, v):
         call("v", g.vector.memset, out, [v], us(out, []))
 
     def act(out, a, fn=F.Copy, **kw):
-        call("s", g.scalar.activation, out, [a, fn], us(out, [a]) if a[0] == "*" else max(70, cols(out)) * CYC, **kw)
+        call("s", g.scalar.activation, out, [a, fn], us(out, [a], first=0.081) if "*" in (a[0], out[0]) else FIX + max(64, cols(out)) * CYC, **kw)
+
+    either = {}
+
+    def lin(who, out, a, scale=1.0, bias=0.0, relu=False):
+        ins = [x for x in (a, scale, bias) if isinstance(x, tuple)]
+        plain = scale == 1.0 and bias == 0.0 and not relu
+        fn = {"v": (lambda: g.vector.tensor_copy(ap(out), ap(a))) if plain else
+              (lambda: g.vector.tensor_scalar(ap(out), ap(a), ap(scale), ap(bias), A.mult, A.max if relu else A.add)),
+              "s": lambda: g.scalar.activation(ap(out), ap(a), F.Relu if relu else F.Identity, bias=ap(bias), scale=ap(scale))}
+        cost = {"v": us(out, [a]), "s": us(out, [a], first=0.081) if a[0] == "*" else FIX + max(64, cols(out)) * CYC}
+        if who != "x":
+            return add(who, SN[who], 1, ins, [out], cost[who], 0.0, fn[who])
+        either[len(rec)] = cost
+        add("x%d" % len(rec), None, 1, ins, [out], cost["v"], 0.0, fn)
 
     def mm(out, lhsT, rhs, start, stop):
         call("t", g.tensor.matmul, out, [lhsT, rhs, start, stop], max(64, cols(rhs)) * PEC * (4 if DTYPE[rhs[0]] == FP else 1))
@@ -141,23 +172,25 @@ def rank_program(g, core, T, topo):
         kw = {} if DTYPE[out[0]] == I32 else {"allow_small_or_imprecise_dtypes": True}
         call("g", g.iota, out, [pat, base, cm], 0.15 + 2 * CYC * cols(out), **kw)
 
-    def select(out, a, pat, op, base, cm):
-        call("g", g.affine_select, out, [a, pat, op, 0.0, base, cm], 0.2 + 2 * CYC * cols(out))
+    def select(out, a, pat, op, base, cm, other=0.0):
+        call("g", g.affine_select, out, [a, pat, op, other, base, cm], 0.2 + 2 * CYC * cols(out))
 
-    loaded = [1.8]
+    loaded = [1.2]
 
     def load(e, sem, out, src):
-        loaded[0] += 0.4 + cols(out) * (2 if DTYPE[out[0]] == BF else 4) * 0.0004
+        loaded[0] += 0.4 + cols(out) * (2 if DTYPE[out[0]] == BF else 4) * LOAD
         add(e, sem, 16, [], [out], 0.1, loaded[0], lambda: Q[e].dma_start(ap(out), src), follow=last[e])
         last[e] = [len(rec) - 1]
 
     def store(e, sem, dst, a):
-        add(e, sem, 16, [a], [], 0.1, 3.0, lambda: Q[e].dma_start(dst, ap(a)))
+        n = add(e, sem, 16, [a], [], 0.1, 0.0, lambda: Q[e].dma_start(dst, ap(a)))
+        rec.append([None, None, 0, {n}, set(), 0.0, 0.0, None])
+        rec[n][6] = 1.4 + cols(a) * 2 * LOAD
 
     lands, last = {}, {"send": [], "y": [], "s": []}
 
     def land(sem, name, at):
-        lands[sem] = add(None, sem, 12, [], [X(name, at(p), at(p) + 48) for p in peers], 0.0, HOP, None)
+        lands[sem] = add(None, sem, 12, [], [X(name, at(p), at(p) + 48) for p in peers], 0.0, HOP + FIRST * (sem == "pre0"), None)
 
     def send(sem, dst, to, src, at):
         tr = []
@@ -165,7 +198,7 @@ def rank_program(g, core, T, topo):
             rid, pid, _ = topo.addr(T.cores[p])
             eng = topo.engines(core, T.cores[p])
             tr.append(RemoteDMATransfer(dst_ids=[DstId(rid=rid, pnc=pid)], dma_engine_mask=sum(1 << x for x in eng[4 * n:4 * n + 4]),
-                                        remote_sem=S[sem], src=T[src][:, at(p):at(p) + 48], dst=T[dst][:, to:to + 48]))
+                                        remote_sem=S[sem], src=ap(X(src, at(p), at(p) + 48)), dst=ap(X(dst, to, to + 48))))
         n = add("g", "loc", 12, [X(src, at(p), at(p) + 48) for p in peers], [], 0.3, 1.0, lambda: g.remote_dma_fused(tr, local_sem=S.loc), follow=last["send"])
         last["send"] = [n]
         rec[lands[sem]][4].add(n)
@@ -176,11 +209,11 @@ def rank_program(g, core, T, topo):
         for k in range(n):
             for i in rec[k][3] | rec[k][4]:
                 soft = i not in rec[k][3] or (rec[k][0] == "t" and rec[i][0] == "t")
-                gap = 0.0 if soft else rec[i][6] + WAKE
+                gap = 0.0 if soft else rec[i][6] + (WAKE if rec[i][0] == rec[k][0] else CROSS)
                 ahead[i].append((k, gap))
                 back[k].append((i, gap))
 
-        def plan(nxt, prv, weight):
+        def plan(nxt, prv, weight, fixed=None):
             left, can, end, order = [len(x) for x in prv], [0.0] * n, [0.0] * n, []
             ready, now = {e: [] for e in Q}, {e: 0.0 for e in Q}
 
@@ -196,7 +229,8 @@ def rank_program(g, core, T, topo):
                     end[k] = can[k]
                     done(k)
                 else:
-                    ready[rec[k][0]].append(k)
+                    for e in [rec[k][0]] if k not in either else fixed[k] if fixed else "vs":
+                        ready[e].append(k)
             for k in [i for i in range(n) if not left[i]]:
                 free(k)
             while any(ready.values()):
@@ -205,26 +239,47 @@ def rank_program(g, core, T, topo):
                     if ready[e]:
                         k = min(ready[e], key=lambda i: (max(now[e], can[i]), -weight[i]))
                         t0 = max(now[e], can[k]) + min(SLACK, 0.6 * rec[k][5])
-                        k = max([i for i in ready[e] if can[i] <= t0], key=lambda i: weight[i])
+                        k = max([i for i in ready[e] if can[i] <= t0], key=lambda i: weight[i] - (OWN if e == "v" and i in either else 0))
                         if best is None or max(now[e], can[k]) < best[0]:
                             best = (max(now[e], can[k]), e, k)
                 st, e, i = best
-                ready[e].remove(i)
-                now[e] = end[i] = st + rec[i][5]
-                order.append(i)
+                for q in "vs" if i in either and not fixed else [e]:
+                    ready[q].remove(i)
+                now[e] = end[i] = st + (either[i][e] if i in either else rec[i][5])
+                order.append((i, e))
                 done(i)
             return order, end
-        order, end = plan(ahead, back, [-i for i in range(n)])
-        best = (max(end), order)
-        for _ in range(PASSES):
-            order, end = plan(ahead, back, plan(back, ahead, end)[1])
-            best = min(best, (max(end), order))
+        def fits(order):
+            at = {i: k for k, (i, _) in enumerate(order)}
+            for i in range(n):
+                if rec[i][0] is None:
+                    at[i] = max([-1] + [at.get(d, n) for d, _ in back[i]])
+            return len(at) == n and all(at[d] <= at[i] for i in range(n) for d, _ in back[i])
+        if not PLANNED or not fits(PLANNED["best"][1]):
+            order, end = plan(ahead, back, [-i for i in range(n)])
+            best = None
+            for k in range(PASSES):
+                late = np.array(plan(back, ahead, end, dict(order))[1])
+                order, end = plan(ahead, back, late.tolist())
+                if best is None or max(end) < best[0]:
+                    best = (max(end), order, late, np.array(end))
+            shake = np.random.default_rng(0)
+            for k in range(TRIES):
+                at = shake.random() * best[0]
+                late = best[2] + (np.abs(best[3] - at) < 3.0) * SHAKE * shake.random() * shake.standard_normal(n)
+                order, end = plan(ahead, back, late.tolist())
+                if max(end) <= best[0]:
+                    best = (max(end), order, late, np.array(end))
+            PLANNED.update(best=best)
+        best = PLANNED["best"]
         cnt, known, snap, pos = {k: 0 for k in SEMAPHORES}, {e: {} for e in Q}, {}, {}
         for i in lands.values():
             cnt[rec[i][1]] += rec[i][2]
             pos[i] = (rec[i][1], rec[i][2])
-        for i in best[1]:
-            e, sem, inc, before, _, cost, late, fn = rec[i]
+        for i, e in best[1]:
+            _, sem, inc, before, _, cost, late, fn = rec[i]
+            if i in either:
+                sem, fn = SN[e], fn[e]
             need = {}
             for d in before:
                 if not (e == "t" and rec[d][0] == "t") and known[e].get(pos[d][0], 0) < pos[d][1]:
@@ -265,16 +320,16 @@ def rank_program(g, core, T, topo):
     load("y", "dlm", LM, T.lm[:])
     load("y", "dtl", X("TLI"), T.tl[:])
     load("y", "dmo", X("MO"), T.mo[:])
-    load("y", "dsn", SNW, T.sn[:])
     load("y", "dfr", X("FR"), T.fr[:])
+    load("y", "dsn", SNW, T.sn[:])
 
-    rp, gp, pf, ecol, ini, cap, row0, not0 = [X("PF", k, k + 1) for k in range(8)]
+    rp, gp, pf, ecol, ini, cap, row0, not0, g16, r4, x4, x15 = [X("PF", k, k + 1) for k in range(12)]
     iota(X("CI"), [[1, 128]], 0, 0)
     iota(X("PI", 0, 1), [[0, 1]], 0, 1)
-    iota(X("JC"), [[-2048, 16], [0, 8]], 32768, 0)
+    iota(X("JC"), [[0, 2], [-2048, 16], [0, 4]], 32768, 0)
     fill(X("ONES"), 1.0)
-    fill(X("C255"), 255.0)
-    fill(X("C20"), -16 * 65536.0)
+    for c, v in ((X("C19"), 129 * 4096), (X("C255"), 255), (X("C20"), -16 * 65536), (X("C12", 0, 256), 4096), (X("C12", 256, 512), 0)):
+        iota(c, [[0, cols(c)]], v, 0)
     ts(X("CM"), X("CI"), 15, A.bitwise_and)
     ts(X("CG"), X("CI"), 4, A.arith_shift_right)
     ts(X("PI", 1, 2), X("PI", 0, 1), 15, A.bitwise_and)
@@ -284,26 +339,48 @@ def rank_program(g, core, T, topo):
     cp(gp, X("PI", 2, 3))
     cp(pf, X("PI", 0, 1))
     ts(X("BLK"), X("CG"), gp, A.is_equal)
-    ts(X("IDN"), X("CI"), pf, A.is_equal)
-    ts(X("IDM"), X("CI"), pf, A.is_equal, -1.0, A.mult)
+    select(X("IDN"), X("ONES", 0, 128), [[-1, 128]], A.is_equal, 0, 1)
+    act(X("IDM"), X("IDN"), scale=-1.0)
     cp(X("WF", 0, 3), X("WKI"))
     ts(X("WN", 0, 3), X("WKI"), -1.0, A.mult)
     ts(X("Z"), X("CM"), 99.0, A.add)
     tt(X("Z"), X("Z"), X("BLK"), A.mult)
     for r in range(16):
-        ts(blk("MS", r), X("Z"), 99.0 + r, A.is_equal)
+        ts(blk("VN", r), X("Z"), 99.0 + r, A.is_equal, -65536.0, A.mult)
+    for h in range(2):
+        ts(X("W2", 8 * h, 8 * h + 8), X("CI", 0, 8), gp, A.is_equal, X("WN", h, h + 1), A.mult)
+    iota(X("Z4C"), [[0, 32], [1, 4]], 99, 0)
+    tt(X("Z4C"), X("Z4C"), X("BLK"), A.mult)
+    for h in range(8):
+        ts(blk("W4", h), X("Z4C"), 99.0 + h % 4, A.is_equal, X("WF", h // 4, h // 4 + 1), A.mult)
+    ts(X("PI", 5, 6), X("PI", 1, 2), 2, A.arith_shift_right)
+    ts(g16, X("PI", 5, 6), 99.0, A.add)
+    iota(X("OWN"), [[0, 32], [1, 4]], 99, 0)
+    ts(X("OWN"), X("OWN"), g16, A.is_equal)
+    iota(X("DK"), [[0, 4], [1, 16], [0, 4]], 0, 0)
+    ts(X("DK"), X("DK"), rp, A.is_equal, X("WF", 2, 3), A.mult)
+    mm(X("m1", 0, 256), X("BLK"), X("DK"), True, True)
+    act(X("KJ"), X("m1", 0, 256))
+    iota(X("LF", 0, 8), [[64, 2], [1, 4]], 0, 0)
+    iota(X("LF", 16, 32), [[4, 4], [0, 4]], 0, 0)
+    ts(X("PI", 4, 5), X("PI", 0, 1), 3, A.bitwise_and)
+    cp(r4, X("PI", 4, 5))
+    ts(x4, rp, 4.0, A.mult)
+    ts(X("LC", 0, 8), X("LF", 0, 8), x4, A.add)
+    ts(X("LC", 16, 32), X("LF", 16, 32), r4, A.add)
+    ts(x15, r4, -15.0, A.mult)
+    ts(X("LC", 8, 9), rp, 16.0, A.mult, x15, A.add)
+    act(X("IDF"), X("IDN"))
+    act(X("WB", 0, 128), X("BLK"), scale=X("WF", 0, 1))
+    act(X("WB", 128, 256), X("BLK"), scale=X("WF", 1, 2))
     for h in range(4):
         o = (512 * h, 512 * h + 512)
-        ts(X("WU", *o), X("MS", *o), X("WN", 0, 1), A.mult)
-        act(X("WV", *o), X("MS", *o), scale=X("WN", 1, 2))
-        act(X("VN", *o), X("MS", *o), scale=-65536.0)
-    ts(X("DK"), X("CI", 0, 16), rp, A.is_equal, X("WF", 2, 3), A.mult)
-    mm(X("m1", 0, 16), X("BLK"), X("DK"), True, True)
-    cp(X("KJ"), X("m1", 0, 16))
-    act(X("WBU"), X("BLK"), scale=X("WF", 0, 1))
-    act(X("WBV"), X("BLK"), scale=X("WF", 1, 2))
-    select(X("EX"), X("ONES"), [[-1, 128], [0, 16]], A.is_equal, 0, 1)
-    select(X("SEL"), X("ONES"), [[-1, 16], [-16, 8], [0, 16]], A.is_equal, 0, 1)
+        select(X("EX", *o), X("ONES"), [[-1, 32], [0, 16]], A.is_equal, -32 * h, 1)
+    for t in range(4):
+        send("pre%d" % t, "SM%d" % t, 256 * rank, "FR", lambda p: 256 * t + 48 * p)
+    for h in range(4):
+        gate["g"] = last["send"]
+        select(X("SEL", 512 * h, 512 * h + 512), X("ONES"), [[-1, 4], [-16, 8], [0, 16]], A.is_equal, -4 * h, 1)
     for i in range(16):
         select(blk("CUM", i), X("BLK"), [[0, 8], [1, 16]], A.is_ge, -i, 0)
     select(X("TRI"), X("VN"), [[0, 16], [16, 8], [1, 16]], A.is_gt, 0, -1)
@@ -314,17 +391,23 @@ def rank_program(g, core, T, topo):
     act(X("BLF"), X("BLK"))
     for h in range(2):
         ts(X("DIAG", 128 * h, 128 * h + 128), X("CM"), rp, A.is_equal)
-        ts(X("SEG", 128 * h, 128 * h + 128), X("CM"), 0.0, A.is_gt)
+    select(X("SEG"), X("ONES", 0, 256), [[0, 16], [1, 16]], A.is_gt, 0, 0)
+    select(X("SEN"), X("C12", 256, 384), [[0, 8], [1, 16]], A.is_gt, 0, 0, -2.0 ** 30)
     ts(X("LANE"), X("CI", 0, 16), 16.0, A.mult, rp, A.add)
-    ts(X("BASE"), X("LANE"), 16.0, A.mult, 16.0, A.add)
-    ts(X("L4"), X("LANE"), 4096.0, A.add)
+    act(X("BASE"), X("LANE"), F.Identity, scale=16 * 65536.0, bias=16 * 65536.0)
+    for t in range(4):
+        act(X("L4", 16 * t, 16 * t + 16), X("LANE"), F.Identity, scale=65536.0, bias=(4096 + 256 * t) * 65536.0)
     ts(ecol, X("PI", 3, 4), -4.0, A.add)
     ts(ini, rp, -8.0, A.add, 0.0, A.max)
     ts(ini, ini, 256.0, A.mult)
     ts(cap, rp, 8.0, A.is_lt, 256.0, A.mult)
-    ts(X("CAPC"), X("ONES", 0, 256), cap, A.mult, ini, A.max)
+    tt(cap, cap, ini, A.max)
+    act(X("CAPC"), X("ONES", 0, 256), scale=cap)
     ts(row0, rp, 0.0, A.is_equal, 8192.0, A.mult)
-    ts(not0, rp, 0.0, A.is_gt, -1.0, A.mult)
+    ts(not0, rp, 0.0, A.is_gt)
+    iota(X("SGN"), [[0, 2], [2, 2], [0, 16]], -1, 0)
+    act(X("NDF"), X("IDM"))
+    act(X("BD6"), X("BD"), scale=6144.0)
     act(X("NBL"), X("BLK"), scale=-2.0 ** 30)
     for t in range(2):
         for d in range(4):
@@ -333,39 +416,40 @@ def rank_program(g, core, T, topo):
         ts(X("TL", 256 + 512 * h, 768 + 512 * h), X("TLI", 512 * h, 512 * h + 512), -1.0, A.mult, 4096.0, A.add)
     for h in range(8):
         o = X("TAB", 2304 + 512 * h, 2816 + 512 * h)
-        if PLAN["NEG"][h] == "s":
-            act(o, o, F.Identity, bias=255.0, scale=-1.0)
-        else:
-            ts(o, o, -1.0, A.mult, 255.0, A.add)
+        lin(PLAN["NEG"][h], o, o, -1.0, 255.0)
     for t in range(4):
-        send("pre%d" % t, "SM%d" % t, 256 * rank, "FR", lambda p: 256 * t + 48 * p)
         act(X("SM%d" % t, 256 * rank, 256 * rank + 48), X("FR", 256 * t + 48 * rank, 256 * t + 48 * rank + 48))
         act(X("M", 256 * t + 448, 256 * t + 512), X("FR", 256 * t + 192, 256 * t + 256))
+        if t < 3:
+            act(X("MR", 64 * t, 64 * t + 64), X("FR", 256 * t + 192, 256 * t + 256))
 
-    def candidates(t, c0, c1):
-        n, li, lf = c1 - c0, 64 * t, 48 * t
-        src = X("M", 256 * t + 16 * c0, 256 * t + 16 * c1)
-        lists(X("m2", 256, 256 + n), "WU", src, True, False)
-        lists(X("m2", 256 + n, 256 + 2 * n), "WV", src, False, True)
-        uv, u, v = X("LI", li + 2 * c0, li + 2 * c1), X("LI", li + 2 * c0, li + c0 + c1), X("LI", li + c0 + c1, li + 2 * c1)
+    def candidates(t, c0, c1, name="M"):
+        n, li = c1 - c0, 64 * t
+        src = X("M", 256 * t + 16 * c0, 256 * t + 16 * c1) if name == "M" else X(name)
+        for h in range(8):
+            mm(X("m2", 256 + 4 * n * (h // 4), 256 + 4 * n * (h // 4 + 1)), blk("W4", h), X(src[0], src[1] + h % 4, src[2], 4), h == 0, h == 7)
+        uv, u, v = X("LI", li + c0, li + c1 + n), X("LI", li + c0, li + c1), X("LI", li + c1, li + c1 + n)
         a = X("LI", li + 32 + c0, li + 32 + c1)
-        ts(uv, X("m2", 256, 256 + 2 * n), -1.0, A.mult)
+        tt(X("U4", 0, 8 * n), X("m2", 256, 256 + 8 * n), X("OWN", 0, 8 * n), A.mult)
+        tt(X("U2", 0, 4 * n), X("U4", 0, 8 * n, 2), X("U4", 1, 8 * n, 2), A.add)
+        tt(uv, X("U2", 0, 4 * n, 2), X("U2", 1, 4 * n, 2), A.add)
         ts(uv, uv, 4095, A.bitwise_and)
         tt(a, u, v, A.mult)
-        cp(X("LF", lf + c0, lf + c1), u)
         ts(a, a, 5, A.arith_shift_right, 2047, A.bitwise_and)
-        cp(X("LF", lf + 16 + c0, lf + 16 + c1), a)
-        for q in [q for q in PLAN["Q"] if c0 <= 4 * q < c1]:
-            o = 256 * t + 128 * (q // 2)
-            for c in range(4 * q, 4 * q + 4):
-                ts(X("CT", o + 2 * (c % 4) + q % 2, o + 128, 8), X("KJ"), X("LF", lf + c, lf + c + 1), A.mult, X("LF", lf + 16 + c, lf + 17 + c), A.add)
-            ct = X("CT", o + q % 2, o + 128, 2)
-            ts(ct, ct, 2047, A.bitwise_and)
-            cp(X("LST", 256 * t + 64 * q, 256 * t + 64 * q + 64), ct)
-            o = 2048 * (t % 2) + 512 * q
-            act(X("MD", o, o + 64), X("M", 256 * t + 64 * q, 256 * t + 64 * q + 64))
-            for w in (64, 128, 256)[:4 - len(PLAN["L" if t else "L0"][q]) // 2]:
-                act(X("MD", o + w, o + 2 * w), X("MD", o, o + w))
+        ct, each = X("CT", 256 * t + 16 * c0, 256 * t + 16 * c1), X("LC", 16 + c0, 16 + c1)
+        tt(X("KU", 0, 16 * n), IX(X("LI", li, li + c1), each), X("KJ", 0, 16 * n), A.mult)
+        tt(ct, IX(X("LI", li + 32, li + 32 + c1), each), X("KU", 0, 16 * n), A.add)
+        ts(ct, ct, 2047, A.bitwise_and)
+        cp(X("LST", *ct[1:3]), ct)
+        for q in [3] if t == 4 else [q for q in PLAN["Q"] if c0 <= 4 * q < c1]:
+            if "v" in PLAN["L" if t else "L0"][q]:
+                repeat(1 if t == 4 else t, q)
+
+    def repeat(t, q):
+        o = 2048 * (t % 2) + 512 * q
+        act(X("MD", o, o + 64), X("M", 256 * t + 64 * q, 256 * t + 64 * q + 64))
+        for w in (64, 128, 256)[:4 - len(PLAN["L" if t else "L0"][q]) // 2]:
+            act(X("MD", o + w, o + 2 * w), X("MD", o, o + w))
 
     pp = [0]
 
@@ -380,7 +464,8 @@ def rank_program(g, core, T, topo):
         if not second:
             mm(X(b, 0, 128), X("IDN"), X("JC"), True, False)
         for u in range(len(who)):
-            off = X("LST", 256 * t + 64 * q + n // 16 * u, 256 * t + 64 * q + n // 16 * (u + 1))
+            at = 960 + 64 * t if t and q == 3 else 256 * t + 64 * q
+            off = X("LST", at + n // 16 * u, at + n // 16 * (u + 1))
             o = (1024 * q + n * u, 1024 * q + n * (u + 1))
             if who[u] == "v":
                 tt(X("FL", *o), IX(LM, off), md, A.is_gt)
@@ -388,85 +473,96 @@ def rank_program(g, core, T, topo):
                 d = X(dbank(), 0, n)
                 act(X("X", *o), IX(LM, off))
                 mm(d, X("IDN"), X("X", *o), True, False)
-                mm(d, X("IDM"), md, False, True)
+                for h in range(0, n, 64):
+                    mm(X(d[0], h, h + 64), X("IDM"), X("M", 256 * t + 64 * q, 256 * t + 64 * q + 64), False, h + 64 == n)
                 act(X("FL", *o), d, F.Sign, bias=-0.5)
-                mm(X(b, q % 2 + n // 8 * u, n // 8 * (u + 1), 2), X("IDN"), X("C20", 0, n // 16), False, False)
-        lists(X(b, q % 2, 128, 2), "VN", X("FL", 1024 * q, 1024 * q + 1024), False, second)
+                mm(X(b, 64 * (q % 2) + n // 16 * u, 64 * (q % 2) + n // 16 * (u + 1)), X("IDN"), X("C20", 0, n // 16), False, False)
+        lists(X(b, 64 * (q % 2), 64 * (q % 2) + 64), "VN", X("FL", 1024 * q, 1024 * q + 1024), False, second)
         if second:
-            s, c0 = 128 * k, 8 * k
-            tt(X("SC", s, s + 128), X(b, 0, 128), X("CT", 256 * t + s, 256 * t + s + 128), A.add)
-            for h in (64, 32, 16):
-                tt(X("SC", s, s + h), X("SC", s, s + h), X("SC", s + h, s + 2 * h), A.max)
-            for h in range(2):
-                tt(X("SCM", c0 + 4 * h, c0 + 4 * h + 4), X("SC", s + h, s + 8, 2), X("SC", s + 8 + h, s + 16, 2), A.max)
-            ts(X("GI", c0, c0 + 8), X("SCM", c0, c0 + 8), 2047, A.bitwise_and)
-            cp(X("GL", c0, c0 + 8), X("GI", c0, c0 + 8))
+            o, gi = (128 * k, 128 * k + 128), X("GI", 8 * k, 8 * k + 8)
+            tt(X("SC", *o), X(b, 0, 128), X("CT", 256 * t + o[0], 256 * t + o[1]), A.add)
+            lin(PLAN["F"][0][0], X("SP", *o), IX(X("SC", *o), X("LC", 0, 8)))
+            scan(X("SX", *o), X("SEN"), X("SP", *o), 0.0, A.add, A.max)
+            cp(gi, X("SX", o[0] + 15, o[1], 16))
+            ts(gi, gi, 2047, A.bitwise_and)
+            cp(X("GL", 8 * k, 8 * k + 8), gi)
 
     def products(t, k):
         c0, c1 = BLOCKS[k]
         n, b, s, gl = 16 * (c1 - c0), "b%d" % k, 16 * c0, X("GL", c0, c1)
         if t:
-            ts(X("TG", s, s + n), IX(TLW, gl), -1.0, A.mult, 4096.0, A.add)
+            ts(X("TG", s, s + n), IX(TLW, gl), -1.0, A.mult, 4096.25, A.add)
         else:
             cp(X("TG", s, s + n), IX(X("TLI"), gl))
-        act(X("LG", s, s + n), IX(LM, gl))
+        lin(PLAN["F"][0][1], X("LG", s, s + n), IX(LM, gl))
         mm(X(b, 0, 128, 1, n), X("M", 256 * t + s, 256 * t + s + n), X("IDN"), True, False)
-        mm(X(b, 0, 128, 1, n), X("LG", s, s + n), X("IDM"), False, True)
+        mm(X(b, 0, 128, 1, n), X("LG", s, s + n), X("IDM"), False, PLAN["NG"][k] == "v")
+        if PLAN["NG"][k] == "s":
+            mm(X(b, 128, 256), X("IDN"), X("LG", s, s + n), False, False)
+            mm(X(b, 128, 256), X("IDM"), X("M", 256 * t + s, 256 * t + s + n), False, True)
         qt = X("QT", 128 * k, 128 * k + 128, 1, n)
-        act(qt, X(b, 0, 128, 1, n), F.Identity, bias=-255.0)
-        mm(X(b, 0, n), X("WBU"), X("C255", 0, n), True, False)
-        mm(X(b, n, 2 * n), X("WBV"), X("C255", 0, n), False, False)
-        run = 2 if n % 64 == 0 else n // 32
+        lin(PLAN["F"][0][2], qt, X(b, 0, 128, 1, n), 1.0, -255.0)
+        if PLAN["NG"][k] == "s":
+            act(X("NG", s, s + n), X(b, 128, 256), F.Relu)
+        else:
+            tt(X("NG", s, s + n), X("LG", s, s + n), X("M", 256 * t + s, 256 * t + s + n), A.is_gt)
+        mm(X(b, 0, 256), X("C255"), X("WB"), True, False)
+        mm(X(b, 0, 256), X("IDN"), X("C19"), False, False)
         for u in range(n // 32):
             l0 = s + 32 * u
             o, src = (16 * l0, 16 * l0 + 512), IX(X("MO"), X("TG", l0, l0 + 32))
             d = X(dbank())
-            if PLAN["PG"][k][u] == "v":
-                cp(X("X", *o), src)
-            else:
-                act(X("X", *o), src)
+            who = PLAN["PG"][k]
+            if PLAN["TWO"] and u % 2 == 0 and who[u] == who[u + 1] != "x":
+                lin(who[u], X("X", o[0], o[1] + 512), IX(X("MO"), X("TG", l0, l0 + 64)))
+            elif not (PLAN["TWO"] and u % 2 and who[u] == who[u - 1] != "x"):
+                lin(who[u], X("X", *o), src)
             mm(d, X("IDN"), X("X", *o), True, False)
             mm(d, qt, X("EX", 512 * u, 512 * u + 512, 1, n), False, True)
-            if PLAN["PP"][k][u] == "v":
-                ts(X("R", *o), d, -1.0, A.mult, 0.0, A.max)
-            else:
-                act(X("R", *o), d, F.Relu, scale=-1.0)
-            if u % run == run - 1:
-                a = 32 * (u + 1 - run)
-                for h, w in ((0, "WU"), (n, "WV")):
-                    for i in range(16):
-                        mm(X(b, h + a, h + 32 * u + 32), blk(w, i), X("R", 16 * (s + a) + i, o[1], 16), False, bool(h and i == 15 and 32 * u + 32 == n))
+            lin(PLAN["PP"][k][u], X("R", *o), d, -1.0, 0.0, True)
+        for i in range(16):
+            mm(X(b, i, 256, 16), X("R", 16 * s + i, 16 * (s + n), 16), X("W2"), False, i == 15)
         ui, hp = X("UI", 2 * s, 2 * s + 2 * n), X("HP", s, s + n)
-        cp(ui, X(b, 0, 2 * n))
-        ts(ui, ui, 4095, A.bitwise_and)
+        if PLAN["MOD"][k] == "s":
+            lin(PLAN["F"][0][4], X("UF", 2 * s, 2 * s + 2 * n), X(b, 0, 2 * n), 1.0, -2047.5)
+            tt(ui, X(b, 0, 2 * n), X("UF", 2 * s, 2 * s + 2 * n), A.subtract)
+        else:
+            cp(ui, X(b, 0, 2 * n))
+            ts(ui, ui, 4095, A.bitwise_and)
         tt(X("PRD", s, s + n), X("UI", 2 * s, 2 * s + n), X("UI", 2 * s + n, 2 * s + 2 * n), A.mult)
-        ts(hp, X("PRD", s, s + n), 5, A.arith_shift_right)
-        tt(hp, hp, X(b, 0, n), A.add)
-        ts(X("HI", s, s + n), hp, 4095, A.bitwise_and)
-        cp(X("HL", s, s + n), X("HI", s, s + n))
-        ts(X("D3", s, s + n), hp, 3, A.bitwise_and)
-        tt(X("NG", s, s + n), X("LG", s, s + n), X("M", 256 * t + s, 256 * t + s + n), A.is_gt)
+        ts(hp, X("PRD", s, s + n), 5, A.arith_shift_right, 4095, A.bitwise_and)
+        tt(X("HY", s, s + n), hp, X(b, 0, n), A.add)
+        lin(PLAN["F"][0][3], X("HF", s, s + n), X("HY", s, s + n), 1.0, -2047.5)
+        h = X(b, 256, 384)
+        mm(h, X("HY", s, s + n), X("IDF"), True, False)
+        mm(h, X("HF", s, s + n), X("IDM"), False, True)
+        cp(X("HL", s, s + n), h)
+        cp(X("HI", s, s + n), h)
+        ts(X("D3", s, s + n), X("HI", s, s + n), 3, A.bitwise_and)
 
     def seen(t, k):
         c0, c1 = BLOCKS[k]
         n, b, s = 16 * (c1 - c0), "b%d" % k, 16 * c0
-        run = 2 if n % 64 == 0 else n // 32
+        w = n // len(PLAN["S"][k])
         mm(X(b, 0, n), X("NBL"), X("NG", s, s + n), True, False)
-        for u in range(n // 32):
-            l0 = s + 32 * u
-            o, src = (16 * l0, 16 * l0 + 512), IX(SNW, X("HL", l0, l0 + 32))
-            if PLAN["S"][k][u] == "v":
+        for u in range(n // w):
+            l0 = s + w * u
+            o, src = (16 * l0, 16 * (l0 + w)), IX(SNW, X("HL", l0, l0 + w))
+            if PLAN["TWO"] and PLAN["S"][k][u - u % 2:u - u % 2 + 2] == "vv":
+                if u % 2 == 0:
+                    tt(X("FL", o[0], o[1] + 16 * w), IX(SNW, X("HL", l0, l0 + 2 * w)), X("R", o[0], o[1] + 16 * w), A.not_equal)
+            elif PLAN["S"][k][u] == "v":
                 tt(X("FL", *o), src, X("R", *o), A.not_equal)
             else:
-                d = X(dbank())
+                d = X(dbank(), 0, 16 * w)
                 act(X("X", *o), src)
                 mm(d, X("IDN"), X("X", *o), True, False)
                 mm(d, X("IDM"), X("R", *o), False, True)
                 act(X("FL", *o), d, F.Square)
-            if u % run == run - 1:
-                a = 32 * (u + 1 - run)
+            if w * (u + 1) % 64 == 0:
+                a = w * (u + 1) - 64
                 for i in range(16):
-                    mm(X(b, a, 32 * u + 32), blk("CUM", i), X("FL", 16 * (s + a) + i, o[1], 16), False, i == 15 and 32 * u + 32 == n)
+                    mm(X(b, a, a + 64), blk("CUM", i), X("FL", 16 * (s + a) + i, o[1], 16), False, i == 15 and a + 64 == n)
         o = (s, s + n)
         ts(X("ZB", *o), X(b, 0, n), 0.0, A.is_gt)
         mm(X("m1", *o), X("BD"), X("ZB", *o), True, True)
@@ -474,107 +570,125 @@ def rank_program(g, core, T, topo):
         tt(X("TD", *o), X("m1", *o), X("D3", *o), A.mult)
         mm(X("m2", *o), X("BLK"), X("TD", *o), False, True)
 
+
+    def children(t):
+        lists(X("b0", 0, 16), "VN", X("ZB"))
+        tt(X("PLF"), X("B2"), X("b0", 0, 16), A.add)
+        ts(X("PL"), X("PLF"), 2.0 ** -16, A.mult)
+        act(X("PCB"), IX(X("R", 0, 4352 + 256 * t), X("PL")), F.Identity, bias=255.0, scale=-1.0)
+        ts(X("E"), X("m2", 0, 256), ecol, A.is_equal)
+        scan(X("CS"), X("E"), X("CAPC"), ini, A.add, A.min)
+        tt(X("SL"), X("CS"), X("E"), A.mult)
+        lists(X("b1", 0, 16), "VN", X("SL"))
+        ts(X("SLOT"), X("b1", 0, 16), -2.0 ** -16, A.mult, -1.0, A.add)
+        cp(IX(X("SM%d" % t), X("SLOT")), X("PCB"))
+
     def keys(t):
         ka = X("LI", 64 * t + 48, 64 * t + 64)
-        ts(X("HASB"), X("SCM"), 2048.0, A.is_ge, 8192.0, A.mult)
-        for q in range(4):
-            o = 256 * t + 128 * (q // 2)
-            tt(X("K1", 4 * q, 4 * q + 4), X("CT", o + q % 2, o + 8, 2), X("HASB", 4 * q, 4 * q + 4), A.subtract)
+        ts(X("HASB"), X("SX", 15, 256, 16), 2048.0, A.is_ge, 2.0 ** 29, A.mult)
+        tt(X("K1"), IX(X("CT", 256 * t, 256 * t + 256), X("LC", 8, 9)), X("HASB"), A.subtract)
         ts(ka, X("K1"), 256.0, A.add, 0.0, A.max)
         both = X("LI", 64 * t + 32, 64 * t + 64)
         ts(X("KP", 0, 32), both, 8160, A.bitwise_and)
         ts(X("KP", 32, 64), both, 31, A.bitwise_and)
-        cp(X("KPB"), X("KP"))
+        tt(X("KPB"), X("KP"), X("SGN"), A.mult)
         for h in range(2):
             for r in range(16):
-                mm(X("m0", r, 512, 16), blk("SEL", r), X("KPB", 32 * h, 32 * h + 32), h + r == 0, h + r == 16 and t == 3)
-        tt(X("B2"), X("L4"), X("HASB"), A.subtract)
+                mm(X("m0", r, 512, 16), blk("SEL", r), X("KPB", 32 * h, 32 * h + 32), h + r == 0 and t == 3, h + r == 16 and t == 3)
+        tt(X("B2"), X("L4", 16 * t, 16 * t + 16), X("HASB"), A.subtract)
         tt(X("B2"), X("B2"), X("BASE"), A.max)
 
     def winners(kb, kf):
-        first = PLAN["EQ"]
-        cp(X("KR"), X(kb, 256, 512))
+        first = PLAN["EQ" if kf[3] > 1 else "EQ3"]
         if first < 16:
+            act(X("KRF", 16 * first, 256), X(kb, 256 + 16 * first, 512))
             act(X("NKF"), kf, scale=-1.0)
+        if first:
+            cp(X("KR"), X(kb, 256, 512))
         at = 0
         for c in range(first, 16):
             n = 256 - 16 * c
-            act(X("EQT", at, at + n), X(kb, 256 + 16 * c, 512), F.Abs, bias=X("NKF", c, c + 1))
+            act(X("EQT", at, at + n), X("KRF", 16 * c, 256), F.Abs, bias=X("NKF", c, c + 1))
             act(X("EQ", 272 * c, 256 * c + 256), X("EQT", at, at + n), F.Relu, bias=1.0, scale=-1.0)
             at += n
-        for c in range(16):
+        mm(X("d0", 16, 256), X("IDN"), X("C12", 272, 512), True, False)
+        turn = list(range(first, 15)) + list(range(min(first, 15)))
+        for c in turn + [15] * (first == 16):
             if c < first:
                 ts(X("EQ", 272 * c, 256 * c + 256), X("KR", 16 * c, 256), X(kf[0], kf[1] + c * kf[3], kf[1] + c * kf[3] + 1), A.is_equal)
             if c < 15:
-                mm(X("d0", 16 * c + 16, 256), X("BLK"), X("EQ", 272 * c + 16, 256 * c + 256), c == 0, c == 14)
-        act(X("DUPS", 16, 256), X("d0", 16, 256), scale=-65536.0)
+                mm(X("d0", 16 * c + 16, 256), X("BLK"), X("EQ", 272 * c + 16, 256 * c + 256), False, c == turn[-1])
+        act(X("DUPS", 16, 256), X("d0", 16, 256))
+        last["dups"] = [len(rec) - 1]
+        mm(X("d1", 0, 16), X("IDF"), kf, True, False)
         for r in range(16):
-            mm(X("d1", 0, 16), blk("TRI", r), X("EQ", r, 4096, 272), r == 0, False)
-        lists(X("d1", 1, 16), "MS", X("DUPS", 16, 256), False, True)
-        tt(X("XK"), X("d1", 0, 16), kf, A.add)
+            mm(X("d1", 0, 16), blk("TRI", r), X("EQ", r, 4096, 272), False, False)
+        lists(X("d1", 1, 16), "VN", X("DUPS", 16, 256), False, True)
+        tt(X("X2"), X("d1", 0, 16), X("LANE"), A.max)
+        cp(X("LLA"), X("X2"))
 
     candidates(0, 0, 16)
     for t in range(4):
         m, nx = X("M", 256 * t, 256 * t + 256), 256 * t + 256
-        act(X("R", 4096, 4352), m)
-        for step in PLAN["ORDER"].split():
-            if step[0] in "LPS":
-                {"L": leaders, "P": products, "S": seen}[step[0]](t, int(step[1]))
-            elif step == "K":
-                keys(t)
-            elif step == "C" and t < 3:
-                candidates(t + 1, 12, 16)
-            elif step == "W" and t == 3:
-                cp(X("KF"), X("LI", 64 * t + 48, 64 * t + 64))
-                winners("m0", X("KF"))
-                tt(X("X2"), X("XK"), X("LANE"), A.max)
-                cp(X("LLA"), X("X2"))
-                cp(IX(X("TAB", 0, 2304), X("LLA")), m)
-                store("y", "dyl", T.yl[:], LM)
         if t < 3:
             n = 192 if t else 0
             if n:
                 tt(X("MT", 0, n), X("LT", 192 * t - 192, 192 * t), X("TL", 256, 256 + n), A.max)
                 act(X("TA", 0, n), X("MT", 0, n), F.Abs, bias=-4096.0)
-            act(X("TA", n, 256), X("TL", 256 + n, 512), F.Identity, bias=4096.0, scale=not0)
-            act(X("TB"), X("TA"), F.Identity, bias=4096.0, scale=-1.0)
+                act(X("TB", 0, n), X("TA", 0, n), F.Relu, bias=4096.0, scale=-1.0)
+            act(X("TB", n, 256), X("TL", 256 + n, 512), scale=not0)
+            mm(X("m0"), X("IDN"), X("C12"), True, False)
+            mm(X("m0", 0, 256), X("NDF"), X("TB"), False, False)
+        for step in PLAN["ORDER"].split():
+            if step[0] in "LPS":
+                {"L": leaders, "P": products, "S": seen}[step[0]](t, int(step[1]))
+            elif step == "K":
+                keys(t)
+            elif step == "C" and t == 0:
+                candidates(4, 0, 12, "MR")
+                for u in range(1, 4):
+                    cp(X("CT", 256 * u + 192, 256 * u + 256), X("CT", 960 + 64 * u, 1024 + 64 * u))
+                    cp(X("LI", 64 * u + 44, 64 * u + 48), X("LI", 284 + 4 * u, 288 + 4 * u))
+            elif step == "C" and t < 3 and "v" in PLAN["L"][3]:
+                repeat(t + 1, 3)
+            elif step == "W" and t == 3:
+                cp(X("KF"), X("LI", 64 * t + 48, 64 * t + 64))
+                winners("m0", X("KF"))
         if t < 2:
             act(X("TGF"), IX(TLW, X("GL")), F.Identity, bias=8192.0, scale=-1.0)
         mask = X("m1", 0, 256)
-        lists(X("b0", 0, 16), "MS", X("ZB"))
-        tt(X("PLF"), X("B2"), X("b0", 0, 16), A.subtract)
-        cp(X("PL"), X("PLF"))
-        act(X("PCB"), IX(X("R"), X("PL")), F.Identity, bias=255.0, scale=-1.0)
-        ts(X("E"), X("m2", 0, 256), ecol, A.is_equal)
-        call("v", g.vector.tensor_tensor_scan, X("CS"), [X("E"), X("CAPC"), ini, A.add, A.min], us(X("CS"), [X("E")]))
-        tt(X("SL"), X("CS"), X("E"), A.mult)
-        lists(X("b1", 0, 16), "MS", X("SL"))
-        ts(X("SLOT"), X("b1", 0, 16), -1.0, A.add)
+        children(t)
+        if t == 3:
+            gate["v"] = [len(rec) - 1]
+            cp(IX(X("TAB", 0, 2304), X("LLA")), m)
+            store("y", "dyl", T.yl[:], LM)
         sm = "SM%d" % t
-        cp(IX(X(sm), X("SLOT")), X("PCB"))
         send("fm%d" % (t + 1), "M", nx + 48 * rank, sm, lambda p: 256 * p)
         act(X("M", nx + 48 * rank, nx + 48 * rank + 48), X(sm, 256 * rank, 256 * rank + 48))
-        if t < 2:
+        if t < 2 and PLAN["ST"] == "v":
             act(X("MSK"), mask, scale=8192.0)
+        elif t < 2:
+            mm(X("b0", 256, 512), X("IDF"), X("TGF"), True, False)
+            mm(X("b0", 256, 512), X("BD6"), X("ZB"), False, True)
+            act(X("MSK"), X("b0", 256, 512))
         if t < 3:
             tt(X("TH"), mask, X("HI"), A.mult)
             mm(X("m0", 256, 512), X("ZK"), X("ZB"), False, False)
             mm(X("m0", 256, 512), X("BLF"), X("TH"), False, True)
             tt(X("KD"), X("m0", 256, 512), X("DIAG"), A.mult)
-            call("v", g.vector.tensor_tensor_scan, X("KS"), [X("SEG"), X("KD"), 0.0, A.mult, A.add], us(X("KS"), [X("KD")]))
-            act(X("VAL"), IX(X("R"), X("PL")))
+            scan(X("KS"), X("SEG"), X("KD"), 0.0, A.mult, A.add)
+            act(X("VAL"), X("PCB"), F.Identity, bias=255.0, scale=-1.0)
             winners("m0", X("KS", 15, 256, 16))
-            tt(X("TY"), X("TA"), X("m0", 0, 256), A.subtract)
-            tt(X("X2"), X("XK"), X("LANE"), A.max)
-            cp(X("LLA"), X("X2"))
+            tt(X("TY"), X("m0", 0, 256), X("TB"), A.max)
             cp(IX(X("TAB"), X("LLA")), X("VAL"))
-            tt(X("X2"), X("XK"), X("HASB"), A.subtract)
-            tt(X("X2"), X("X2"), X("LANE"), A.max)
-            cp(X("LLB"), X("X2"))
-            tt(IX(X("TL"), X("LLB")), X("TB"), X("TY"), A.max)
+            act(IX(X("TL"), X("LLA")), X("TY"), F.Silu)
         if t < 2:
             st = "ST%d" % t
-            tt(IX(X(st), X("SLOT")), X("MSK"), X("TGF"), A.max)
+            if PLAN["ST"] == "v":
+                tt(IX(X(st), X("SLOT")), X("MSK"), X("TGF"), A.max)
+            else:
+                gate["s"] = last["dups"] * PLAN["GATE"]
+                act(IX(X(st), X("SLOT")), X("MSK"), F.Silu)
             send("ft%d" % (t + 1), "LT", 192 * t + 48 * rank, st, lambda p: 256 * p)
             act(X("LT", 192 * t + 48 * rank, 192 * t + 48 * rank + 48), X(st, 256 * rank, 256 * rank + 48))
         if t < 3:

import numpy as np
from concourse.bass import DstId, RemoteDMATransfer
from concourse.mybir import AluOpType as A, ActivationFunctionType as F

BF, FP, I32, U16 = "bfloat16", "float32", "int32", "uint16"
BLOCKS = [(0, 8), (8, 16)]
PLAN = {"L": ["ss", "vvsv", "vvvv", "ssss"], "L0": ["sv", "vvss", "vv", "vsss"], "PG": ["vxxx", "xvxx"], "PP": ["svss", "ssxv"],
        "S": ["vvsv", "sssvvsvv"], "NEG": "xxxxxxxx", "EQ": 9, "EQ3": 4, "MOD": "ss", "NG": ["s", "v"], "F": ["sssxs"], "ST": "s", "GATE": 1, "TWO": 0,
        "Q": [3, 2, 0, 1], "ORDER": "L3 L2 L0 L1 P1 P0 S1 C S0 K W", "D": ["d0", "d1", "b2"]}
SIZES = {
    BF: {"TAB": 6400, "MO": 2048, "FR": 1024, "MD": 4096, "ONES": 512, "BLK": 128, "IDN": 128, "IDM": 128, "Z": 128, "Z4C": 128, "OWN": 128, "W4": 1024, "SEN": 128, "DK": 256, "SGN": 64, "C12": 512, "BD6": 128, "C21": 128, "C19": 256, "UF": 512,
         "WB": 256, "MR": 192, "EQT": 2176, "W2": 16, "HF": 256, "BD": 128, "Z4": 128, "ZK": 128, "NBL": 128, "C255": 128, "C20": 32, "JC": 128, "VN": 2048,
         "SEL": 2048, "TRI": 2048, "CUM": 2048, "EX": 2048, "X": 4096, "FL": 4096, "R": 5376, "LG": 256, "QT": 256, "NG": 256, "ZB": 256,
         "TD": 256, "DIAG": 256, "SEG": 256, "E": 256, "CS": 256, "SL": 256, "CAPC": 256, "PCB": 256, "VAL": 256, "KPB": 64, "EQ": 4096, "DUPS": 256,
         "SM0": 1280, "SM1": 1280, "SM2": 1280, "SM3": 1280},
    FP: {"TL": 6400, "PF": 12, "WF": 4, "WN": 4, "KJ": 256, "KU": 256, "LF": 32, "IDF": 128, "HY": 256, "U4": 128, "U2": 64, "NDF": 128, "SC": 256, "SP": 256, "SX": 256, "LANE": 16, "BASE": 16, "L4": 64, "HASB": 16, "B2": 16, "PLF": 16,
         "K1": 16, "KF": 16, "NKF": 16, "XK": 16, "X2": 16, "LT": 384, "MT": 256, "TA": 256, "TB": 256, "TY": 256, "TGF": 256,
         "MSK": 256, "KRF": 256, "TH": 256, "KD": 256, "KS": 256, "BLF": 128, "ST0": 1280, "ST1": 1280},
    I32: {"TLI": 2048, "WKI": 3, "CI": 128, "CM": 128, "CG": 128, "PI": 8, "LI": 320, "CT": 1216, "GI": 16, "KP": 64,
          "UI": 512, "PRD": 256, "HP": 256, "HI": 256, "D3": 256},
    U16: {"LST": 1216, "TG": 256, "HL": 256, "KR": 256, "GL": 16, "PL": 16, "SLOT": 16, "LLA": 16, "LC": 32},
}
SCRATCH, WIDTH, DTYPE, SMALL = {}, {}, {}, {}
for _d in SIZES:
    _p = "small_" + _d
    WIDTH[_p], DTYPE[_p] = 0, _d
    for _n, _w in SIZES[_d].items():
        if _w <= 128:
            SMALL[_n] = (_p, WIDTH[_p], _w)
            WIDTH[_p] += -(-_w // 16) * 16
        else:
            WIDTH[_n], DTYPE[_n] = _w, _d
SMALL["M"] = ("R", 4096, 1280)
for _n in WIDTH:
    SCRATCH[_n] = ("sbuf", [128, WIDTH[_n]], DTYPE[_n])
BANKS = ["b0", "b1", "b2", "d0", "d1", "m0", "m1", "m2"]
for _b in BANKS:
    SCRATCH[_b] = ("psum", [128, 512], FP)
    WIDTH[_b], DTYPE[_b] = 512, FP
_DMAS = ["wk", "fm", "fr", "lm", "tl", "mo", "sn", "yl", "yf"]
SEMAPHORES = (["sv", "ss", "st", "sg", "loc"] + ["d" + x for x in _DMAS]
              + ["pre%d" % t for t in range(4)] + ["fm%d" % t for t in range(1, 5)] + ["ft%d" % t for t in range(1, 3)])
CYC, FIX, PEC, WAKE, HOP, SLACK, PASSES, SHAKE, LOAD, OWN = 0.00094, 0.0, 0.00048, 0.15, 2.5, 0.35, 3, 0.5, 0.0006, 1.0

TRIES, PLANNED, CROSS, FIRST = 0, {}, 0.15, 10.0


def X(name, a=0, b=None, s=1, p=None):
    if name in SMALL:
        name, at, w = SMALL[name]
        return (name, at + a, at + (w if b is None else b), s, p)
    return (name, a, WIDTH[name] if b is None else b, s, p)


def IX(win, off):
    return ("*", win, off)


def cols(x):
    return 16 * cols(x[2]) if x[0] == "*" else len(range(x[1], x[2], x[3]))


def rank_program(g, core, T, topo):
    rank = T.rank_of(core)
    if rank is None:
        return
    peers = [r for r in range(len(T.cores)) if r != rank]
    S = T.sem
    Q = {"v": g.vector, "s": g.scalar, "t": g.tensor, "g": g, "y": g.sync}
    SN = {"v": "sv", "s": "ss", "t": "st", "g": "sg"}

    def ap(x):
        if not isinstance(x, tuple):
            return x
        if x[0] == "*":
            return ap(x[1]).indirect(ap(x[2]))
        rows = slice(None) if x[4] is None else slice(0, x[4])
        return T[x[0]][rows, x[1]:x[2]] if x[3] == 1 else T[x[0]][rows, x[1]:x[2]:x[3]]

    rec = []
    writer = {n: np.full(WIDTH[n], -1) for n in WIDTH}
    readers = {n: [] for n in WIDTH}
    bank = {}
    gate = {}

    def add(e, sem, inc, rd, wr, cost, late, call, follow=()):
        n, before, order = len(rec), set(), set(follow) | set(gate.pop(e, ()))
        rd = [y for x in rd if isinstance(x, tuple) for y in (x[1:] if x[0] == "*" else [x])] + [x[2] for x in wr if x[0] == "*"]
        wr = [x[1] if x[0] == "*" else x for x in wr]
        for x in rd + wr:
            if x[0] in BANKS:
                cur = bank.setdefault(x[0], [None, [], []])
                if cur[0] != e:
                    bank[x[0]] = cur = [e, [], cur[1]]
                before.update(cur[2])
                if e == "t":
                    order.update(cur[1][-1:])
                cur[1].append(n)
            else:
                before.update(np.unique(writer[x[0]][x[1]:x[2]:x[3]]).tolist())
        for x in wr:
            if x[0] not in BANKS:
                keep = []
                for i, mask in readers[x[0]]:
                    if mask[x[1]:x[2]:x[3]].any():
                        before.add(i)
                        mask[x[1]:x[2]:x[3]] = False
                    if mask.any():
                        keep.append((i, mask))
                readers[x[0]] = keep
                writer[x[0]][x[1]:x[2]:x[3]] = n
        for x in rd:
            if x[0] not in BANKS:
                mask = np.zeros(WIDTH[x[0]], bool)
                mask[x[1]:x[2]:x[3]] = True
                readers[x[0]].append((n, mask))
        before -= {n, -1}
        order.discard(n)
        rec.append([e, sem, inc, before, order, cost, late, call])
        return n

    def us(out, ins, two=False, first=0.063):
        if out[0] == "*":
            return first + 3.8 * CYC * cols(out)
        if ins and ins[0][0] == "*":
            return first + 1.56 * CYC * cols(out)
        r = 0.5 if all(DTYPE[x[0]] in (BF, U16) for x in [out] + ins) else 1.0
        if two and not any(x[0] in BANKS for x in ins):
            r *= 2
        return FIX + max(64, r * cols(out)) * CYC

    def call(e, f, out, args, cost, **kw):
        ins = [x for x in list(args) + list(kw.values()) if isinstance(x, tuple)]
        return add(e, SN[e], 1, ins, [out], cost, 0.0, lambda: f(ap(out), *[ap(x) for x in args], **{k: ap(kw[k]) for k in kw}))

    def cp(out, a):
        call("v", g.vector.tensor_copy, out, [a], us(out, [a]))

    def tt(out, a, b, op):
        call("v", g.vector.tensor_tensor, out, [a, b, op], us(out, [a, b], True))

    def ts(out, a, s1, op0, s2=None, op1=None):
        call("v", g.vector.tensor_scalar, out, [a, s1, s2, op0] + ([] if op1 is None else [op1]), us(out, [a]))

    def scan(out, a, b, first, op0, op1):
        call("v", g.vector.tensor_tensor_scan, out, [a, b, first, op0, op1], us(out, [a, b]))

    def fill(out, v):
        call("v", g.vector.memset, out, [v], us(out, []))

    def act(out, a, fn=F.Copy, **kw):
        call("s", g.scalar.activation, out, [a, fn], us(out, [a], first=0.081) if "*" in (a[0], out[0]) else FIX + max(64, cols(out)) * CYC, **kw)

    either = {}

    def lin(who, out, a, scale=1.0, bias=0.0, relu=False):
        ins = [x for x in (a, scale, bias) if isinstance(x, tuple)]
        plain = scale == 1.0 and bias == 0.0 and not relu
        fn = {"v": (lambda: g.vector.tensor_copy(ap(out), ap(a))) if plain else
              (lambda: g.vector.tensor_scalar(ap(out), ap(a), ap(scale), ap(bias), A.mult, A.max if relu else A.add)),
              "s": lambda: g.scalar.activation(ap(out), ap(a), F.Relu if relu else F.Identity, bias=ap(bias), scale=ap(scale))}
        cost = {"v": us(out, [a]), "s": us(out, [a], first=0.081) if a[0] == "*" else FIX + max(64, cols(out)) * CYC}
        if who != "x":
            return add(who, SN[who], 1, ins, [out], cost[who], 0.0, fn[who])
        either[len(rec)] = cost
        add("x%d" % len(rec), None, 1, ins, [out], cost["v"], 0.0, fn)

    def mm(out, lhsT, rhs, start, stop):
        call("t", g.tensor.matmul, out, [lhsT, rhs, start, stop], max(64, cols(rhs)) * PEC * (4 if DTYPE[rhs[0]] == FP else 1))

    def iota(out, pat, base, cm):
        kw = {} if DTYPE[out[0]] == I32 else {"allow_small_or_imprecise_dtypes": True}
        call("g", g.iota, out, [pat, base, cm], 0.15 + 2 * CYC * cols(out), **kw)

    def select(out, a, pat, op, base, cm, other=0.0):
        call("g", g.affine_select, out, [a, pat, op, other, base, cm], 0.2 + 2 * CYC * cols(out))

    loaded = [1.2]

    def load(e, sem, out, src):
        loaded[0] += 0.4 + cols(out) * (2 if DTYPE[out[0]] == BF else 4) * LOAD
        add(e, sem, 16, [], [out], 0.1, loaded[0], lambda: Q[e].dma_start(ap(out), src), follow=last[e])
        last[e] = [len(rec) - 1]

    def store(e, sem, dst, a):
        n = add(e, sem, 16, [a], [], 0.1, 0.0, lambda: Q[e].dma_start(dst, ap(a)))
        rec.append([None, None, 0, {n}, set(), 0.0, 0.0, None])
        rec[n][6] = 1.4 + cols(a) * 2 * LOAD

    lands, last = {}, {"send": [], "y": [], "s": []}

    def land(sem, name, at):
        lands[sem] = add(None, sem, 12, [], [X(name, at(p), at(p) + 48) for p in peers], 0.0, HOP + FIRST * (sem == "pre0"), None)

    def send(sem, dst, to, src, at):
        tr = []
        for n, p in enumerate(peers):
            rid, pid, _ = topo.addr(T.cores[p])
            eng = topo.engines(core, T.cores[p])
            tr.append(RemoteDMATransfer(dst_ids=[DstId(rid=rid, pnc=pid)], dma_engine_mask=sum(1 << x for x in eng[4 * n:4 * n + 4]),
                                        remote_sem=S[sem], src=ap(X(src, at(p), at(p) + 48)), dst=ap(X(dst, to, to + 48))))
        n = add("g", "loc", 12, [X(src, at(p), at(p) + 48) for p in peers], [], 0.3, 1.0, lambda: g.remote_dma_fused(tr, local_sem=S.loc), follow=last["send"])
        last["send"] = [n]
        rec[lands[sem]][4].add(n)

    def issue():
        n = len(rec)
        ahead, back = [[] for _ in rec], [[] for _ in rec]
        for k in range(n):
            for i in rec[k][3] | rec[k][4]:
                soft = i not in rec[k][3] or (rec[k][0] == "t" and rec[i][0] == "t")
                gap = 0.0 if soft else rec[i][6] + (WAKE if rec[i][0] == rec[k][0] else CROSS)
                ahead[i].append((k, gap))
                back[k].append((i, gap))

        def plan(nxt, prv, weight, fixed=None):
            left, can, end, order = [len(x) for x in prv], [0.0] * n, [0.0] * n, []
            ready, now = {e: [] for e in Q}, {e: 0.0 for e in Q}

            def done(i):
                for k, gap in nxt[i]:
                    left[k] -= 1
                    can[k] = max(can[k], end[i] + gap)
                    if not left[k]:
                        free(k)

            def free(k):
                if rec[k][0] is None:
                    end[k] = can[k]
                    done(k)
                else:
                    for e in [rec[k][0]] if k not in either else fixed[k] if fixed else "vs":
                        ready[e].append(k)
            for k in [i for i in range(n) if not left[i]]:
                free(k)
            while any(ready.values()):
                best = None
                for e in Q:
                    if ready[e]:
                        k = min(ready[e], key=lambda i: (max(now[e], can[i]), -weight[i]))
                        t0 = max(now[e], can[k]) + min(SLACK, 0.6 * rec[k][5])
                        k = max([i for i in ready[e] if can[i] <= t0], key=lambda i: weight[i] - (OWN if e == "v" and i in either else 0))
                        if best is None or max(now[e], can[k]) < best[0]:
                            best = (max(now[e], can[k]), e, k)
                st, e, i = best
                for q in "vs" if i in either and not fixed else [e]:
                    ready[q].remove(i)
                now[e] = end[i] = st + (either[i][e] if i in either else rec[i][5])
                order.append((i, e))
                done(i)
            return order, end
        def fits(order):
            at = {i: k for k, (i, _) in enumerate(order)}
            for i in range(n):
                if rec[i][0] is None:
                    at[i] = max([-1] + [at.get(d, n) for d, _ in back[i]])
            return len(at) == n and all(at[d] <= at[i] for i in range(n) for d, _ in back[i])
        if not PLANNED or not fits(PLANNED["best"][1]):
            order, end = plan(ahead, back, [-i for i in range(n)])
            best = None
            for k in range(PASSES):
                late = np.array(plan(back, ahead, end, dict(order))[1])
                order, end = plan(ahead, back, late.tolist())
                if best is None or max(end) < best[0]:
                    best = (max(end), order, late, np.array(end))
            shake = np.random.default_rng(0)
            for k in range(TRIES):
                at = shake.random() * best[0]
                late = best[2] + (np.abs(best[3] - at) < 3.0) * SHAKE * shake.random() * shake.standard_normal(n)
                order, end = plan(ahead, back, late.tolist())
                if max(end) <= best[0]:
                    best = (max(end), order, late, np.array(end))
            PLANNED.update(best=best)
        best = PLANNED["best"]
        cnt, known, snap, pos = {k: 0 for k in SEMAPHORES}, {e: {} for e in Q}, {}, {}
        for i in lands.values():
            cnt[rec[i][1]] += rec[i][2]
            pos[i] = (rec[i][1], rec[i][2])
        for i, e in best[1]:
            _, sem, inc, before, _, cost, late, fn = rec[i]
            if i in either:
                sem, fn = SN[e], fn[e]
            need = {}
            for d in before:
                if not (e == "t" and rec[d][0] == "t") and known[e].get(pos[d][0], 0) < pos[d][1]:
                    need[pos[d][0]] = max(need.get(pos[d][0], 0), pos[d][1])
            for s, v in need.items():
                if not any(s2 != s and snap.get((s2, need[s2]), {}).get(s, 0) >= v for s2 in need):
                    Q[e].wait_ge(S[s], v)
            for s, v in need.items():
                known[e][s] = max(known[e].get(s, 0), v)
                for a, b in snap.get((s, v), {}).items():
                    known[e][a] = max(known[e].get(a, 0), b)
            cnt[sem] += inc
            pos[i] = (sem, cnt[sem])
            ins = fn()
            if sem != "loc":
                ins.then_inc(S[sem], inc)
            snap[pos[i]] = dict(known[e])
        for s in SEMAPHORES:
            if cnt[s] and known["y"].get(s, 0) < cnt[s]:
                g.sync.wait_ge(S[s], cnt[s])

    def blk(name, r):
        return X(name, 128 * r, 128 * r + 128)

    def lists(out, w, src, start=True, stop=True):
        for r in range(16):
            mm(out, blk(w, r), X(src[0], src[1] + r, src[2], 16), start and r == 0, stop and r == 15)

    LM, SNW, TLW = X("TAB", 256, 2304), X("TAB", 2304, 6400), X("TL", 256, 2304)

    for t in range(4):
        land("pre%d" % t, "SM%d" % t, lambda p: 256 * p)
        land("fm%d" % (t + 1), "M", lambda p: 256 * t + 256 + 48 * p)
    for t in range(2):
        land("ft%d" % (t + 1), "LT", lambda p: 192 * t + 48 * p)
    load("y", "dwk", X("WKI"), T.wk[:])
    load("s", "dfm", X("M", 0, 256), T.fm[:])
    load("y", "dlm", LM, T.lm[:])
    load("y", "dtl", X("TLI"), T.tl[:])
    load("y", "dmo", X("MO"), T.mo[:])
    load("y", "dfr", X("FR"), T.fr[:])
    load("y", "dsn", SNW, T.sn[:])

    rp, gp, pf, ecol, ini, cap, row0, not0, g16, r4, x4, x15 = [X("PF", k, k + 1) for k in range(12)]
    iota(X("CI"), [[1, 128]], 0, 0)
    iota(X("PI", 0, 1), [[0, 1]], 0, 1)
    iota(X("JC"), [[0, 2], [-2048, 16], [0, 4]], 32768, 0)
    fill(X("ONES"), 1.0)
    for c, v in ((X("C19"), 129 * 4096), (X("C255"), 255), (X("C20"), -16 * 65536), (X("C12", 0, 256), 4096), (X("C12", 256, 512), 0)):
        iota(c, [[0, cols(c)]], v, 0)
    ts(X("CM"), X("CI"), 15, A.bitwise_and)
    ts(X("CG"), X("CI"), 4, A.arith_shift_right)
    ts(X("PI", 1, 2), X("PI", 0, 1), 15, A.bitwise_and)
    ts(X("PI", 2, 3), X("PI", 0, 1), 4, A.arith_shift_right)
    ts(X("PI", 3, 4), X("PI", 0, 1), 7, A.bitwise_and)
    cp(rp, X("PI", 1, 2))
    cp(gp, X("PI", 2, 3))
    cp(pf, X("PI", 0, 1))
    ts(X("BLK"), X("CG"), gp, A.is_equal)
    select(X("IDN"), X("ONES", 0, 128), [[-1, 128]], A.is_equal, 0, 1)
    act(X("IDM"), X("IDN"), scale=-1.0)
    cp(X("WF", 0, 3), X("WKI"))
    ts(X("WN", 0, 3), X("WKI"), -1.0, A.mult)
    ts(X("Z"), X("CM"), 99.0, A.add)
    tt(X("Z"), X("Z"), X("BLK"), A.mult)
    for r in range(16):
        ts(blk("VN", r), X("Z"), 99.0 + r, A.is_equal, -65536.0, A.mult)
    for h in range(2):
        ts(X("W2", 8 * h, 8 * h + 8), X("CI", 0, 8), gp, A.is_equal, X("WN", h, h + 1), A.mult)
    iota(X("Z4C"), [[0, 32], [1, 4]], 99, 0)
    tt(X("Z4C"), X("Z4C"), X("BLK"), A.mult)
    for h in range(8):
        ts(blk("W4", h), X("Z4C"), 99.0 + h % 4, A.is_equal, X("WF", h // 4, h // 4 + 1), A.mult)
    ts(X("PI", 5, 6), X("PI", 1, 2), 2, A.arith_shift_right)
    ts(g16, X("PI", 5, 6), 99.0, A.add)
    iota(X("OWN"), [[0, 32], [1, 4]], 99, 0)
    ts(X("OWN"), X("OWN"), g16, A.is_equal)
    iota(X("DK"), [[0, 4], [1, 16], [0, 4]], 0, 0)
    ts(X("DK"), X("DK"), rp, A.is_equal, X("WF", 2, 3), A.mult)
    mm(X("m1", 0, 256), X("BLK"), X("DK"), True, True)
    act(X("KJ"), X("m1", 0, 256))
    iota(X("LF", 0, 8), [[64, 2], [1, 4]], 0, 0)
    iota(X("LF", 16, 32), [[4, 4], [0, 4]], 0, 0)
    ts(X("PI", 4, 5), X("PI", 0, 1), 3, A.bitwise_and)
    cp(r4, X("PI", 4, 5))
    ts(x4, rp, 4.0, A.mult)
    ts(X("LC", 0, 8), X("LF", 0, 8), x4, A.add)
    ts(X("LC", 16, 32), X("LF", 16, 32), r4, A.add)
    ts(x15, r4, -15.0, A.mult)
    ts(X("LC", 8, 9), rp, 16.0, A.mult, x15, A.add)
    act(X("IDF"), X("IDN"))
    act(X("WB", 0, 128), X("BLK"), scale=X("WF", 0, 1))
    act(X("WB", 128, 256), X("BLK"), scale=X("WF", 1, 2))
    for h in range(4):
        o = (512 * h, 512 * h + 512)
        select(X("EX", *o), X("ONES"), [[-1, 32], [0, 16]], A.is_equal, -32 * h, 1)
    for t in range(4):
        send("pre%d" % t, "SM%d" % t, 256 * rank, "FR", lambda p: 256 * t + 48 * p)
    for h in range(4):
        gate["g"] = last["send"]
        select(X("SEL", 512 * h, 512 * h + 512), X("ONES"), [[-1, 4], [-16, 8], [0, 16]], A.is_equal, -4 * h, 1)
    for i in range(16):
        select(blk("CUM", i), X("BLK"), [[0, 8], [1, 16]], A.is_ge, -i, 0)
    select(X("TRI"), X("VN"), [[0, 16], [16, 8], [1, 16]], A.is_gt, 0, -1)
    select(X("BD"), X("BLK"), [[1, 128]], A.is_equal, -1, -1)
    tt(X("BD"), X("IDN"), X("BD"), A.subtract)
    act(X("Z4"), blk("SEL", 15), scale=-4.0)
    act(X("ZK"), blk("SEL", 15), scale=2304.0)
    act(X("BLF"), X("BLK"))
    for h in range(2):
        ts(X("DIAG", 128 * h, 128 * h + 128), X("CM"), rp, A.is_equal)
    select(X("SEG"), X("ONES", 0, 256), [[0, 16], [1, 16]], A.is_gt, 0, 0)
    select(X("SEN"), X("C12", 256, 384), [[0, 8], [1, 16]], A.is_gt, 0, 0, -2.0 ** 30)
    ts(X("LANE"), X("CI", 0, 16), 16.0, A.mult, rp, A.add)
    act(X("BASE"), X("LANE"), F.Identity, scale=16 * 65536.0, bias=16 * 65536.0)
    for t in range(4):
        act(X("L4", 16 * t, 16 * t + 16), X("LANE"), F.Identity, scale=65536.0, bias=(4096 + 256 * t) * 65536.0)
    ts(ecol, X("PI", 3, 4), -4.0, A.add)
    ts(ini, rp, -8.0, A.add, 0.0, A.max)
    ts(ini, ini, 256.0, A.mult)
    ts(cap, rp, 8.0, A.is_lt, 256.0, A.mult)
    tt(cap, cap, ini, A.max)
    act(X("CAPC"), X("ONES", 0, 256), scale=cap)
    ts(row0, rp, 0.0, A.is_equal, 8192.0, A.mult)
    ts(not0, rp, 0.0, A.is_gt)
    iota(X("SGN"), [[0, 2], [2, 2], [0, 16]], -1, 0)
    act(X("NDF"), X("IDM"))
    act(X("BD6"), X("BD"), scale=6144.0)
    act(X("NBL"), X("BLK"), scale=-2.0 ** 30)
    for t in range(2):
        for d in range(4):
            act(X("ST%d" % t, 256 * d, 256 * d + 48), X("ONES", 0, 48), scale=row0)
    for h in range(4):
        ts(X("TL", 256 + 512 * h, 768 + 512 * h), X("TLI", 512 * h, 512 * h + 512), -1.0, A.mult, 4096.0, A.add)
    for h in range(8):
        o = X("TAB", 2304 + 512 * h, 2816 + 512 * h)
        lin(PLAN["NEG"][h], o, o, -1.0, 255.0)
    for t in range(4):
        act(X("SM%d" % t, 256 * rank, 256 * rank + 48), X("FR", 256 * t + 48 * rank, 256 * t + 48 * rank + 48))
        act(X("M", 256 * t + 448, 256 * t + 512), X("FR", 256 * t + 192, 256 * t + 256))
        if t < 3:
            act(X("MR", 64 * t, 64 * t + 64), X("FR", 256 * t + 192, 256 * t + 256))

    def candidates(t, c0, c1, name="M"):
        n, li = c1 - c0, 64 * t
        src = X("M", 256 * t + 16 * c0, 256 * t + 16 * c1) if name == "M" else X(name)
        for h in range(8):
            mm(X("m2", 256 + 4 * n * (h // 4), 256 + 4 * n * (h // 4 + 1)), blk("W4", h), X(src[0], src[1] + h % 4, src[2], 4), h == 0, h == 7)
        uv, u, v = X("LI", li + c0, li + c1 + n), X("LI", li + c0, li + c1), X("LI", li + c1, li + c1 + n)
        a = X("LI", li + 32 + c0, li + 32 + c1)
        tt(X("U4", 0, 8 * n), X("m2", 256, 256 + 8 * n), X("OWN", 0, 8 * n), A.mult)
        tt(X("U2", 0, 4 * n), X("U4", 0, 8 * n, 2), X("U4", 1, 8 * n, 2), A.add)
        tt(uv, X("U2", 0, 4 * n, 2), X("U2", 1, 4 * n, 2), A.add)
        ts(uv, uv, 4095, A.bitwise_and)
        tt(a, u, v, A.mult)
        ts(a, a, 5, A.arith_shift_right, 2047, A.bitwise_and)
        ct, each = X("CT", 256 * t + 16 * c0, 256 * t + 16 * c1), X("LC", 16 + c0, 16 + c1)
        tt(X("KU", 0, 16 * n), IX(X("LI", li, li + c1), each), X("KJ", 0, 16 * n), A.mult)
        tt(ct, IX(X("LI", li + 32, li + 32 + c1), each), X("KU", 0, 16 * n), A.add)
        ts(ct, ct, 2047, A.bitwise_and)
        cp(X("LST", *ct[1:3]), ct)
        for q in [3] if t == 4 else [q for q in PLAN["Q"] if c0 <= 4 * q < c1]:
            if "v" in PLAN["L" if t else "L0"][q]:
                repeat(1 if t == 4 else t, q)

    def repeat(t, q):
        o = 2048 * (t % 2) + 512 * q
        act(X("MD", o, o + 64), X("M", 256 * t + 64 * q, 256 * t + 64 * q + 64))
        for w in (64, 128, 256)[:4 - len(PLAN["L" if t else "L0"][q]) // 2]:
            act(X("MD", o + w, o + 2 * w), X("MD", o, o + w))

    pp = [0]

    def dbank():
        pp[0] += 1
        return PLAN["D"][pp[0] % len(PLAN["D"])]

    def leaders(t, q):
        k, who = q // 2, PLAN["L" if t else "L0"][q]
        b, n, second = "b%d" % k, 1024 // len(who), PLAN["Q"].index(q) > PLAN["Q"].index(q ^ 1)
        md = X("MD", 2048 * (t % 2) + 512 * q, 2048 * (t % 2) + 512 * q + n)
        if not second:
            mm(X(b, 0, 128), X("IDN"), X("JC"), True, False)
        for u in range(len(who)):
            at = 960 + 64 * t if t and q == 3 else 256 * t + 64 * q
            off = X("LST", at + n // 16 * u, at + n // 16 * (u + 1))
            o = (1024 * q + n * u, 1024 * q + n * (u + 1))
            if who[u] == "v":
                tt(X("FL", *o), IX(LM, off), md, A.is_gt)
            else:
                d = X(dbank(), 0, n)
                act(X("X", *o), IX(LM, off))
                mm(d, X("IDN"), X("X", *o), True, False)
                for h in range(0, n, 64):
                    mm(X(d[0], h, h + 64), X("IDM"), X("M", 256 * t + 64 * q, 256 * t + 64 * q + 64), False, h + 64 == n)
                act(X("FL", *o), d, F.Sign, bias=-0.5)
                mm(X(b, 64 * (q % 2) + n // 16 * u, 64 * (q % 2) + n // 16 * (u + 1)), X("IDN"), X("C20", 0, n // 16), False, False)
        lists(X(b, 64 * (q % 2), 64 * (q % 2) + 64), "VN", X("FL", 1024 * q, 1024 * q + 1024), False, second)
        if second:
            o, gi = (128 * k, 128 * k + 128), X("GI", 8 * k, 8 * k + 8)
            tt(X("SC", *o), X(b, 0, 128), X("CT", 256 * t + o[0], 256 * t + o[1]), A.add)
            lin(PLAN["F"][0][0], X("SP", *o), IX(X("SC", *o), X("LC", 0, 8)))
            scan(X("SX", *o), X("SEN"), X("SP", *o), 0.0, A.add, A.max)
            cp(gi, X("SX", o[0] + 15, o[1], 16))
            ts(gi, gi, 2047, A.bitwise_and)
            cp(X("GL", 8 * k, 8 * k + 8), gi)

    def products(t, k):
        c0, c1 = BLOCKS[k]
        n, b, s, gl = 16 * (c1 - c0), "b%d" % k, 16 * c0, X("GL", c0, c1)
        if t:
            ts(X("TG", s, s + n), IX(TLW, gl), -1.0, A.mult, 4096.25, A.add)
        else:
            cp(X("TG", s, s + n), IX(X("TLI"), gl))
        lin(PLAN["F"][0][1], X("LG", s, s + n), IX(LM, gl))
        mm(X(b, 0, 128, 1, n), X("M", 256 * t + s, 256 * t + s + n), X("IDN"), True, False)
        mm(X(b, 0, 128, 1, n), X("LG", s, s + n), X("IDM"), False, PLAN["NG"][k] == "v")
        if PLAN["NG"][k] == "s":
            mm(X(b, 128, 256), X("IDN"), X("LG", s, s + n), False, False)
            mm(X(b, 128, 256), X("IDM"), X("M", 256 * t + s, 256 * t + s + n), False, True)
        qt = X("QT", 128 * k, 128 * k + 128, 1, n)
        lin(PLAN["F"][0][2], qt, X(b, 0, 128, 1, n), 1.0, -255.0)
        if PLAN["NG"][k] == "s":
            act(X("NG", s, s + n), X(b, 128, 256), F.Relu)
        else:
            tt(X("NG", s, s + n), X("LG", s, s + n), X("M", 256 * t + s, 256 * t + s + n), A.is_gt)
        mm(X(b, 0, 256), X("C255"), X("WB"), True, False)
        mm(X(b, 0, 256), X("IDN"), X("C19"), False, False)
        for u in range(n // 32):
            l0 = s + 32 * u
            o, src = (16 * l0, 16 * l0 + 512), IX(X("MO"), X("TG", l0, l0 + 32))
            d = X(dbank())
            who = PLAN["PG"][k]
            if PLAN["TWO"] and u % 2 == 0 and who[u] == who[u + 1] != "x":
                lin(who[u], X("X", o[0], o[1] + 512), IX(X("MO"), X("TG", l0, l0 + 64)))
            elif not (PLAN["TWO"] and u % 2 and who[u] == who[u - 1] != "x"):
                lin(who[u], X("X", *o), src)
            mm(d, X("IDN"), X("X", *o), True, False)
            mm(d, qt, X("EX", 512 * u, 512 * u + 512, 1, n), False, True)
            lin(PLAN["PP"][k][u], X("R", *o), d, -1.0, 0.0, True)
        for i in range(16):
            mm(X(b, i, 256, 16), X("R", 16 * s + i, 16 * (s + n), 16), X("W2"), False, i == 15)
        ui, hp = X("UI", 2 * s, 2 * s + 2 * n), X("HP", s, s + n)
        if PLAN["MOD"][k] == "s":
            lin(PLAN["F"][0][4], X("UF", 2 * s, 2 * s + 2 * n), X(b, 0, 2 * n), 1.0, -2047.5)
            tt(ui, X(b, 0, 2 * n), X("UF", 2 * s, 2 * s + 2 * n), A.subtract)
        else:
            cp(ui, X(b, 0, 2 * n))
            ts(ui, ui, 4095, A.bitwise_and)
        tt(X("PRD", s, s + n), X("UI", 2 * s, 2 * s + n), X("UI", 2 * s + n, 2 * s + 2 * n), A.mult)
        ts(hp, X("PRD", s, s + n), 5, A.arith_shift_right, 4095, A.bitwise_and)
        tt(X("HY", s, s + n), hp, X(b, 0, n), A.add)
        lin(PLAN["F"][0][3], X("HF", s, s + n), X("HY", s, s + n), 1.0, -2047.5)
        h = X(b, 256, 384)
        mm(h, X("HY", s, s + n), X("IDF"), True, False)
        mm(h, X("HF", s, s + n), X("IDM"), False, True)
        cp(X("HL", s, s + n), h)
        cp(X("HI", s, s + n), h)
        ts(X("D3", s, s + n), X("HI", s, s + n), 3, A.bitwise_and)

    def seen(t, k):
        c0, c1 = BLOCKS[k]
        n, b, s = 16 * (c1 - c0), "b%d" % k, 16 * c0
        w = n // len(PLAN["S"][k])
        mm(X(b, 0, n), X("NBL"), X("NG", s, s + n), True, False)
        for u in range(n // w):
            l0 = s + w * u
            o, src = (16 * l0, 16 * (l0 + w)), IX(SNW, X("HL", l0, l0 + w))
            if PLAN["TWO"] and PLAN["S"][k][u - u % 2:u - u % 2 + 2] == "vv":
                if u % 2 == 0:
                    tt(X("FL", o[0], o[1] + 16 * w), IX(SNW, X("HL", l0, l0 + 2 * w)), X("R", o[0], o[1] + 16 * w), A.not_equal)
            elif PLAN["S"][k][u] == "v":
                tt(X("FL", *o), src, X("R", *o), A.not_equal)
            else:
                d = X(dbank(), 0, 16 * w)
                act(X("X", *o), src)
                mm(d, X("IDN"), X("X", *o), True, False)
                mm(d, X("IDM"), X("R", *o), False, True)
                act(X("FL", *o), d, F.Square)
            if w * (u + 1) % 64 == 0:
                a = w * (u + 1) - 64
                for i in range(16):
                    mm(X(b, a, a + 64), blk("CUM", i), X("FL", 16 * (s + a) + i, o[1], 16), False, i == 15 and a + 64 == n)
        o = (s, s + n)
        ts(X("ZB", *o), X(b, 0, n), 0.0, A.is_gt)
        mm(X("m1", *o), X("BD"), X("ZB", *o), True, True)
        mm(X("m2", *o), X("Z4"), X("ZB", *o), True, False)
        tt(X("TD", *o), X("m1", *o), X("D3", *o), A.mult)
        mm(X("m2", *o), X("BLK"), X("TD", *o), False, True)


    def children(t):
        lists(X("b0", 0, 16), "VN", X("ZB"))
        tt(X("PLF"), X("B2"), X("b0", 0, 16), A.add)
        ts(X("PL"), X("PLF"), 2.0 ** -16, A.mult)
        act(X("PCB"), IX(X("R", 0, 4352 + 256 * t), X("PL")), F.Identity, bias=255.0, scale=-1.0)
        ts(X("E"), X("m2", 0, 256), ecol, A.is_equal)
        scan(X("CS"), X("E"), X("CAPC"), ini, A.add, A.min)
        tt(X("SL"), X("CS"), X("E"), A.mult)
        lists(X("b1", 0, 16), "VN", X("SL"))
        ts(X("SLOT"), X("b1", 0, 16), -2.0 ** -16, A.mult, -1.0, A.add)
        cp(IX(X("SM%d" % t), X("SLOT")), X("PCB"))

    def keys(t):
        ka = X("LI", 64 * t + 48, 64 * t + 64)
        ts(X("HASB"), X("SX", 15, 256, 16), 2048.0, A.is_ge, 2.0 ** 29, A.mult)
        tt(X("K1"), IX(X("CT", 256 * t, 256 * t + 256), X("LC", 8, 9)), X("HASB"), A.subtract)
        ts(ka, X("K1"), 256.0, A.add, 0.0, A.max)
        both = X("LI", 64 * t + 32, 64 * t + 64)
        ts(X("KP", 0, 32), both, 8160, A.bitwise_and)
        ts(X("KP", 32, 64), both, 31, A.bitwise_and)
        tt(X("KPB"), X("KP"), X("SGN"), A.mult)
        for h in range(2):
            for r in range(16):
                mm(X("m0", r, 512, 16), blk("SEL", r), X("KPB", 32 * h, 32 * h + 32), h + r == 0 and t == 3, h + r == 16 and t == 3)
        tt(X("B2"), X("L4", 16 * t, 16 * t + 16), X("HASB"), A.subtract)
        tt(X("B2"), X("B2"), X("BASE"), A.max)

    def winners(kb, kf):
        first = PLAN["EQ" if kf[3] > 1 else "EQ3"]
        if first < 16:
            act(X("KRF", 16 * first, 256), X(kb, 256 + 16 * first, 512))
            act(X("NKF"), kf, scale=-1.0)
        if first:
            cp(X("KR"), X(kb, 256, 512))
        at = 0
        for c in range(first, 16):
            n = 256 - 16 * c
            act(X("EQT", at, at + n), X("KRF", 16 * c, 256), F.Abs, bias=X("NKF", c, c + 1))
            act(X("EQ", 272 * c, 256 * c + 256), X("EQT", at, at + n), F.Relu, bias=1.0, scale=-1.0)
            at += n
        mm(X("d0", 16, 256), X("IDN"), X("C12", 272, 512), True, False)
        turn = list(range(first, 15)) + list(range(min(first, 15)))
        for c in turn + [15] * (first == 16):
            if c < first:
                ts(X("EQ", 272 * c, 256 * c + 256), X("KR", 16 * c, 256), X(kf[0], kf[1] + c * kf[3], kf[1] + c * kf[3] + 1), A.is_equal)
            if c < 15:
                mm(X("d0", 16 * c + 16, 256), X("BLK"), X("EQ", 272 * c + 16, 256 * c + 256), False, c == turn[-1])
        act(X("DUPS", 16, 256), X("d0", 16, 256))
        last["dups"] = [len(rec) - 1]
        mm(X("d1", 0, 16), X("IDF"), kf, True, False)
        for r in range(16):
            mm(X("d1", 0, 16), blk("TRI", r), X("EQ", r, 4096, 272), False, False)
        lists(X("d1", 1, 16), "VN", X("DUPS", 16, 256), False, True)
        tt(X("X2"), X("d1", 0, 16), X("LANE"), A.max)
        cp(X("LLA"), X("X2"))

    candidates(0, 0, 16)
    for t in range(4):
        m, nx = X("M", 256 * t, 256 * t + 256), 256 * t + 256
        if t < 3:
            n = 192 if t else 0
            if n:
                tt(X("MT", 0, n), X("LT", 192 * t - 192, 192 * t), X("TL", 256, 256 + n), A.max)
                act(X("TA", 0, n), X("MT", 0, n), F.Abs, bias=-4096.0)
                act(X("TB", 0, n), X("TA", 0, n), F.Relu, bias=4096.0, scale=-1.0)
            act(X("TB", n, 256), X("TL", 256 + n, 512), scale=not0)
            mm(X("m0"), X("IDN"), X("C12"), True, False)
            mm(X("m0", 0, 256), X("NDF"), X("TB"), False, False)
        for step in PLAN["ORDER"].split():
            if step[0] in "LPS":
                {"L": leaders, "P": products, "S": seen}[step[0]](t, int(step[1]))
            elif step == "K":
                keys(t)
            elif step == "C" and t == 0:
                candidates(4, 0, 12, "MR")
                for u in range(1, 4):
                    cp(X("CT", 256 * u + 192, 256 * u + 256), X("CT", 960 + 64 * u, 1024 + 64 * u))
                    cp(X("LI", 64 * u + 44, 64 * u + 48), X("LI", 284 + 4 * u, 288 + 4 * u))
            elif step == "C" and t < 3 and "v" in PLAN["L"][3]:
                repeat(t + 1, 3)
            elif step == "W" and t == 3:
                cp(X("KF"), X("LI", 64 * t + 48, 64 * t + 64))
                winners("m0", X("KF"))
        if t < 2:
            act(X("TGF"), IX(TLW, X("GL")), F.Identity, bias=8192.0, scale=-1.0)
        mask = X("m1", 0, 256)
        children(t)
        if t == 3:
            gate["v"] = [len(rec) - 1]
            cp(IX(X("TAB", 0, 2304), X("LLA")), m)
            store("y", "dyl", T.yl[:], LM)
        sm = "SM%d" % t
        send("fm%d" % (t + 1), "M", nx + 48 * rank, sm, lambda p: 256 * p)
        act(X("M", nx + 48 * rank, nx + 48 * rank + 48), X(sm, 256 * rank, 256 * rank + 48))
        if t < 2 and PLAN["ST"] == "v":
            act(X("MSK"), mask, scale=8192.0)
        elif t < 2:
            mm(X("b0", 256, 512), X("IDF"), X("TGF"), True, False)
            mm(X("b0", 256, 512), X("BD6"), X("ZB"), False, True)
            act(X("MSK"), X("b0", 256, 512))
        if t < 3:
            tt(X("TH"), mask, X("HI"), A.mult)
            mm(X("m0", 256, 512), X("ZK"), X("ZB"), False, False)
            mm(X("m0", 256, 512), X("BLF"), X("TH"), False, True)
            tt(X("KD"), X("m0", 256, 512), X("DIAG"), A.mult)
            scan(X("KS"), X("SEG"), X("KD"), 0.0, A.mult, A.add)
            act(X("VAL"), X("PCB"), F.Identity, bias=255.0, scale=-1.0)
            winners("m0", X("KS", 15, 256, 16))
            tt(X("TY"), X("m0", 0, 256), X("TB"), A.max)
            cp(IX(X("TAB"), X("LLA")), X("VAL"))
            act(IX(X("TL"), X("LLA")), X("TY"), F.Silu)
        if t < 2:
            st = "ST%d" % t
            if PLAN["ST"] == "v":
                tt(IX(X(st), X("SLOT")), X("MSK"), X("TGF"), A.max)
            else:
                gate["s"] = last["dups"] * PLAN["GATE"]
                act(IX(X(st), X("SLOT")), X("MSK"), F.Silu)
            send("ft%d" % (t + 1), "LT", 192 * t + 48 * rank, st, lambda p: 256 * p)
            act(X("LT", 192 * t + 48 * rank, 192 * t + 48 * rank + 48), X(st, 256 * rank, 256 * rank + 48))
        if t < 3:
            candidates(t + 1, 0, 12)
    store("s", "dyf", T.yf[:], X("M", 1024, 1280))
    issue()
